import numpy as np, ml_dtypes
CORES = [5,29,101,125,133,157,229,253]
N = 8
BF = ml_dtypes.bfloat16
def f(rng, *shape):
    return (rng.standard_normal(shape, dtype=np.float32) * np.exp2(rng.integers(-2, 3, shape[:-1] + (1,)))).astype(BF)
def wide(rng, *shape):
    v = f(rng, *shape).astype(np.float32); k = shape[:-2] + (1, shape[-1])
    return (v * np.exp2(rng.integers(-6, 7, k)) * (rng.random(k) > 0.0625)).astype(BF)
def gentries(a):
    return np.ascontiguousarray(a.reshape(8, 16, -1).transpose(0, 2, 1)).reshape(8, -1)
def gtable(e):
    e = np.asarray(e); return np.ascontiguousarray(e.reshape(8, -1, 16).transpose(0, 2, 1)).reshape(128, -1).astype(np.int32)
L, M, S0, R = 2304, 3584, 12, 3
S = 16
def tame(v):
    u = np.minimum(np.maximum(v.astype(np.float32), np.float32(-960)), np.float32(960))
    return np.where(np.abs(u) < np.float32(2.0 ** -16), np.float32(0), u).astype(BF)
def speech(rng):
    q = 2.0 ** (-0.4 * rng.permutation(24)); ks = rng.integers(2, 7, 24); ks[np.argmax(q)] = 5
    W = [rng.permutation(S0)[:k] for k in ks]; w = np.zeros((N, 8, L), np.int64)
    for r in range(N):
        acc = np.add.accumulate(q * 2.0 ** rng.integers(-1, 2, 24))
        for g in range(8):
            i = np.minimum(np.searchsorted(acc, rng.random(L // 2) * acc[-1], side="right"), 23)
            v = np.concatenate([W[j] for j in i])[:L]; w[r, g] = np.where(rng.random(L) < 0.1, rng.integers(0, S0, L), v)
    return w
def lengths(rng):
    le = rng.integers(L // 2, L + 1, (N, 8)); le[rng.integers(0, N), rng.integers(0, 8)] = L
    return le
def plant(rng, w, le):
    r = rng.integers(0, len(w)); w[r, np.argmax(le[r]), :S0] = rng.permutation(S0)
def make(rng, w, le):
    st = np.zeros((N, 8, M), np.int32); ps = np.zeros((N, 8, L), np.int64)
    for r in range(N):
        for g in range(8):
            v = rng.permutation(np.concatenate((np.arange(S0), rng.integers(0, S0, M - S0)))); o = np.argsort(v, kind="stable")
            c = np.bincount(v, minlength=S0); first = np.add.accumulate(c) - c
            st[r, g] = v; ps[r, g] = o[first[w[r, g]] + rng.integers(0, c[w[r, g]])]
    return {"ve": tame(f(rng, N, 128, M)), "st": st, "pos": np.stack([gtable(p) for p in ps]), "le": le.reshape(N, 8, 1).astype(np.int32)}
def setup_inputs(rng):
    w, le = speech(rng), lengths(rng); plant(rng, w, le); return make(rng, w, le)
def setup_inputs_ends(rng):
    w, le = speech(rng), lengths(rng)
    for r in range(N): le[r, rng.permutation(8)[:4]] = np.array([0, 1, 2, L])
    ab = rng.permutation(S0)[:2]; v = w.reshape(N, 8, L // 2, 2); v[rng.random((N, 8, L // 2)) < 0.4] = ab; w = v.reshape(N, 8, L); w[:, :, :2] = ab
    for r in range(N):
        for g in range(8):
            if le[r, g] >= 2: w[r, g, le[r, g] - 2:le[r, g]] = ab
    plant(rng, w, le); d = make(rng, w, le)
    d["pos"][:, 8::16, 2] = 0; d["pos"][:, 9::16, 2] = M - 1; return d
def setup_inputs_ties(rng):
    w, le = speech(rng)[:N // 2], lengths(rng)[:N // 2]; plant(rng, w, le)
    return make(rng, np.concatenate((w, w ^ 1)), np.concatenate((le, le)))
def setup_inputs_few(rng):
    w = speech(rng); le = rng.integers(0, 2, (N, 8)); r, q = rng.permutation(N)[:2]; g = rng.integers(0, 8); le[q] = 0; le[q, (g + 3) % 8] = 1; le[r, g] = S0 + 2
    p = 1 + rng.permutation(S0 - 1); w[r, g, :S0 + 2] = np.concatenate((p[:1], [0], p[1:], [0], p[:1])); return make(rng, w, le)
def setup_inputs_loop(rng):
    W = [rng.permutation(S0)[:k] for k in range(2, 8)]; le = lengths(rng); w = np.zeros((N, 8, L), np.int64)
    for r in range(N):
        for g, i in enumerate(rng.permutation(np.array([0, 1, 2, 2, 3, 4, 5, 5]))): w[r, g] = W[i][(np.arange(L) + rng.integers(0, 8)) % len(W[i])]
    plant(rng, w, le); return make(rng, w, le)
def setup_inputs_spread(rng):
    w = np.stack([np.stack([np.repeat(rng.integers(0, S0, L), rng.integers(1, 40, L))[:L] for g in range(8)]) for r in range(N)])
    le = np.maximum(np.floor(L * rng.random((N, 8)) ** 4).astype(np.int64), 1); le[np.arange(N), rng.integers(0, 8, N)] = L
    plant(rng, w, le); d = make(rng, w, le); d["ve"] = tame(wide(rng, N, 128, M)); return d
def rounds(st, pos, le):
    s, pl = [], []
    for r in range(N):
        P = gentries(pos[r]).astype(np.int64)
        for g in range(8):
            p = P[g, :int(le[r, g, 0])]; pl.append(p); s.append(st[r, g][p].astype(np.int64))
    mg = np.zeros((R, 3), np.float32)
    for t in range(R):
        h = np.zeros(S * S, np.int64)
        for v in s: h += np.bincount((v[:-1] * S + v[1:])[v[:-1] != v[1:]], minlength=S * S)
        k = int(np.argmax(h)); a = k // S; b = k - S * a; mg[t] = a, b, h[k]
        for i in range(len(s)):
            v = s[i]; hit = np.zeros(v.size, bool); hit[:-1] = (v[:-1] == a) & (v[1:] == b)
            keep = np.ones(v.size, bool); keep[1:] = ~hit[:-1]
            s[i] = np.where(hit, S0 + t, v)[keep]; pl[i] = pl[i][keep]
    return s, pl, mg
def check_inputs(d):
    try:
        bad = []
        if not np.isfinite(d["ve"].astype(np.float32)).all(): bad.append("ve is finite")
        if d["st"].min() < 0 or d["st"].max() >= S0: bad.append("st is 0 to S0 - 1")
        if d["pos"].min() < 0 or d["pos"].max() >= M: bad.append("pos is 0 to M - 1")
        if d["le"].min() < 0 or d["le"].max() > L: bad.append("le is 0 to L")
        if not bad and rounds(d["st"], d["pos"], d["le"])[2][:, 2].min() < 1: bad.append("a pair is left in every round")
        return bad
    except Exception:
        return ["shapes"]
def reference(ve, st, pos, le):
    s, pl, mg = rounds(st, pos, le)
    y = np.zeros((N, 128, L), BF); fs = np.full((N, 8, L), -1, np.float32); fl = np.zeros((N, 8, 1), np.float32)
    for r in range(N):
        for g in range(8):
            v, p = s[8 * r + g], pl[8 * r + g]; fl[r, g, 0] = v.size; fs[r, g, :v.size] = v
            y[r, 16 * g:16 * g + 16, :v.size] = ve[r, 16 * g:16 * g + 16][:, p]
    return {"y": y, "fs": fs, "fl": fl, "mg": np.tile(mg, (N, 1, 1))}

@@ -1,0 +1,582 @@
+from concourse.bass import DstId, RemoteDMATransfer
+from concourse.mybir import AluOpType, AxisListType, ActivationFunctionType
+
+A = AluOpType
+F = ActivationFunctionType
+L, M, S0 = 2304, 3584, 12
+CH = L // 16
+SW = M // 16
+HL, HR = 4, 6
+MAGIC = 3221225472.0
+ROUND = 12582912.0
+CNT0 = 28672.0
+PAY = (16, 32, 32)
+
+
+def _sb(n, d):
+    return ("sbuf", [128, n], d)
+
+
+SCRATCH = {}
+for _n in ("cur0", "rc1", "rc2", "c0", "cz", "ca", "cbk", "ne", "h0", "h1", "ma", "mb", "vm", "val0", "cz2", "s1", "kk",
+           "ca2", "ek", "et", "kt", "nd", "m14", "xs", "zb", "z1", "zw", "zi", "tmpb", "ml", "km93", "k18", "sq0", "sq1", "sq2"):
+    SCRATCH[_n] = _sb(160, "bfloat16")
+for _n in ("xf", "x16", "xg", "c16", "jt", "oo", "av", "llo", "lal", "mlo", "mal", "g2", "tm", "tq", "gs"):
+    SCRATCH[_n] = _sb(160, "float32")
+for _n in ("posi", "qi", "ri", "idx", "zz", "oi", "om"):
+    SCRATCH[_n] = _sb(CH, "int32")
+for _n in ("posu", "qu", "ru", "tu"):
+    SCRATCH[_n] = _sb(CH, "uint16")
+for _n in ("bones", "btri", "nbones", "nbtri", "bt0", "i16x", "i93"):
+    SCRATCH[_n] = _sb(128, "bfloat16")
+SCRATCH.update({
+    "sti": _sb(SW, "int32"), "lei": _sb(4, "int32"), "pi": _sb(8, "int32"), "col": _sb(64, "float32"),
+    "win": _sb(64, "float32"), "i16": _sb(16, "bfloat16"),
+    "mk": _sb(L, "bfloat16"), "gg": _sb(L + 32, "bfloat16"), "oh": _sb(146 * 16, "bfloat16"),
+    "ves": _sb(M, "bfloat16"), "y0": _sb(L + 16, "bfloat16"), "yo": _sb(L, "bfloat16"),
+    "symw": _sb(L + 16, "bfloat16"), "fso": _sb(L, "float32"),
+    "cb0": _sb(448, "bfloat16"), "cb1": _sb(448, "bfloat16"), "mrk": _sb(432, "bfloat16"),
+    "ohz": _sb(16 * CH, "bfloat16"), "junk": _sb(9 * CH, "bfloat16"), "xd": _sb(288, "bfloat16"), "xt": _sb(288, "bfloat16"),
+    "k4096": _sb(CH, "bfloat16"), "bsel": _sb(128, "float32"),
+    "sel": _sb(128, "float16"), "lv1": _sb(128, "float16"), "lv2": _sb(128, "float16"),
+    "ptie": _sb(48, "float16"), "poff": _sb(16, "float16"), "cor1": _sb(16, "float16"), "cor2": _sb(16, "float16"),
+    "corv": _sb(16, "float16"), "dead1": _sb(16, "float16"), "dead2": _sb(16, "float16"),
+    "coef1": _sb(32, "float32"), "coef2": _sb(32, "float32"), "neg": _sb(48, "float32"),
+    "sc": _sb(64, "float32"), "sct": _sb(32, "float32"), "thr": _sb(16, "float32"), "eh": _sb(16, "float32"),
+    "sm": _sb(32, "float32"), "smi": _sb(16, "int32"), "mgb": _sb(16, "float32"),
+    "offx": _sb(8, "uint16"), "offd": _sb(18, "uint16"), "offt": _sb(10, "uint16"), "ehu": _sb(10, "uint16"),
+    "land0": _sb(8 * 16, "float16"), "land1": _sb(8 * 32, "float16"), "land2": _sb(8 * 32, "float16"),
+    "hand": _sb(3 * 32, "float16"),
+})
+for _k in range(8):
+    SCRATCH["ps%d" % _k] = ("psum", [128, 512], "float32")
+
+SEMAPHORES = ["sv", "sa", "sp", "sg", "ls", "ad0", "ad1", "ad2", "ar0", "ar1", "ar2", "rl0", "rl1", "rl2",
+              "dpos", "dst", "dle", "dve", "dout"]
+
+
+def bits(engines):
+    m = 0
+    for e in engines:
+        m |= 1 << e
+    return m
+
+
+def routes(T, topo, core):
+    others = [c for c in T.cores if c != core]
+    direct = [c for c in others if topo.may_write(core, c)]
+    far = [c for c in others if not topo.may_write(core, c)]
+    cand = [c for c in topo.cores_of(core) if T.rank_of(c) is None and all(topo.may_write(c, d) for d in far)]
+    cand.sort(key=lambda c: (topo.die(c) != topo.die(core), c))
+    rel = cand[:2]
+    half = (len(far) + 1) // 2
+    return direct, [(rel[0], far[:half]), (rel[1], far[half:])]
+
+
+def dst_id(topo, d, s):
+    rid, pid = topo.addr(d, s)
+    return DstId(rid=rid, pnc=pid)
+
+
+def relay_main(g, core, T, topo, owner, dests):
+    r = T.rank_of(owner)
+    eng = topo.engines(core, dests[0])
+    per = len(eng) // len(dests)
+    n_in = len(topo.engines(owner, core)) // 2
+    for t in range(3):
+        w = PAY[t]
+        g.wait_ge(T.sem["rl%d" % t], n_in)
+        g.remote_dma_fused([RemoteDMATransfer(dst_ids=[dst_id(topo, d, core)], dma_engine_mask=bits(eng[k * per:(k + 1) * per]),
+                                              remote_sem=T.sem["ar%d" % t], src=T.hand[:, 32 * t:32 * t + w],
+                                              dst=T["land%d" % t][:, w * r:w * r + w]) for k, d in enumerate(dests)],
+                           local_sem=T.sem.ls)
+    g.wait_ge(T.sem.ls, 3 * per * len(dests))
+
+
+def rank_program(g, core, T, topo):
+    if T.rank_of(core) is not None:
+        rank_main(g, core, T, topo)
+        return
+    for c in topo.cores_of(core):
+        if T.rank_of(c) is not None:
+            for rl, dests in routes(T, topo, c)[1]:
+                if rl == core:
+                    relay_main(g, core, T, topo, c, dests)
+
+
+def rank_main(g, core, T, topo):
+    rank = T.rank_of(core)
+    Q = {"v": g.vector, "a": g.scalar, "p": g.tensor, "g": g, "s": g.sync}
+    SEM = {"v": "sv", "a": "sa", "p": "sp", "g": "sg"}
+    cnt = {"v": 0, "a": 0, "p": 0, "g": 0}
+    seen = {}
+    wr, rd = {}, {}
+
+    def deps(q, r, w):
+        need = {}
+
+        def add(h):
+            need[h[0]] = max(need.get(h[0], 0), h[1])
+        for k in r:
+            if k in wr:
+                add(wr[k])
+            if k.startswith("ps"):
+                bank = k[:3]
+                for h in rd.get(bank, []):
+                    if h[0] != SEM.get(q):
+                        add(h)
+        for k in w:
+            if k in wr:
+                add(wr[k])
+            for h in rd.get(k, []):
+                add(h)
+        for s in need:
+            wait(q, (s, need[s]))
+
+    def wait(q, h):
+        if h[0] == "sp" and q == "p":
+            return
+        if seen.get((q, h[0]), 0) < h[1]:
+            Q[q].wait_ge(T.sem[h[0]], h[1])
+            seen[(q, h[0])] = h[1]
+
+    def note(h, r, w):
+        for k in r:
+            rd.setdefault(k, []).append(h)
+        for k in w:
+            wr[k] = h
+            rd[k] = []
+
+    def op(q, r, w, fn):
+        deps(q, r, w)
+        cnt[q] += 1
+        fn().then_inc(T.sem[SEM[q]], 1)
+        note((SEM[q], cnt[q]), r, w)
+
+    outs = [0]
+
+    def dma(q, r, w, out, in_, sem=None):
+        deps(q, r, w)
+        if sem is None:
+            outs[0] += 16
+            Q[q].dma_start(out, in_).then_inc(T.sem.dout, 16)
+        else:
+            Q[q].dma_start(out, in_).then_inc(T.sem[sem], 16)
+            note((sem, 16), r, w)
+
+    V, ACT, PE = g.vector, g.scalar, g.tensor
+
+    def ts(r, w, out, in0, s1, o1, s2=None, o2=None):
+        if o2 is None:
+            op("v", r, w, lambda: V.tensor_scalar(out, in0, s1, None, o1))
+        else:
+            op("v", r, w, lambda: V.tensor_scalar(out, in0, s1, s2, o1, o2))
+
+    def tt(r, w, out, in0, in1, o):
+        op("v", r, w, lambda: V.tensor_tensor(out, in0, in1, o))
+
+    def cp(r, w, out, in_):
+        op("v", r, w, lambda: V.tensor_copy(out, in_))
+
+    def ms(w, ap, c):
+        op("v", [], w, lambda: V.memset(ap, c))
+
+    def scan(r, w, out, d0, d1, init, o0, o1):
+        op("v", r, w, lambda: V.tensor_tensor_scan(out, d0, d1, init, o0, o1))
+
+    def mm(r, w, out, lhsT, rhs, start, stop):
+        op("p", r, w, lambda: PE.matmul(out, lhsT, rhs, start, stop))
+
+    def lin(bank, n, terms):
+        for k, (mat, name, lo) in enumerate(terms):
+            lhsT = ident if mat == "zi" else T[mat][:]
+            mm([mat, name], [bank], T[bank][:, 0:n], lhsT, S(name, lo, lo + n), k == 0, k == len(terms) - 1)
+
+    def act(r, w, out, in_, func, **kw):
+        op("a", r, w, lambda: ACT.activation(out, in_, func, **kw))
+
+    def iota(w, out, pat, base, cm):
+        op("g", [], w, lambda: g.iota(out, pat, base, cm, allow_small_or_imprecise_dtypes=True))
+
+    def S(name, lo, hi):
+        return T[name][:, HL + lo:HL + hi]
+
+    def P(k, lo, hi):
+        return T.ps3[:, 160 * k + HL + lo:160 * k + HL + hi]
+
+    def C(k):
+        return T.col[:, k:k + 1]
+
+    def W(k):
+        return T.win[:, k:k + 1]
+
+    ident = T.zi[:, 15:143]
+
+    dma("s", [], ["posi"], T.posi[:], T.pos[:], "dpos")
+    dma("a", [], ["sti"], T.sti[:], T.st[:], "dst")
+    dma("s", [], ["lei"], T.lei[0:8, 0:1], T.le[:], "dle")
+    dma("s", ["posi", "sti"], ["ves"], T.ves[:], T.ve[:], "dve")
+
+    op("g", [], ["pi"], lambda: g.iota(T.pi[:, 0:1], [[0, 1]], 0, 1))
+    iota(["xf"], T.xf[:], [[1, 160]], 0, 0)
+    iota(["xg"], T.xg[:, 0:128], [[16, 8], [0, 16]], 0, 0)
+    iota(["x16"], T.x16[:, 0:128], [[0, 8], [1, 16]], 0, 0)
+    iota(["c16"], T.c16[:, 0:CH], [[16, CH]], 0, 0)
+    iota(["sm0"], T.sm[:, 0:18], [[16, 9], [0, 2]], 0, 0)
+    ms(["ggl"], T.gg[:, 0:16], -0.0625)
+    ms(["ggr"], T.gg[:, 16 + L:32 + L], 0.0)
+    for s in range(12, 16):
+        ms(["oh%d" % s], T.oh[:, s:146 * 16:16], 0.0)
+    ts(["pi"], ["pm"], T.pi[:, 1:2], T.pi[:, 0:1], 15, A.bitwise_and)
+    cp(["pi", "pm"], ["c01"], T.col[:, 0:2], T.pi[:, 0:2])
+    tt(["c01"], ["c2_"], C(2), C(0), C(1), A.subtract)
+    ts(["xf", "c01"], ["i16"], T.i16[:], T.xf[:, 0:16], C(1), A.is_equal)
+    ts(["c01"], ["c3"], C(3), C(0), 16.0, A.mult)
+    ts(["xf", "c2_"], ["z1"], T.z1[:, 0:144], T.xf[:, 0:144], -15.0, A.add, C(2), A.is_equal)
+    ts(["c01"], ["c4"], C(4), C(1), -144.0, A.mult, HL - 0.5, A.add)
+    ts(["xg", "c3"], ["bsel"], T.bsel[0:8, :], T.xg[0:8, 0:128], T.col[0:8, 3:4], A.is_equal)
+    cp(["c01"], ["offx0"], T.offx[:, 0:1], C(0))
+
+    ts(["posi"], ["qi"], T.qi[:], T.posi[:], 1.0 / SW, A.mult, -111.5 / SW, A.add)
+    cp(["qi"], ["qu"], T.qu[:], T.qi[:])
+    ts(["qi"], ["ps3a"], T.ps3[:, 0:CH], T.qi[:], -float(SW), A.mult)
+    tt(["ps3a", "posi"], ["ri"], T.ri[:], T.ps3[:, 0:CH], T.posi[:], A.add)
+    cp(["ri"], ["ru"], T.ru[:], T.ri[:])
+    cuts = [0, 24, 64, 104, 134, 144]
+    for k in range(len(cuts) - 1):
+        a, b = cuts[k], cuts[k + 1]
+        act(["i16", "qu"], ["mk%d" % k], T.mk[:, 16 * a:16 * b], T.i16[:, 0:16].indirect(T.qu[:, a:b]), F.Copy)
+    done = 0
+    for k in range(len(cuts) - 1):
+        a, b = cuts[k], cuts[k + 1]
+        tt(["sti", "ru", "mk%d" % k], ["gg%d" % k], T.gg[:, 16 + 16 * a:16 + 16 * b],
+           T.sti[:, 0:SW].indirect(T.ru[:, a:b]), T.mk[:, 16 * a:16 * b], A.mult)
+        if k == 0:
+            cp(["lei"], ["lef"], T.col[0:8, 5:6], T.lei[0:8, 0:1])
+            mm(["bsel", "lef"], ["ps4"], T.ps4[:, 0:1], T.bsel[0:8, :], T.col[0:8, 5:6], True, True)
+            act(["ps4", "c4"], ["c6"], C(6), T.ps4[:, 0:1], F.Identity, bias=C(4))
+            act(["xf", "c6"], ["tmpb"], T.tmpb[:, 0:154], T.xf[:, 0:154], F.Sign, bias=C(6), scale=-1.0)
+            act(["tmpb"], ["vm"], T.vm[:, 0:154], T.tmpb[:, 0:154], F.Identity, bias=49.0, scale=50.0)
+        while done < 16 and (CH * done + CH + HR <= 16 * b or b == CH):
+            i = done
+            mm(["z1", "ggl", "ggr"] + ["gg%d" % u for u in range(k + 1)], ["ps0"], T.ps0[:, 0:154], T.z1[:, 15 - i:143 - i],
+               T.gg[:, 16 + CH * i - HL:16 + CH * i + CH + HR], i == 0, i == 15)
+            done += 1
+    cp(["posi"], ["posu"], T.posu[:], T.posi[:])
+    tt(["ps0", "vm"], ["cur0"], T.cur0[:, 0:154], T.ps0[:, 0:154], T.vm[:, 0:154], A.min)
+
+    def oh_v(cur, n, s, val):
+        ts([cur], ["oh%d" % s], T.oh[:, s:16 * n:16], S(cur, 0, n), float(val), A.is_equal)
+
+    def oh_a(cur, n, pairs):
+        for k, (s, val) in enumerate(pairs):
+            act([cur], ["sq%d" % k], T["sq%d" % k][:, 0:n], S(cur, 0, n), F.Square, bias=-float(val))
+        for k, (s, val) in enumerate(pairs):
+            act(["sq%d" % k], ["oh%d" % s], T.oh[:, s:16 * n:16], T["sq%d" % k][:, 0:n], F.Relu, bias=1.0, scale=-1.0)
+
+    OH = ["oh%d" % s for s in range(16)]
+    oh_a("cur0", 145, [(10, 10), (11, 11)])
+    for s in range(10):
+        oh_v("cur0", 145, s, s)
+    for m in range(18):
+        mm(OH, ["ps1"], T.ps1[:, 0:128], T.oh[:, 128 * m:128 * m + 128], T.oh[:, 128 * m + 16:128 * m + 144], m == 0, m == 17)
+    for k in range(2):
+        act(["ves", "posu"], ["y0%d" % k], T.y0[:, 1 + 1152 * k:1 + 1152 * (k + 1)],
+            T.ves[:, 0:M].indirect(T.posu[:, 72 * k:72 * (k + 1)]), F.Copy)
+    ts(["x16", "c01"], ["sel"], T.sel[:], T.x16[:, 0:128], C(1), A.is_equal, 256.0, A.mult)
+    ts(["c01"], ["c8"], C(8), C(1), -16.0, A.mult, 111.0, A.add)
+    ms(["ptieb"], T.ptie[:, 16:48], -30000.0)
+    ts(["x16", "c8"], ["ptiea"], T.ptie[:, 0:16], T.x16[:, 0:16], C(8), A.subtract, -1.0 / 2048, A.mult)
+    ts(["i16"], ["poff"], T.poff[:], T.i16[:], -30000.0, A.mult, -CNT0 / 8 + 2048.0, A.add)
+    ms(["neg"], T.neg[:], -1e9)
+    ts(["ps1"], ["gs"], T.gs[:, 0:128], T.ps1[:, 0:128], -256.0, A.add)
+    cp(["gs", "offx0"], ["own0"], T.land0[:, 16 * rank:16 * rank + 16], T.gs[:, 0:128].indirect(T.offx[:, 0:1]))
+
+    direct, relays = routes(T, topo, core)
+    off_eng = topo.engines(core, direct[0])
+    on_eng = topo.engines(core, relays[0][0])
+    per = len(on_eng) // 2
+    sent = [0]
+
+    def send(t):
+        w = PAY[t]
+        src = T["land%d" % t][:, w * rank:w * rank + w]
+        deps("g", ["own%d" % t], [])
+        g.remote_dma_fused([RemoteDMATransfer(dst_ids=[dst_id(topo, rl, core)], dma_engine_mask=bits(on_eng[k * per:(k + 1) * per]),
+                                              remote_sem=T.sem["rl%d" % t], src=src, dst=T.hand[:, 32 * t:32 * t + w])
+                            for k, (rl, _) in enumerate(relays)], local_sem=T.sem.ls)
+        g.remote_dma_fused([RemoteDMATransfer(dst_ids=[dst_id(topo, d, core) for d in direct], dma_engine_mask=bits(off_eng),
+                                              remote_sem=T.sem["ad%d" % t], srcs=[src], dsts=[src for d in direct])],
+                           local_sem=T.sem.ls)
+        sent[0] += 2 * per + len(off_eng)
+
+    near = [T.rank_of(c) for c in direct]
+    farr = [r for r in range(8) if r != rank and r not in near]
+    n_ad = sum(len(topo.engines(c, core)) for c in direct)
+    n_ar = 0
+    for r in farr:
+        for rl, dests in routes(T, topo, T.cores[r])[1]:
+            if core in dests:
+                n_ar += len(topo.engines(rl, core)) // len(dests)
+
+    def key_terms(t, ranks, last):
+        land = T["land%d" % t]
+        for n, r in enumerate(ranks):
+            fin = last and n == len(ranks) - 1
+            rk = ["own%d" % t] if r == rank else []
+            if t == 0:
+                mm(["sel"] + rk, ["ps2"], T.ps2[:, 0:16], T.sel[:], land[:, 16 * r:16 * r + 16], False, fin)
+            else:
+                mm(["sel"] + rk, ["ps2"], T.ps2[:, 0:16], T.sel[:], land[:, 32 * r:32 * r + 16], False, False)
+                mm(["lv%d" % t] + rk, ["ps2"], T.ps2[:, 0:16], T["lv%d" % t][:], land[:, 32 * r + 16:32 * r + 32], False, fin)
+
+    def key_fix(u):
+        mm(["sel", "dead%d" % u], ["ps2"], T.ps2[:, 0:16], T.sel[:], T["dead%d" % u][:], False, False)
+        mm(["sel", "cor%d" % u], ["ps2"], T.ps2[:, 0:16], T.sel[:], T["cor%d" % u][:], False, False)
+        mm(["lv%d" % u, "corv"], ["ps2"], T.ps2[:, 0:16], T["lv%d" % u][:], T.corv[:], False, False)
+
+    def key_open(t):
+        mm(["sel", "ptiea", "ptieb"], ["ps2"], T.ps2[:, 0:48], T.sel[:], T.ptie[:], True, False)
+        mm(["sel", "poff"], ["ps2"], T.ps2[:, 0:16], T.sel[:], T.poff[:], False, False)
+        for u in range(t):
+            if u > 0:
+                key_fix(u)
+            key_terms(u, list(range(8)), False)
+
+    def key_close(t):
+        if t > 0:
+            key_fix(t)
+        key_terms(t, [rank], False)
+        wait("p", ("ad%d" % t, n_ad))
+        key_terms(t, near, False)
+        wait("p", ("ar%d" % t, n_ar))
+        key_terms(t, farr, True)
+
+    def winner(t):
+        b = 8 * t
+        scan(["ps2", "neg"], ["sc"], T.sc[:, 16:64], T.ps2[:, 0:48], T.neg[:], -1e9, A.max, A.max)
+        op("v", ["sc"], ["sct"], lambda: V.transpose(T.sct[:], T.sc[:, 32:64]))
+        op("v", ["sct"], ["w0%d" % t], lambda: V.tensor_reduce(W(b), T.sct[:], AxisListType.X, A.max))
+        ts(["w0%d" % t], ["w1%d" % t], W(b + 1), W(b), MAGIC, A.add, MAGIC, A.subtract)
+
+    def record(t):
+        b = 8 * t
+        act(["w4%d" % t, "w2%d" % t], ["w7%d" % t], W(b + 7), W(b + 4), F.Identity, bias=W(b + 2), scale=16.0)
+        act(["w1%d" % t], ["mg%db" % t], T.mgb[:, 3 * t + 2:3 * t + 3], W(b + 1), F.Identity, bias=CNT0, scale=1.0 / 256)
+        act(["w7%d" % t], ["w5%d" % t], W(b + 5), W(b + 7), F.Identity, bias=111.0, scale=-1.0)
+        act(["w4%d" % t, "w5%d" % t], ["mg%da" % t], T.mgb[:, 3 * t:3 * t + 2], T.win[:, b + 4:b + 6], F.Copy)
+
+    def delta(t):
+        b, u = 8 * t, t + 1
+        cb, n = "cb%d" % t, S0 + t
+        ts([cb + "a", cb + "b", cb + "c", "w0%d" % t, "w1%d" % t], ["mrk"], T.mrk[:], T[cb][:, 3:435], W(b + 1), A.add, W(b), A.is_equal)
+        for m in range(18):
+            mm(OH + ["mrk"], ["ps1"], T.ps1[:, 0:24], T.oh[:, 128 * m:128 * m + 128], T.mrk[:, 24 * m:24 * m + 24], m == 0, m == 17)
+        tt(["w0%d" % t, "w1%d" % t], ["w2%d" % t], W(b + 2), W(b), W(b + 1), A.subtract)
+        ts(["w2%d" % t], ["w3%d" % t], W(b + 3), W(b + 2), -1.0 / 16, A.mult, 104.5 / 16, A.add)
+        ts(["w3%d" % t], ["w4%d" % t], W(b + 4), W(b + 3), ROUND, A.add, ROUND, A.subtract)
+        ts(["x16", "w4%d" % t], ["coef%da" % u], T["coef%d" % u][:, 0:n], T.x16[:, 0:n], W(b + 4), A.is_equal, -1.0, A.mult)
+        ts(["c01", "c7", "w4%d" % t], ["offx%d" % u], T.offx[:, 2 * u:2 * u + 1], C(1), W(b + 4), A.not_equal, C(7), A.add)
+        ts(["ps1"], ["gs"], T.gs[:, 0:24], T.ps1[:, 0:24], -256.0, A.add)
+        tt(["gs", "offx%d" % u, "offv", "coef%da" % u, "coef%db" % u], ["own%d" % u], T["land%d" % u][:, 32 * rank:32 * rank + 32],
+           T.gs[:, 0:24].indirect(T.offx[:, 2 * u:2 * u + 2]), T["coef%d" % u][:], A.mult)
+        send(u)
+        record(t)
+
+    def fixes(t):
+        b, u, n = 8 * t, t + 1, S0 + t
+        ts(["c01", "w4%d" % t], ["w6%d" % t], W(b + 6), C(1), W(b + 4), A.is_equal, -30000.0, A.mult)
+        ts(["x16", "w5%d" % t], ["lv%d" % u], T["lv%d" % u][:], T.x16[:, 0:128], W(b + 5), A.is_equal, -256.0, A.mult)
+        ts(["coef%da" % u, "coef%db" % u], ["cor%d" % u], T["cor%d" % u][:], T["coef%d" % u][:, 0:16], 2048.0, A.mult)
+        ts(["x16", "w5%d" % t, "w6%d" % t], ["dead%d" % u], T["dead%d" % u][:], T.x16[:, 0:16], W(b + 5), A.is_equal, W(b + 6), A.mult)
+        ms(["lv%d" % u], T["lv%d" % u][:, n:128:16], 256.0)
+        key_open(u)
+        key_close(u)
+
+    send(0)
+    key_open(0)
+    key_close(0)
+
+    ts(["cur0"], ["ps3a"], P(0, -4, 149), S("cur0", -4, 149), -16.0, A.mult, 111.0, A.add)
+    ts(["c2_"], ["c7"], C(7), C(2), 3.0 / 16, A.mult)
+    tt(["ps3a", "cur0"], ["c0"], S("c0", -4, 149), P(0, -4, 149), S("cur0", -3, 150), A.subtract)
+    ts(["c7"], ["offv"], T.offx[:, 3:4], C(7), 2.0, A.add)
+    tt(["c0"], ["ps3b"], P(1, -1, 144), S("c0", 0, 145), S("c0", -2, 143), A.not_equal)
+    cp(["c0"], ["cb0a"], T.cb0[:, 0:435:3], S("c0", 0, 145))
+    tt(["ps3b", "c0"], ["cb0b"], T.cb0[:, 4:436:3], P(1, 0, 144), S("c0", 1, 145), A.mult)
+    tt(["ps3b", "c0"], ["cb0c"], T.cb0[:, 5:437:3], P(1, -1, 143), S("c0", -2, 142), A.mult)
+    ts(["c7"], ["offv"], T.offx[:, 5:6], C(7), 2.0, A.add)
+    for u in (1, 2):
+        n = S0 + u - 1
+        ts(["x16"], ["coef%db" % u], T["coef%d" % u][:, n:16], T.x16[:, n:16], float(n), A.is_equal)
+        cp(["i16"], ["coef%db" % u], T["coef%d" % u][:, 16:32], T.i16[:])
+    ts(["i16"], ["corv"], T.corv[:], T.i16[:], 2048.0, A.mult)
+    ts(["xf", "c01"], ["zi"], T.zi[:], T.xf[:], -15.0, A.add, C(0), A.is_equal)
+    ms(["km93"], T.km93[:], -93.0)
+    ts(["zi"], ["i16x"], T.i16x[:], ident, 16.0, A.mult)
+    ts(["zi"], ["i93"], T.i93[:], ident, 93.0, A.mult)
+    ms(["k18"], T.k18[:], 18.0)
+    ts(["cur0"], ["val0"], S("val0", 0, 144), S("cur0", 0, 144), 0.0, A.is_ge)
+    ts(["c01"], ["c11"], C(11), C(1), 1.0, A.add)
+    ts(["xg", "c2_"], ["bones"], T.bones[:], T.xg[:, 0:128], C(2), A.is_equal)
+    ts(["z1", "c11"], ["zw"], T.zw[:, 0:144], T.z1[:, 0:144], C(11), A.mult)
+    ts(["xf", "c01"], ["bt0"], T.bt0[:], T.xf[:, 0:128], C(0), A.is_gt)
+    ts(["zi"], ["btri"], T.btri[:], ident, -4096.0, A.mult)
+    tt(["bt0", "bones"], ["bt0"], T.bt0[:], T.bt0[:], T.bones[:], A.mult)
+    ts(["bones"], ["nbones"], T.nbones[:], T.bones[:], -1.0, A.mult)
+    tt(["bt0", "btri"], ["btri"], T.btri[:], T.btri[:], T.bt0[:], A.add)
+    ms(["k4096"], T.k4096[:], 4096.0)
+    ts(["btri"], ["nbtri"], T.nbtri[:], T.btri[:], -1.0, A.mult)
+    ts(["c16", "c01"], ["jt"], T.jt[:, 0:CH], T.c16[:, 0:CH], C(1), A.add)
+    ts(["sm0", "c01"], ["offd"], T.offd[:], T.sm[:, 0:18], C(1), A.add)
+    ts(["jt"], ["smi"], T.smi[:, 0:9], T.jt[:, 0:9], 1.0 / 9, A.mult, -4.0 / 9, A.add)
+    ts(["pi"], ["pg"], T.pi[:, 2:3], T.pi[:, 0:1], 16, A.bitwise_and)
+    ts(["jt"], ["thr"], T.thr[:, 0:9], T.jt[:, 0:9], 32.0, A.mult)
+    cp(["pg"], ["c12"], C(12), T.pi[:, 2:3])
+    ms(["y0z"], T.y0[:, 0:1], 0.0)
+    ts(["smi", "c12"], ["sm1"], T.sm[:, 20:29], T.smi[:, 0:9], -287.0, A.mult, C(12), A.add)
+    ms(["symz"], T.symw[:, 0:1], 15.0)
+    tt(["thr", "sm1"], ["sm1"], T.sm[:, 20:29], T.sm[:, 20:29], T.thr[:, 0:9], A.add)
+    ms(["oo0"], T.oo[:, 0:1], 0.0)
+    cp(["sm1"], ["offt"], T.offt[:, 0:9], T.sm[:, 20:29])
+    ts(["jt"], ["thr"], T.thr[:, 0:9], T.jt[:, 0:9], 16.0, A.mult, 15.5, A.add)
+    ms(["g20"], T.g2[:, 0:1], 0.0)
+
+    winner(0)
+    delta(0)
+    tie0 = W(2)
+    ts(["c0", "w20"], ["h0"], S("h0", -4, 149), S("c0", -4, 149), tie0, A.is_equal)
+    lin("ps0", 152, [("zi", "cur0", -3), ("i16x", "h0", -3), ("i16x", "h0", -4)])
+    act(["ps0"], ["rc1"], S("rc1", -3, 149), T.ps0[:, 0:152], F.Relu, bias=12.0, scale=-1.0)
+    lin("ps6", 151, [("zi", "km93", -3), ("i93", "h0", -3), ("i16x", "rc1", -3), ("zi", "rc1", -2)])
+    act(["ps6"], ["cz"], S("cz", -3, 148), T.ps6[:, 0:151], F.Copy)
+    oh_a("rc1", 144, [(10, 2), (11, 1), (12, 0)])
+    ts(["c0", "w20"], ["ps3b"], P(1, -4, 149), S("c0", -4, 149), tie0, A.not_equal)
+    fixes(0)
+    oh_v("rc1", 144, 0, 12)
+    oh_v("rc1", 144, 1, 11)
+    tt(["ps6", "h0"], ["ne"], S("ne", -1, 147), T.ps6[:, 3:151], S("h0", -1, 147), A.mult)
+    scan(["h0", "cz"], ["cbk"], S("cbk", -2, 147), S("h0", -3, 146), S("cz", -3, 146), 0.0, A.mult, A.add)
+    tt(["ps6", "ne"], ["ca"], S("ca", -1, 147), T.ps6[:, 2:150], S("ne", -1, 147), A.add)
+    tt(["ps3b", "cbk"], ["ps3c"], P(2, -1, 144), P(1, -1, 144), S("cbk", -1, 144), A.mult)
+    tt(["ps3b", "ca"], ["cb1a"], T.cb1[:, 0:435:3], P(1, -1, 144), S("ca", 0, 145), A.mult)
+    oh_v("rc1", 144, 2, 10)
+    tt(["ps3c", "cb1a"], ["ne"], S("ne", -1, 144), P(2, -1, 144), T.cb1[:, 0:435:3], A.not_equal)
+    oh_v("rc1", 144, 3, 9)
+    tt(["ps3c", "ne"], ["cb1c"], T.cb1[:, 5:437:3], P(2, -1, 143), S("ne", -1, 143), A.mult)
+    tt(["cb1a", "ne"], ["cb1b"], T.cb1[:, 4:436:3], T.cb1[:, 3:435:3], S("ne", 0, 144), A.mult)
+    for s in range(4, 10):
+        oh_v("rc1", 144, s, 12 - s)
+
+    winner(1)
+    delta(1)
+    tie1 = W(10)
+    ts(["ca", "w21"], ["ma"], S("ma", -1, 147), S("ca", -1, 147), tie1, A.is_equal, -16.0, A.mult)
+    ts(["cbk", "w21"], ["mb"], S("mb", -1, 147), S("cbk", -1, 147), tie1, A.is_equal, -16.0, A.mult)
+    ts(["cz", "w21"], ["h1"], S("h1", -1, 146), S("cz", -1, 146), tie1, A.is_equal)
+    lin("ps0", 148, [("zi", "rc1", -1), ("zi", "ma", -1), ("zi", "mb", -1)])
+    act(["ps0"], ["rc2"], S("rc2", -1, 147), T.ps0[:, 0:148], F.Relu, bias=1.0)
+    lin("ps7", 147, [("zi", "h0", -1), ("zi", "h1", -1)])
+    lin("ps6", 147, [("zi", "k18", -1), ("i16x", "rc2", -1), ("zi", "rc2", 0)])
+    fixes(1)
+    tt(["ps7", "val0"], ["kk"], T.kk[:, 0:CH], T.ps7[:, 0:CH], S("val0", 0, 144), A.is_lt)
+    ts(["ps7"], ["tmpb"], S("tmpb", 0, 146), T.ps7[:, 1:147], 0.5, A.is_lt)
+    tt(["ps6", "kk"], ["ek"], T.ek[:, 0:CH], T.ps6[:, 0:CH], T.kk[:, 0:CH], A.mult)
+    tt(["ps6", "tmpb"], ["cz2"], S("cz2", 0, 146), T.ps6[:, 1:147], S("tmpb", 0, 146), A.mult)
+    cp(["ek", "offd"], ["xd"], T.xd[:], T.ek[:, 0:CH].indirect(T.offd[:, 0:18]))
+    tt(["ps7", "cz2"], ["ps3a"], P(0, 0, 145), S("cz2", 1, 146), T.ps7[:, 1:146], A.mult)
+    op("v", ["xd"], ["xt"], lambda: V.transpose(T.xt[:], T.xd[:]))
+    tt(["ps3a", "cz2"], ["s1"], S("s1", 0, 145), P(0, 0, 145), S("cz2", 0, 145), A.add)
+    ts(["xt", "offt"], ["et"], T.et[:, 0:CH], T.xt[:, 0:288].indirect(T.offt[:, 0:9]), -128.0, A.add)
+    tt(["ps7", "s1"], ["ps3b"], P(1, 0, 144), S("s1", 1, 145), T.ps7[:, 1:145], A.mult)
+    ts(["et"], ["kt"], T.kt[:, 0:CH], T.et[:, 0:CH], -127.5, A.is_gt)
+    tt(["ps3b", "cz2"], ["ca2"], S("ca2", 0, 144), P(1, 0, 144), S("cz2", 0, 144), A.add)
+    mm(["bones", "kt"], ["ps4"], T.ps4[:, 0:CH], T.bones[:], T.kt[:, 0:CH], True, False)
+    mm(["zi", "k4096"], ["ps5"], T.ps5[:, 0:CH], ident, T.k4096[:], True, False)
+    mm(["btri", "kt"], ["ps5"], T.ps5[:, 0:CH], T.btri[:], T.kt[:, 0:CH], False, False)
+
+    winner(2)
+    ts(["et", "w02", "w12"], ["nd"], T.nd[:, 0:CH], T.et[:, 0:CH], W(17), A.add, W(16), A.is_equal)
+    mm(["nbones", "nd"], ["ps4"], T.ps4[:, 0:CH], T.nbones[:], T.nd[:, 0:CH], False, True)
+    mm(["nbtri", "nd"], ["ps5"], T.ps5[:, 0:CH], T.nbtri[:], T.nd[:, 0:CH], False, True)
+    ts(["w02", "w12"], ["w62"], W(22), W(16), W(17), A.subtract, 128.0, A.add)
+    scan(["ps4", "k4096"], ["oo"], T.oo[:, 1:145], T.ps4[:, 0:CH], T.k4096[:], 0.0, A.add, A.min)
+    ts(["ca2", "w62"], ["m14"], S("m14", 0, 144), S("ca2", 0, 144), W(22), A.is_equal, -16.0, A.mult)
+    lin("ps0", CH, [("zi", "rc2", 0), ("zi", "m14", 0)])
+
+    def count(u):
+        act(["oo", "oo0", "thr"], ["eh%d" % u], T.junk[:, CH * u:CH * u + CH], T.oo[:, 0:CH], F.Sign, bias=T.thr[:, u:u + 1],
+            scale=-1.0, accum_out=T.eh[:, u:u + 1])
+
+    count(0)
+    act(["ps0"], ["xs"], T.xs[:, 0:CH], T.ps0[:, 0:CH], F.Relu, bias=1.0)
+    for u in range(1, 9):
+        count(u)
+    dma("s", ["oo"], [], T.fl[:], T.oo[0:128:16, 144:145])
+    tt(["ps5", "oo", "oo0"], ["idx"], T.idx[:], T.ps5[:, 0:CH], T.oo[:, 0:CH], A.add)
+    cp(["oo", "oo0"], ["oi"], T.oi[:], T.oo[:, 0:CH])
+    ts(["idx"], ["zz"], T.zz[:], T.idx[:], 4096 + 15, A.bitwise_and)
+    ts(["oi"], ["om"], T.om[:], T.oi[:], 15, A.bitwise_and)
+    cp(["zz"], ["zb"], T.zb[:, 0:CH], T.zz[:])
+    ts(["om", "c01"], ["ml"], T.ml[:, 0:CH], T.om[:], C(1), A.is_le, 4096.0, A.mult)
+
+    banks = ["ps1", "ps7", "ps2", "ps0", "ps4", "ps5"]
+
+    def rows(k):
+        for i in range(3 * k, min(3 * k + 3, 16)):
+            o = CH * (i - 3 * k)
+            mm(["zi", "xs"], [banks[k]], T[banks[k]][:, o:o + CH], T.zi[:, 15 + i:143 + i], T.xs[:, 0:CH], True, True)
+
+    def rowcopy(k):
+        n = CH * (min(3 * k + 3, 16) - 3 * k)
+        act([banks[k]], ["symw%d" % k], T.symw[:, 1 + 432 * k:1 + 432 * k + n], T[banks[k]][:, 0:n], F.Copy)
+
+    rows(0)
+    rows(1)
+    for r in range(16):
+        ts(["zb"], ["ohz%d" % r], T.ohz[:, CH * r:CH * r + CH], T.zb[:, 0:CH], float(r), A.is_equal)
+        mm(["zw", "ohz%d" % r], ["ps6"], T.ps6[:, 0:CH], T.zw[:, 15 - r:143 - r], T.ohz[:, CH * r:CH * r + CH], r == 0, r == 15)
+    for k in range(2, 6):
+        rows(k)
+    rowcopy(0)
+    rowcopy(1)
+    act(["w02", "w12"], ["w22"], W(18), W(17), F.Identity, bias=W(16), scale=-1.0)
+    act(["w22"], ["w32"], W(19), W(18), F.Identity, bias=104.5 / 16, scale=-1.0 / 16)
+    rowcopy(2)
+    act(["w32"], ["w72"], W(23), W(19), F.Identity, bias=ROUND)
+    rowcopy(3)
+    act(["w72"], ["w42"], W(20), W(23), F.Identity, bias=-ROUND)
+    rowcopy(4)
+    rowcopy(5)
+    record(2)
+    dma("s", ["mg%d%s" % (t, s) for t in range(3) for s in "ab"], [], T.mg[:], T.mgb[0:1, 0:9])
+    ts(["jt", "oo"], ["ps3a"], T.ps3[:, 0:CH], T.jt[:, 0:CH], T.oo[:, 144:145], A.is_lt, 4096.0, A.mult)
+    ts(["eh%d" % u for u in range(9)], ["ehu"], T.ehu[:, 0:9], T.eh[:, 0:9], 0.5, A.mult, 71.0, A.add)
+    tt(["ps6", "c16"], ["av"], T.av[:, 0:CH], T.ps6[:, 0:CH], T.c16[:, 0:CH], A.add)
+    ts(["ps6"], ["lal"], T.lal[:, 0:CH], T.ps6[:, 0:CH], 4096.0, A.mult)
+    tt(["ps6", "ml"], ["llo"], T.llo[:, 0:CH], T.ps6[:, 0:CH], T.ml[:, 0:CH], A.mult)
+    scan(["lal", "av"], ["mal"], T.mal[:, 0:CH], T.lal[:, 0:CH], T.av[:, 0:CH], 0.0, A.max, A.min)
+    scan(["llo", "av"], ["mlo"], T.mlo[:, 0:CH], T.llo[:, 0:CH], T.av[:, 0:CH], 0.0, A.max, A.min)
+    cp(["mal", "ehu"], ["g2"], T.g2[:, 1:145], T.mal[:, 0:CH].indirect(T.ehu[:, 0:9]))
+    tt(["mlo", "ehu", "g2", "g20"], ["tm"], T.tm[:, 0:CH], T.mlo[:, 0:CH].indirect(T.ehu[:, 0:9]), T.g2[:, 0:CH], A.max)
+    tt(["tm", "ps3a"], ["tq"], T.tq[:, 0:CH], T.tm[:, 0:CH], T.ps3[:, 0:CH], A.min)
+    cp(["tq"], ["tu"], T.tu[:], T.tq[:, 0:CH])
+
+    ycut = [0, 48, 92, 128, 144]
+    for k in range(4):
+        a, b = ycut[k], ycut[k + 1]
+        cp(["y00", "y01", "y0z", "tu"], ["yo%d" % k], T.yo[:, 16 * a:16 * b], T.y0[:, 0:L + 1].indirect(T.tu[:, a:b]))
+        dma("s", ["yo%d" % k], [], T.y[:, 16 * a:16 * b], T.yo[:, 16 * a:16 * b])
+    SY = ["symw%d" % k for k in range(6)] + ["symz", "tu"]
+    fcut = [0, 112, 144]
+    for k in range(2):
+        a, b = fcut[k], fcut[k + 1]
+        act(SY, ["fso%d" % k], T.fso[:, 16 * a:16 * b], T.symw[:, 0:L + 1].indirect(T.tu[:, a:b]), F.Identity, bias=14.0, scale=-1.0)
+        dma("a", ["fso%d" % k], [], T.fs[:, 16 * a:16 * b], T.fso[0:128:16, 16 * a:16 * b])
+
+    for q in ("v", "a", "p", "g"):
+        g.wait_ge(T.sem[SEM[q]], cnt[q])
+    for s in ("dpos", "dst", "dle", "dve"):
+        g.wait_ge(T.sem[s], 16)
+    g.wait_ge(T.sem.ls, sent[0])
+    g.wait_ge(T.sem.dout, outs[0])

@@ -10,6 +10,12 @@ HL, HR = 4, 6
 MAGIC = 3221225472.0
 ROUND = 12582912.0
 CNT0 = 28672.0
+PRES = 128.0
+FA = 800
+VCUT = [(44, 72), (26, 44), (8, 26), (0, 8)]
+ACUT = [(72, 100), (100, 118), (118, 136), (136, 144)]
+YCUT, FCUT = [0, 64, 104, 132, 144], [0, 64, 128, 144]
+UA = 4
 PAY = (16, 32, 32)
 
 
@@ -18,26 +24,28 @@ def _sb(n, d):
 
 
 SCRATCH = {}
-for _n in ("cur0", "rc1", "rc2", "c0", "cz", "ca", "cbk", "ne", "h0", "h1", "ma", "mb", "vm", "val0", "cz2", "s1", "kk",
-           "ca2", "ek", "et", "kt", "nd", "m14", "xs", "zb", "z1", "zw", "zi", "tmpb", "ml", "km93", "k18", "sq0", "sq1", "sq2"):
+for _n in ("cur0", "rc1", "rc2", "c0", "cz", "ca", "cbk", "ne", "h0", "h1", "ma", "mb", "s1", "kone", "kbig", "crow",
+           "ca2", "et", "kt", "nd", "m14", "xs", "zb", "z1", "zw", "zi", "tmpb", "km93", "k18", "sq0", "sq1", "sq2"):
     SCRATCH[_n] = _sb(160, "bfloat16")
-for _n in ("xf", "x16", "xg", "c16", "jt", "oo", "av", "llo", "lal", "mlo", "mal", "g2", "tm", "tq", "gs"):
+for _n in ("xf", "x16", "xg", "c16", "jt", "oo", "lo", "ml", "xm", "gs"):
     SCRATCH[_n] = _sb(160, "float32")
-for _n in ("posi", "qi", "ri", "idx", "zz", "oi", "om"):
+for _n in ("posi", "ri"):
     SCRATCH[_n] = _sb(CH, "int32")
-for _n in ("posu", "qu", "ru", "tu"):
+for _n in ("idx", "zz"):
+    SCRATCH[_n] = _sb(CH + 1, "int32")
+for _n in ("posu", "tu"):
     SCRATCH[_n] = _sb(CH, "uint16")
-for _n in ("bones", "btri", "nbones", "nbtri", "bt0", "i16x", "i93"):
+for _n in ("bones", "btri", "nbones", "nbtri", "bt0", "bs0", "i16x", "i93"):
     SCRATCH[_n] = _sb(128, "bfloat16")
 SCRATCH.update({
-    "sti": _sb(SW, "int32"), "lei": _sb(4, "int32"), "pi": _sb(8, "int32"), "col": _sb(64, "float32"),
+    "sti": _sb(SW, "int32"), "stb": _sb(SW, "bfloat16"), "stw": _sb(M + 16, "bfloat16"),
+    "lei": _sb(4, "int32"), "pi": _sb(8, "int32"), "col": _sb(64, "float32"),
     "win": _sb(64, "float32"), "i16": _sb(16, "bfloat16"),
-    "mk": _sb(L, "bfloat16"), "gg": _sb(L + 32, "bfloat16"), "oh": _sb(146 * 16, "bfloat16"),
-    "ves": _sb(M, "bfloat16"), "y0": _sb(L + 16, "bfloat16"), "yo": _sb(L, "bfloat16"),
-    "symw": _sb(L + 16, "bfloat16"), "fso": _sb(L, "float32"),
+    "gg": _sb(L + 32, "bfloat16"), "oh": _sb(146 * 16, "bfloat16"), "cz2": _sb(176, "bfloat16"),
+    "ves": _sb(M + 16, "bfloat16"), "y0": _sb(L + 16, "bfloat16"), "yo": _sb(L, "bfloat16"), "fso": _sb(L, "float32"),
     "cb0": _sb(448, "bfloat16"), "cb1": _sb(448, "bfloat16"), "mrk": _sb(432, "bfloat16"),
-    "ohz": _sb(16 * CH, "bfloat16"), "junk": _sb(9 * CH, "bfloat16"), "xd": _sb(288, "bfloat16"), "xt": _sb(288, "bfloat16"),
-    "k4096": _sb(CH, "bfloat16"), "bsel": _sb(128, "float32"),
+    "ohz": _sb(16 * CH, "bfloat16"), "junk": _sb(9 * 146, "bfloat16"), "xd": _sb(288, "bfloat16"), "xt": _sb(288, "bfloat16"),
+    "bsel": _sb(128, "float32"),
     "sel": _sb(128, "float16"), "lv1": _sb(128, "float16"), "lv2": _sb(128, "float16"),
     "ptie": _sb(48, "float16"), "poff": _sb(16, "float16"), "cor1": _sb(16, "float16"), "cor2": _sb(16, "float16"),
     "corv": _sb(16, "float16"), "dead1": _sb(16, "float16"), "dead2": _sb(16, "float16"),
@@ -52,7 +60,7 @@ for _k in range(8):
     SCRATCH["ps%d" % _k] = ("psum", [128, 512], "float32")
 
 SEMAPHORES = ["sv", "sa", "sp", "sg", "ls", "ad0", "ad1", "ad2", "ar0", "ar1", "ar2", "rl0", "rl1", "rl2",
-              "dpos", "dst", "dle", "dve", "dout"]
+              "dpos", "dst", "dle", "dve", "dsw", "dsy", "dout"]
 
 
 def bits(engines):
@@ -215,55 +223,54 @@ def rank_main(g, core, T, topo):
     dma("s", [], ["posi"], T.posi[:], T.pos[:], "dpos")
     dma("a", [], ["sti"], T.sti[:], T.st[:], "dst")
     dma("s", [], ["lei"], T.lei[0:8, 0:1], T.le[:], "dle")
-    dma("s", ["posi", "sti"], ["ves"], T.ves[:], T.ve[:], "dve")
 
+    iota(["bsel"], T.bsel[0:8, :], [[1, 8], [0, 16]], 0, -1)
+    iota(["c3"], T.col[0:8, 3:4], [[0, 1]], 0, 16)
+    iota(["c16"], T.c16[:, 0:CH], [[16, CH]], 0, 1)
     op("g", [], ["pi"], lambda: g.iota(T.pi[:, 0:1], [[0, 1]], 0, 1))
     iota(["xf"], T.xf[:], [[1, 160]], 0, 0)
-    iota(["xg"], T.xg[:, 0:128], [[16, 8], [0, 16]], 0, 0)
     iota(["x16"], T.x16[:, 0:128], [[0, 8], [1, 16]], 0, 0)
-    iota(["c16"], T.c16[:, 0:CH], [[16, CH]], 0, 0)
+    iota(["xg"], T.xg[:, 0:128], [[16, 8], [0, 16]], 0, 0)
     iota(["sm0"], T.sm[:, 0:18], [[16, 9], [0, 2]], 0, 0)
-    ms(["ggl"], T.gg[:, 0:16], -0.0625)
-    ms(["ggr"], T.gg[:, 16 + L:32 + L], 0.0)
-    for s in range(12, 16):
-        ms(["oh%d" % s], T.oh[:, s:146 * 16:16], 0.0)
-    ts(["pi"], ["pm"], T.pi[:, 1:2], T.pi[:, 0:1], 15, A.bitwise_and)
-    cp(["pi", "pm"], ["c01"], T.col[:, 0:2], T.pi[:, 0:2])
-    tt(["c01"], ["c2_"], C(2), C(0), C(1), A.subtract)
-    ts(["xf", "c01"], ["i16"], T.i16[:], T.xf[:, 0:16], C(1), A.is_equal)
-    ts(["c01"], ["c3"], C(3), C(0), 16.0, A.mult)
-    ts(["xf", "c2_"], ["z1"], T.z1[:, 0:144], T.xf[:, 0:144], -15.0, A.add, C(2), A.is_equal)
-    ts(["c01"], ["c4"], C(4), C(1), -144.0, A.mult, HL - 0.5, A.add)
-    ts(["xg", "c3"], ["bsel"], T.bsel[0:8, :], T.xg[0:8, 0:128], T.col[0:8, 3:4], A.is_equal)
-    cp(["c01"], ["offx0"], T.offx[:, 0:1], C(0))
+    iota(["crowb"], T.crow[:, 1:145], [[16, CH]], 0, 0)
 
-    ts(["posi"], ["qi"], T.qi[:], T.posi[:], 1.0 / SW, A.mult, -111.5 / SW, A.add)
-    cp(["qi"], ["qu"], T.qu[:], T.qi[:])
-    ts(["qi"], ["ps3a"], T.ps3[:, 0:CH], T.qi[:], -float(SW), A.mult)
-    tt(["ps3a", "posi"], ["ri"], T.ri[:], T.ps3[:, 0:CH], T.posi[:], A.add)
-    cp(["ri"], ["ru"], T.ru[:], T.ri[:])
-    cuts = [0, 24, 64, 104, 134, 144]
-    for k in range(len(cuts) - 1):
-        a, b = cuts[k], cuts[k + 1]
-        act(["i16", "qu"], ["mk%d" % k], T.mk[:, 16 * a:16 * b], T.i16[:, 0:16].indirect(T.qu[:, a:b]), F.Copy)
-    done = 0
-    for k in range(len(cuts) - 1):
-        a, b = cuts[k], cuts[k + 1]
-        tt(["sti", "ru", "mk%d" % k], ["gg%d" % k], T.gg[:, 16 + 16 * a:16 + 16 * b],
-           T.sti[:, 0:SW].indirect(T.ru[:, a:b]), T.mk[:, 16 * a:16 * b], A.mult)
-        if k == 0:
-            cp(["lei"], ["lef"], T.col[0:8, 5:6], T.lei[0:8, 0:1])
-            mm(["bsel", "lef"], ["ps4"], T.ps4[:, 0:1], T.bsel[0:8, :], T.col[0:8, 5:6], True, True)
-            act(["ps4", "c4"], ["c6"], C(6), T.ps4[:, 0:1], F.Identity, bias=C(4))
-            act(["xf", "c6"], ["tmpb"], T.tmpb[:, 0:154], T.xf[:, 0:154], F.Sign, bias=C(6), scale=-1.0)
-            act(["tmpb"], ["vm"], T.vm[:, 0:154], T.tmpb[:, 0:154], F.Identity, bias=49.0, scale=50.0)
-        while done < 16 and (CH * done + CH + HR <= 16 * b or b == CH):
-            i = done
-            mm(["z1", "ggl", "ggr"] + ["gg%d" % u for u in range(k + 1)], ["ps0"], T.ps0[:, 0:154], T.z1[:, 15 - i:143 - i],
-               T.gg[:, 16 + CH * i - HL:16 + CH * i + CH + HR], i == 0, i == 15)
-            done += 1
-    cp(["posi"], ["posu"], T.posu[:], T.posi[:])
-    tt(["ps0", "vm"], ["cur0"], T.cur0[:, 0:154], T.ps0[:, 0:154], T.vm[:, 0:154], A.min)
+    ms(["stw0"], T.stw[:, 0:FA], -1.0)
+    act(["stw0"], ["stw2"], T.stw[:, M + 16 - FA:M + 16], T.stw[:, 0:FA], F.Copy)
+    ms(["stw1"], T.stw[:, FA:M + 16 - FA], -1.0)
+    cp(["sti"], ["stb"], T.stb[:], T.sti[:])
+    dma("s", ["stb"], ["stw0", "stw1", "stw2"], T.stw[0:128:16, 0:M], T.stb[:], "dsw")
+    dma("s", [], ["ves"], T.ves[:, 0:M], T.ve[:], "dve")
+    ts(["bsel"], ["bsel"], T.bsel[0:8, :], T.bsel[0:8, :], 0.0, A.is_equal)
+    ts(["lei", "c3"], ["lef"], T.col[0:8, 5:6], T.lei[0:8, 0:1], T.col[0:8, 3:4], A.add)
+    mm(["bsel", "lef"], ["ps4"], T.ps4[:, 0:1], T.bsel[0:8, :], T.col[0:8, 5:6], True, True)
+    ts(["pi"], ["pm"], T.pi[:, 1:2], T.pi[:, 0:1], 15, A.bitwise_and)
+    ms(["ggl"], T.gg[:, 0:16], -1.0)
+    cp(["pi", "pm"], ["c01"], T.col[:, 0:2], T.pi[:, 0:2])
+    ts(["c16", "ps4"], ["ps3a"], T.ps3[:, 0:CH], T.c16[:, 0:CH], T.ps4[:, 0:1], A.is_ge, float(M), A.mult)
+    ts(["c01"], ["c4"], C(4), C(1), 0.0, A.is_equal)
+    tt(["ps3a", "posi"], ["ri"], T.ri[:], T.ps3[:, 0:CH], T.posi[:], A.max)
+    ts(["c01"], ["c9"], C(9), C(0), 15.0, A.add)
+    cp(["ri"], ["posu"], T.posu[:], T.ri[:])
+    ts(["xf", "c9", "c4"], ["z1"], T.z1[:, 0:144], T.xf[:, 0:144], C(9), A.is_equal, C(4), A.mult)
+    ms(["ggr"], T.gg[:, 16 + L:32 + L], -1.0)
+    for s in range(12, 16):
+        act(["xf"], ["oh%d" % s], T.oh[:, s:146 * 16:16], T.xf[:, 0:146], F.Copy, scale=0.0)
+
+    STW = ["stw0", "stw1", "stw2", "posu"]
+    have, todo = [], list(range(16))
+    for (a, b), (c, d) in zip(VCUT, ACUT):
+        cp(STW, ["gg%d" % a], T.gg[:, 16 + 16 * a:16 + 16 * b], T.stw[:, 0:M + 1].indirect(T.posu[:, a:b]))
+        act(STW, ["gg%d" % c], T.gg[:, 16 + 16 * c:16 + 16 * d], T.stw[:, 0:M + 1].indirect(T.posu[:, c:d]), F.Copy)
+        have += [(a, b), (c, d)]
+        for i in list(todo):
+            need = range(max(9 * i - 1, 0), min(9 * i + 10, CH))
+            if all(any(x <= u < z for x, z in have) for u in need):
+                todo.remove(i)
+                mm(["z1", "ggl", "ggr"] + ["gg%d" % x for x, z in have if x < need[-1] + 1 and z > need[0]], ["ps0"],
+                   T.ps0[:, 0:154], T.z1[:, 15 - i:143 - i], T.gg[:, 16 + CH * i - HL:16 + CH * i + CH + HR],
+                   len(todo) == 15, len(todo) == 0)
+    ms(["vesz"], T.ves[:, M:M + 16], 0.0)
+    cp(["ps0"], ["cur0"], T.cur0[:, 0:154], T.ps0[:, 0:154])
 
     def oh_v(cur, n, s, val):
         ts([cur], ["oh%d" % s], T.oh[:, s:16 * n:16], S(cur, 0, n), float(val), A.is_equal)
@@ -275,14 +282,16 @@ def rank_main(g, core, T, topo):
             act(["sq%d" % k], ["oh%d" % s], T.oh[:, s:16 * n:16], T["sq%d" % k][:, 0:n], F.Relu, bias=1.0, scale=-1.0)
 
     OH = ["oh%d" % s for s in range(16)]
-    oh_a("cur0", 145, [(10, 10), (11, 11)])
-    for s in range(10):
+    oh_a("cur0", 145, [(11, 11)])
+    for s in range(11):
         oh_v("cur0", 145, s, s)
     for m in range(18):
         mm(OH, ["ps1"], T.ps1[:, 0:128], T.oh[:, 128 * m:128 * m + 128], T.oh[:, 128 * m + 16:128 * m + 144], m == 0, m == 17)
-    for k in range(2):
-        act(["ves", "posu"], ["y0%d" % k], T.y0[:, 1 + 1152 * k:1 + 1152 * (k + 1)],
-            T.ves[:, 0:M].indirect(T.posu[:, 72 * k:72 * (k + 1)]), F.Copy)
+    act(["ves", "vesz", "posu"], ["y0"], T.y0[:, 0:L], T.ves[:, 0:M + 1].indirect(T.posu[:]), F.Copy)
+    tt(["c01"], ["c2_"], C(2), C(0), C(1), A.subtract)
+    ts(["xf", "c01"], ["i16"], T.i16[:], T.xf[:, 0:16], C(1), A.is_equal)
+    cp(["c01"], ["offx0"], T.offx[:, 0:1], C(0))
+    ts(["ps4", "c01"], ["c6"], C(6), T.ps4[:, 0:1], C(0), A.subtract, -float(L), A.add)
     ts(["x16", "c01"], ["sel"], T.sel[:], T.x16[:, 0:128], C(1), A.is_equal, 256.0, A.mult)
     ts(["c01"], ["c8"], C(8), C(1), -16.0, A.mult, 111.0, A.add)
     ms(["ptieb"], T.ptie[:, 16:48], -30000.0)
@@ -416,31 +425,36 @@ def rank_main(g, core, T, topo):
     ts(["zi"], ["i16x"], T.i16x[:], ident, 16.0, A.mult)
     ts(["zi"], ["i93"], T.i93[:], ident, 93.0, A.mult)
     ms(["k18"], T.k18[:], 18.0)
-    ts(["cur0"], ["val0"], S("val0", 0, 144), S("cur0", 0, 144), 0.0, A.is_ge)
-    ts(["c01"], ["c11"], C(11), C(1), 1.0, A.add)
-    ts(["xg", "c2_"], ["bones"], T.bones[:], T.xg[:, 0:128], C(2), A.is_equal)
-    ts(["z1", "c11"], ["zw"], T.zw[:, 0:144], T.z1[:, 0:144], C(11), A.mult)
+    ts(["c01"], ["c11"], C(11), C(1), PRES, A.add)
+    ts(["c2_"], ["c14"], C(14), C(2), 15.0, A.add)
+    ts(["xg", "c2_"], ["bones"], T.bones[:], T.xg[:, 0:128], C(2), A.is_equal, 2.0, A.mult)
+    ts(["xf", "c14", "c11"], ["zw"], T.zw[:, 0:144], T.xf[:, 0:144], C(14), A.is_equal, C(11), A.mult)
     ts(["xf", "c01"], ["bt0"], T.bt0[:], T.xf[:, 0:128], C(0), A.is_gt)
-    ts(["zi"], ["btri"], T.btri[:], ident, -4096.0, A.mult)
+    ts(["xg", "c01"], ["bs0"], T.bs0[:], T.xg[:, 0:128], C(0), A.is_equal)
     tt(["bt0", "bones"], ["bt0"], T.bt0[:], T.bt0[:], T.bones[:], A.mult)
     ts(["bones"], ["nbones"], T.nbones[:], T.bones[:], -1.0, A.mult)
-    tt(["bt0", "btri"], ["btri"], T.btri[:], T.btri[:], T.bt0[:], A.add)
-    ms(["k4096"], T.k4096[:], 4096.0)
+    tt(["bt0", "zi"], ["btri"], T.btri[:], T.bt0[:], ident, A.subtract)
+    ms(["kbig"], T.kbig[:], 8192.0)
     ts(["btri"], ["nbtri"], T.nbtri[:], T.btri[:], -1.0, A.mult)
-    ts(["c16", "c01"], ["jt"], T.jt[:, 0:CH], T.c16[:, 0:CH], C(1), A.add)
+    ms(["kone"], T.kone[:], 1.0)
+    ms(["crowa"], T.crow[:, 0:1], 0.0)
+    ms(["crowc"], T.crow[:, 145:147], L + PRES)
+    ms(["kt1"], T.kt[:, CH:CH + 1], 1.0)
+    ms(["lo0"], T.lo[:, 145:146], 0.0)
+    ts(["c01"], ["c13"], C(13), C(1), 16384.0, A.mult, 12288.0, A.add)
+    ts(["c16", "c2_"], ["jt"], T.jt[:, 0:16], T.c16[:, 0:16], C(2), A.subtract)
     ts(["sm0", "c01"], ["offd"], T.offd[:], T.sm[:, 0:18], C(1), A.add)
     ts(["jt"], ["smi"], T.smi[:, 0:9], T.jt[:, 0:9], 1.0 / 9, A.mult, -4.0 / 9, A.add)
     ts(["pi"], ["pg"], T.pi[:, 2:3], T.pi[:, 0:1], 16, A.bitwise_and)
     ts(["jt"], ["thr"], T.thr[:, 0:9], T.jt[:, 0:9], 32.0, A.mult)
     cp(["pg"], ["c12"], C(12), T.pi[:, 2:3])
-    ms(["y0z"], T.y0[:, 0:1], 0.0)
+    ms(["y0z"], T.y0[:, L:L + 1], 0.0)
     ts(["smi", "c12"], ["sm1"], T.sm[:, 20:29], T.smi[:, 0:9], -287.0, A.mult, C(12), A.add)
-    ms(["symz"], T.symw[:, 0:1], 15.0)
+    ms(["ggr"], T.gg[:, 16 + L:32 + L], 15.0)
     tt(["thr", "sm1"], ["sm1"], T.sm[:, 20:29], T.sm[:, 20:29], T.thr[:, 0:9], A.add)
     ms(["oo0"], T.oo[:, 0:1], 0.0)
     cp(["sm1"], ["offt"], T.offt[:, 0:9], T.sm[:, 20:29])
-    ts(["jt"], ["thr"], T.thr[:, 0:9], T.jt[:, 0:9], 16.0, A.mult, 15.5, A.add)
-    ms(["g20"], T.g2[:, 0:1], 0.0)
+    ts(["jt"], ["thr"], T.thr[:, 0:9], T.jt[:, 0:9], 32.0, A.mult, 31.0, A.add)
 
     winner(0)
     delta(0)
@@ -479,104 +493,77 @@ def rank_main(g, core, T, topo):
     lin("ps7", 147, [("zi", "h0", -1), ("zi", "h1", -1)])
     lin("ps6", 147, [("zi", "k18", -1), ("i16x", "rc2", -1), ("zi", "rc2", 0)])
     fixes(1)
-    tt(["ps7", "val0"], ["kk"], T.kk[:, 0:CH], T.ps7[:, 0:CH], S("val0", 0, 144), A.is_lt)
-    ts(["ps7"], ["tmpb"], S("tmpb", 0, 146), T.ps7[:, 1:147], 0.5, A.is_lt)
-    tt(["ps6", "kk"], ["ek"], T.ek[:, 0:CH], T.ps6[:, 0:CH], T.kk[:, 0:CH], A.mult)
-    tt(["ps6", "tmpb"], ["cz2"], S("cz2", 0, 146), T.ps6[:, 1:147], S("tmpb", 0, 146), A.mult)
-    cp(["ek", "offd"], ["xd"], T.xd[:], T.ek[:, 0:CH].indirect(T.offd[:, 0:18]))
-    tt(["ps7", "cz2"], ["ps3a"], P(0, 0, 145), S("cz2", 1, 146), T.ps7[:, 1:146], A.mult)
+    ts(["ps7"], ["tmpb"], S("tmpb", -1, 146), T.ps7[:, 0:147], 0.5, A.is_lt)
+    tt(["ps6", "tmpb"], ["cz2"], T.cz2[:, 16:163], T.ps6[:, 0:147], S("tmpb", -1, 146), A.mult)
+    cp(["cz2", "offd"], ["xd"], T.xd[:], T.cz2[:, 16:16 + CH].indirect(T.offd[:, 0:18]))
+    tt(["ps7", "cz2"], ["ps3a"], P(0, 0, 145), T.cz2[:, 18:163], T.ps7[:, 1:146], A.mult)
     op("v", ["xd"], ["xt"], lambda: V.transpose(T.xt[:], T.xd[:]))
-    tt(["ps3a", "cz2"], ["s1"], S("s1", 0, 145), P(0, 0, 145), S("cz2", 0, 145), A.add)
+    tt(["ps3a", "cz2"], ["s1"], S("s1", 0, 145), P(0, 0, 145), T.cz2[:, 17:162], A.add)
     ts(["xt", "offt"], ["et"], T.et[:, 0:CH], T.xt[:, 0:288].indirect(T.offt[:, 0:9]), -128.0, A.add)
     tt(["ps7", "s1"], ["ps3b"], P(1, 0, 144), S("s1", 1, 145), T.ps7[:, 1:145], A.mult)
     ts(["et"], ["kt"], T.kt[:, 0:CH], T.et[:, 0:CH], -127.5, A.is_gt)
-    tt(["ps3b", "cz2"], ["ca2"], S("ca2", 0, 144), P(1, 0, 144), S("cz2", 0, 144), A.add)
-    mm(["bones", "kt"], ["ps4"], T.ps4[:, 0:CH], T.bones[:], T.kt[:, 0:CH], True, False)
-    mm(["zi", "k4096"], ["ps5"], T.ps5[:, 0:CH], ident, T.k4096[:], True, False)
-    mm(["btri", "kt"], ["ps5"], T.ps5[:, 0:CH], T.btri[:], T.kt[:, 0:CH], False, False)
+    tt(["ps3b", "cz2"], ["ca2"], S("ca2", 0, 144), P(1, 0, 144), T.cz2[:, 17:161], A.add)
+    mm(["bones", "kt", "kt1"], ["ps4"], T.ps4[:, 0:145], T.bones[:], T.kt[:, 0:145], True, False)
+    mm(["zi", "kone"], ["ps5"], T.ps5[:, 0:145], ident, T.kone[:, 0:145], True, False)
+    mm(["btri", "kt", "kt1"], ["ps5"], T.ps5[:, 0:145], T.btri[:], T.kt[:, 0:145], False, False)
+    mm(["zi", "crowa", "crowb", "crowc"], ["ps6"], T.ps6[:, 0:147], ident, T.crow[:, 0:147], True, False)
 
     winner(2)
     ts(["et", "w02", "w12"], ["nd"], T.nd[:, 0:CH], T.et[:, 0:CH], W(17), A.add, W(16), A.is_equal)
     mm(["nbones", "nd"], ["ps4"], T.ps4[:, 0:CH], T.nbones[:], T.nd[:, 0:CH], False, True)
     mm(["nbtri", "nd"], ["ps5"], T.ps5[:, 0:CH], T.nbtri[:], T.nd[:, 0:CH], False, True)
     ts(["w02", "w12"], ["w62"], W(22), W(16), W(17), A.subtract, 128.0, A.add)
-    scan(["ps4", "k4096"], ["oo"], T.oo[:, 1:145], T.ps4[:, 0:CH], T.k4096[:], 0.0, A.add, A.min)
     ts(["ca2", "w62"], ["m14"], S("m14", 0, 144), S("ca2", 0, 144), W(22), A.is_equal, -16.0, A.mult)
     lin("ps0", CH, [("zi", "rc2", 0), ("zi", "m14", 0)])
+    scan(["ps4", "kbig"], ["oo"], T.oo[:, 1:146], T.ps4[:, 0:145], T.kbig[:, 0:145], 0.0, A.add, A.min)
 
     def count(u):
-        act(["oo", "oo0", "thr"], ["eh%d" % u], T.junk[:, CH * u:CH * u + CH], T.oo[:, 0:CH], F.Sign, bias=T.thr[:, u:u + 1],
-            scale=-1.0, accum_out=T.eh[:, u:u + 1])
+        c0 = 0 if u < UA else 16 * UA
+        act(["oo", "oo0", "thr"], ["eh%d" % u], T.junk[:, 146 * u + c0:146 * u + 146], T.oo[:, c0:146], F.Sign,
+            bias=T.thr[:, u:u + 1], scale=-1.0, accum_out=T.eh[:, u:u + 1])
 
-    count(0)
     act(["ps0"], ["xs"], T.xs[:, 0:CH], T.ps0[:, 0:CH], F.Relu, bias=1.0)
-    for u in range(1, 9):
+    dma("s", ["xs"], ["gg%d" % a for a, _ in VCUT + ACUT], T.gg[0:128:16, 16:16 + L], T.xs[:, 0:CH], "dsy")
+    tt(["ps5", "oo", "oo0"], ["idx"], T.idx[:], T.ps5[:, 0:145], T.oo[:, 0:145], A.add)
+    ts(["idx"], ["zz"], T.zz[:], T.idx[:], 31, A.bitwise_and)
+    cp(["zz"], ["zb"], T.zb[:, 0:145], T.zz[:])
+    mm(["bs0", "zb"], ["ps7"], T.ps7[:, 0:145], T.bs0[:], T.zb[:, 0:145], True, True)
+    for u in range(9):
         count(u)
-    dma("s", ["oo"], [], T.fl[:], T.oo[0:128:16, 144:145])
-    tt(["ps5", "oo", "oo0"], ["idx"], T.idx[:], T.ps5[:, 0:CH], T.oo[:, 0:CH], A.add)
-    cp(["oo", "oo0"], ["oi"], T.oi[:], T.oo[:, 0:CH])
-    ts(["idx"], ["zz"], T.zz[:], T.idx[:], 4096 + 15, A.bitwise_and)
-    ts(["oi"], ["om"], T.om[:], T.oi[:], 15, A.bitwise_and)
-    cp(["zz"], ["zb"], T.zb[:, 0:CH], T.zz[:])
-    ts(["om", "c01"], ["ml"], T.ml[:, 0:CH], T.om[:], C(1), A.is_le, 4096.0, A.mult)
-
-    banks = ["ps1", "ps7", "ps2", "ps0", "ps4", "ps5"]
-
-    def rows(k):
-        for i in range(3 * k, min(3 * k + 3, 16)):
-            o = CH * (i - 3 * k)
-            mm(["zi", "xs"], [banks[k]], T[banks[k]][:, o:o + CH], T.zi[:, 15 + i:143 + i], T.xs[:, 0:CH], True, True)
-
-    def rowcopy(k):
-        n = CH * (min(3 * k + 3, 16) - 3 * k)
-        act([banks[k]], ["symw%d" % k], T.symw[:, 1 + 432 * k:1 + 432 * k + n], T[banks[k]][:, 0:n], F.Copy)
-
-    rows(0)
-    rows(1)
+        if u == UA - 1:
+            act(["ps7", "c13"], ["ml"], T.ml[:, 0:145], T.ps7[:, 0:145], F.Identity, bias=C(13), scale=-8192.0)
     for r in range(16):
-        ts(["zb"], ["ohz%d" % r], T.ohz[:, CH * r:CH * r + CH], T.zb[:, 0:CH], float(r), A.is_equal)
-        mm(["zw", "ohz%d" % r], ["ps6"], T.ps6[:, 0:CH], T.zw[:, 15 - r:143 - r], T.ohz[:, CH * r:CH * r + CH], r == 0, r == 15)
-    for k in range(2, 6):
-        rows(k)
-    rowcopy(0)
-    rowcopy(1)
-    act(["w02", "w12"], ["w22"], W(18), W(17), F.Identity, bias=W(16), scale=-1.0)
-    act(["w22"], ["w32"], W(19), W(18), F.Identity, bias=104.5 / 16, scale=-1.0 / 16)
-    rowcopy(2)
-    act(["w32"], ["w72"], W(23), W(19), F.Identity, bias=ROUND)
-    rowcopy(3)
-    act(["w72"], ["w42"], W(20), W(23), F.Identity, bias=-ROUND)
-    rowcopy(4)
-    rowcopy(5)
-    record(2)
-    dma("s", ["mg%d%s" % (t, s) for t in range(3) for s in "ab"], [], T.mg[:], T.mgb[0:1, 0:9])
-    ts(["jt", "oo"], ["ps3a"], T.ps3[:, 0:CH], T.jt[:, 0:CH], T.oo[:, 144:145], A.is_lt, 4096.0, A.mult)
-    ts(["eh%d" % u for u in range(9)], ["ehu"], T.ehu[:, 0:9], T.eh[:, 0:9], 0.5, A.mult, 71.0, A.add)
-    tt(["ps6", "c16"], ["av"], T.av[:, 0:CH], T.ps6[:, 0:CH], T.c16[:, 0:CH], A.add)
-    ts(["ps6"], ["lal"], T.lal[:, 0:CH], T.ps6[:, 0:CH], 4096.0, A.mult)
-    tt(["ps6", "ml"], ["llo"], T.llo[:, 0:CH], T.ps6[:, 0:CH], T.ml[:, 0:CH], A.mult)
-    scan(["lal", "av"], ["mal"], T.mal[:, 0:CH], T.lal[:, 0:CH], T.av[:, 0:CH], 0.0, A.max, A.min)
-    scan(["llo", "av"], ["mlo"], T.mlo[:, 0:CH], T.llo[:, 0:CH], T.av[:, 0:CH], 0.0, A.max, A.min)
-    cp(["mal", "ehu"], ["g2"], T.g2[:, 1:145], T.mal[:, 0:CH].indirect(T.ehu[:, 0:9]))
-    tt(["mlo", "ehu", "g2", "g20"], ["tm"], T.tm[:, 0:CH], T.mlo[:, 0:CH].indirect(T.ehu[:, 0:9]), T.g2[:, 0:CH], A.max)
-    tt(["tm", "ps3a"], ["tq"], T.tq[:, 0:CH], T.tm[:, 0:CH], T.ps3[:, 0:CH], A.min)
-    cp(["tq"], ["tu"], T.tu[:], T.tq[:, 0:CH])
+        ts(["zb"], ["ohz%d" % r], T.ohz[:, CH * r:CH * r + CH], T.zb[:, 0:CH], 2.0 * r, A.is_equal)
+        mm(["zw", "ohz%d" % r], ["ps6"], T.ps6[:, 1:145], T.zw[:, 15 - r:143 - r], T.ohz[:, CH * r:CH * r + CH], False, r == 15)
+    ts(["eh%d" % u for u in range(UA)], ["ehua"], T.ehu[:, 0:UA], T.eh[:, 0:UA], 0.5, A.mult, 72.0, A.add)
+    ts(["w62"], ["w32"], W(19), W(22), -1.0 / 16, A.mult, 232.5 / 16, A.add)
+    tt(["ps6", "ml"], ["lo"], T.lo[:, 0:145], T.ps6[:, 1:146], T.ml[:, 0:145], A.min)
+    ts(["w32"], ["mg2a"], T.mgb[:, 6:7], W(19), ROUND, A.add, ROUND, A.subtract)
+    scan(["ps6", "lo", "lo0"], ["xm"], T.xm[:, 0:146], T.ps6[:, 0:146], T.lo[:, 0:146], 0.0, A.max, A.max)
+    ts(["mg2a"], ["w72"], W(23), T.mgb[:, 6:7], -16.0, A.mult, 239.0, A.add)
+    ts(["xm", "ehua"], ["tua"], T.tu[:, 0:16 * UA], T.xm[:, 0:146].indirect(T.ehu[:, 0:UA]), -PRES, A.add)
+    ts(["eh%d" % u for u in range(UA, 9)], ["ehub"], T.ehu[:, UA:9], T.eh[:, UA:9], 0.5, A.mult, 72.0 + 8 * UA, A.add)
 
-    ycut = [0, 48, 92, 128, 144]
-    for k in range(4):
-        a, b = ycut[k], ycut[k + 1]
-        cp(["y00", "y01", "y0z", "tu"], ["yo%d" % k], T.yo[:, 16 * a:16 * b], T.y0[:, 0:L + 1].indirect(T.tu[:, a:b]))
-        dma("s", ["yo%d" % k], [], T.y[:, 16 * a:16 * b], T.yo[:, 16 * a:16 * b])
-    SY = ["symw%d" % k for k in range(6)] + ["symz", "tu"]
-    fcut = [0, 112, 144]
-    for k in range(2):
-        a, b = fcut[k], fcut[k + 1]
-        act(SY, ["fso%d" % k], T.fso[:, 16 * a:16 * b], T.symw[:, 0:L + 1].indirect(T.tu[:, a:b]), F.Identity, bias=14.0, scale=-1.0)
-        dma("a", ["fso%d" % k], [], T.fs[:, 16 * a:16 * b], T.fso[0:128:16, 16 * a:16 * b])
+    for a, b in zip(YCUT, YCUT[1:]):
+        tu = "tua" if a == 0 else "tub"
+        cp(["y0", "y0z", tu], ["yo%d" % a], T.yo[:, 16 * a:16 * b], T.y0[:, 0:L + 1].indirect(T.tu[:, a:b]))
+        dma("s", ["yo%d" % a], [], T.y[:, 16 * a:16 * b], T.yo[:, 16 * a:16 * b])
+        if a == 0:
+            ts(["xm", "ehub"], ["tub"], T.tu[:, 16 * UA:CH], T.xm[:, 0:146].indirect(T.ehu[:, UA:9]), -PRES, A.add)
+    act(["oo", "c6"], ["flv"], C(15), T.oo[:, 144:145], F.Identity, bias=C(6), scale=0.5)
+    dma("a", ["flv"], [], T.fl[:], T.col[0:128:16, 15:16])
+    for a, b in zip(FCUT, FCUT[1:]):
+        tu = "tua" if a == 0 else "tub"
+        act(["gg0", "ggr", tu], ["fso%d" % a], T.fso[:, 16 * a:16 * b], T.gg[:, 16:17 + L].indirect(T.tu[:, a:b]), F.Identity,
+            bias=14.0, scale=-1.0)
+        dma("a", ["fso%d" % a], [], T.fs[:, 16 * a:16 * b], T.fso[0:128:16, 16 * a:16 * b])
+    ts(["w72", "w62"], ["mg2c"], T.mgb[:, 7:8], W(23), W(22), A.subtract)
+    ts(["w12"], ["mg2b"], T.mgb[:, 8:9], W(17), 1.0 / 256, A.mult, CNT0, A.add)
+    dma("s", ["mg%d%s" % (t, s) for t in range(3) for s in "ab"] + ["mg2c"], [], T.mg[:], T.mgb[0:1, 0:9])
 
     for q in ("v", "a", "p", "g"):
         g.wait_ge(T.sem[SEM[q]], cnt[q])
-    for s in ("dpos", "dst", "dle", "dve"):
+    for s in ("dpos", "dst", "dle", "dve", "dsw", "dsy"):
         g.wait_ge(T.sem[s], 16)
     g.wait_ge(T.sem.ls, sent[0])
     g.wait_ge(T.sem.dout, outs[0])

@@ -8,13 +8,16 @@ CH = L // 16
 SW = M // 16
 HL, HR = 4, 6
 MAGIC = 3221225472.0
-ROUND = 12582912.0
+MAGIC16 = 201326592.0
+MAGIC32 = 402653184.0
+WCOL = {0: 31, 4: 34, 5: 35, 1: 38}
 CNT0 = 28672.0
 PRES = 128.0
 FA = 800
-VCUT = [(44, 72), (26, 44), (8, 26), (0, 8)]
-ACUT = [(72, 100), (100, 118), (118, 136), (136, 144)]
-YCUT, FCUT = [0, 64, 104, 132, 144], [0, 64, 128, 144]
+VCUT = [(44, 72), (18, 44), (8, 18), (0, 8)]
+ACUT = [(72, 100), (100, 128), (128, 136), (136, 144)]
+YCUT, FCUT = [0, 32, 64, 92, 116, 134, 144], [0, 64, 112, 144]
+Y0CUT = [0, 88, 144]
 UA = 4
 PAY = (16, 32, 32)
 
@@ -24,33 +27,35 @@ def _sb(n, d):
 
 
 SCRATCH = {}
-for _n in ("cur0", "rc1", "rc2", "c0", "cz", "ca", "cbk", "ne", "h0", "h1", "ma", "mb", "s1", "kone", "kbig", "crow",
-           "ca2", "et", "kt", "nd", "m14", "xs", "zb", "z1", "zw", "zi", "tmpb", "km93", "k18", "sq0", "sq1", "sq2"):
+for _n in ("cur0", "rc1", "c0", "ca", "cbk", "ne", "h0", "h1", "ha", "hb", "ht", "ma", "mb", "s1", "kone", "kbig", "crow",
+           "ca2", "et", "kt", "nd", "m14", "xs", "zb", "z1", "zw", "zi", "k35", "vm", "sq0", "sq1", "sq2"):
     SCRATCH[_n] = _sb(160, "bfloat16")
-for _n in ("xf", "x16", "xg", "c16", "jt", "oo", "lo", "ml", "xm", "gs"):
+for _n in ("xf", "x16", "c16", "oo", "lo", "ml", "xm", "gs", "idx", "jc"):
     SCRATCH[_n] = _sb(160, "float32")
 for _n in ("posi", "ri"):
     SCRATCH[_n] = _sb(CH, "int32")
-for _n in ("idx", "zz"):
-    SCRATCH[_n] = _sb(CH + 1, "int32")
-for _n in ("posu", "tu"):
+for _n in ("posu", "posv", "tu"):
     SCRATCH[_n] = _sb(CH, "uint16")
-for _n in ("bones", "btri", "nbones", "nbtri", "bt0", "bs0", "i16x", "i93"):
+for _n in ("bones", "btri", "nbones", "nbtri", "bt0", "bs0", "bup", "nbup", "i16x", "nzi", "n512"):
     SCRATCH[_n] = _sb(128, "bfloat16")
 SCRATCH.update({
     "sti": _sb(SW, "int32"), "stb": _sb(SW, "bfloat16"), "stw": _sb(M + 16, "bfloat16"),
     "lei": _sb(4, "int32"), "pi": _sb(8, "int32"), "col": _sb(64, "float32"),
     "win": _sb(64, "float32"), "i16": _sb(16, "bfloat16"),
-    "gg": _sb(L + 32, "bfloat16"), "oh": _sb(146 * 16, "bfloat16"), "cz2": _sb(176, "bfloat16"),
+    "gg": _sb(L + 32, "bfloat16"), "oh": ("sbuf", [128, 146, 16], "bfloat16"), "cz2": _sb(176, "bfloat16"),
     "ves": _sb(M + 16, "bfloat16"), "y0": _sb(L + 16, "bfloat16"), "yo": _sb(L, "bfloat16"), "fso": _sb(L, "float32"),
     "cb0": _sb(448, "bfloat16"), "cb1": _sb(448, "bfloat16"), "mrk": _sb(432, "bfloat16"),
     "ohz": _sb(16 * CH, "bfloat16"), "junk": _sb(9 * 146, "bfloat16"), "xd": _sb(288, "bfloat16"), "xt": _sb(288, "bfloat16"),
-    "bsel": _sb(128, "float32"),
-    "sel": _sb(128, "float16"), "lv1": _sb(128, "float16"), "lv2": _sb(128, "float16"),
+    "bsel": _sb(128, "float32"), "km256": _sb(24, "bfloat16"), "sgn": _sb(24, "bfloat16"),
+    "id32": _sb(128, "float32"), "keep": _sb(48, "float32"), "ctab": _sb(16, "float32"), "xm16": _sb(16, "float32"),
+    "sel": _sb(128, "float16"),
     "ptie": _sb(48, "float16"), "poff": _sb(16, "float16"), "cor1": _sb(16, "float16"), "cor2": _sb(16, "float16"),
     "corv": _sb(16, "float16"), "dead1": _sb(16, "float16"), "dead2": _sb(16, "float16"),
     "coef1": _sb(32, "float32"), "coef2": _sb(32, "float32"), "neg": _sb(48, "float32"),
-    "sc": _sb(64, "float32"), "sct": _sb(32, "float32"), "thr": _sb(16, "float32"), "eh": _sb(16, "float32"),
+    "sc": _sb(64, "float32"), "sct": _sb(40, "float32"), "wo": _sb(120, "float32"), "wadd": _sb(120, "float32"),
+    "x15": ("sbuf", [128, 8, 16], "bfloat16"),
+    "lv1": ("sbuf", [128, 8, 16], "float16"), "lv2": ("sbuf", [128, 8, 16], "float16"),
+    "thr": _sb(16, "float32"), "eh": _sb(16, "float32"),
     "sm": _sb(32, "float32"), "smi": _sb(16, "int32"), "mgb": _sb(16, "float32"),
     "offx": _sb(8, "uint16"), "offd": _sb(18, "uint16"), "offt": _sb(10, "uint16"), "ehu": _sb(10, "uint16"),
     "land0": _sb(8 * 16, "float16"), "land1": _sb(8 * 32, "float16"), "land2": _sb(8 * 32, "float16"),
@@ -59,7 +64,7 @@ SCRATCH.update({
 for _k in range(8):
     SCRATCH["ps%d" % _k] = ("psum", [128, 512], "float32")
 
-SEMAPHORES = ["sv", "sa", "sp", "sg", "ls", "ad0", "ad1", "ad2", "ar0", "ar1", "ar2", "rl0", "rl1", "rl2",
+SEMAPHORES = ["sv", "sa", "sp", "sg", "ls", "ls0", "ls1", "ls2", "ad0", "ad1", "ad2", "ar0", "ar1", "ar2", "rl0", "rl1", "rl2",
               "dpos", "dst", "dle", "dve", "dsw", "dsy", "dout"]
 
 
@@ -90,7 +95,7 @@ def relay_main(g, core, T, topo, owner, dests):
     r = T.rank_of(owner)
     eng = topo.engines(core, dests[0])
     per = len(eng) // len(dests)
-    n_in = len(topo.engines(owner, core)) // 2
+    n_in = (len(topo.engines(owner, core)) - len(eng)) // 2
     for t in range(3):
         w = PAY[t]
         g.wait_ge(T.sem["rl%d" % t], n_in)
@@ -195,16 +200,22 @@ def rank_main(g, core, T, topo):
     def mm(r, w, out, lhsT, rhs, start, stop):
         op("p", r, w, lambda: PE.matmul(out, lhsT, rhs, start, stop))
 
-    def lin(bank, n, terms):
+    def lin(bank, n, terms, first=True, last=True):
         for k, (mat, name, lo) in enumerate(terms):
             lhsT = ident if mat == "zi" else T[mat][:]
-            mm([mat, name], [bank], T[bank][:, 0:n], lhsT, S(name, lo, lo + n), k == 0, k == len(terms) - 1)
+            mm([mat, name], [bank], T[bank][:, 0:n], lhsT, S(name, lo, lo + n), first and k == 0, last and k == len(terms) - 1)
 
     def act(r, w, out, in_, func, **kw):
         op("a", r, w, lambda: ACT.activation(out, in_, func, **kw))
 
     def iota(w, out, pat, base, cm):
         op("g", [], w, lambda: g.iota(out, pat, base, cm, allow_small_or_imprecise_dtypes=True))
+
+    def select(r, w, out, in_, pat, cmp, fill, base, cm):
+        op("g", r, w, lambda: g.affine_select(out, in_, pat, cmp, fill, base, cm))
+
+    def aff(r, w, out, in_, scale, bias):
+        act(r, w, out, in_, F.Identity, bias=bias, scale=scale)
 
     def S(name, lo, hi):
         return T[name][:, HL + lo:HL + hi]
@@ -216,6 +227,8 @@ def rank_main(g, core, T, topo):
         return T.col[:, k:k + 1]
 
     def W(k):
+        if k % 8 in WCOL:
+            return T.wo[:, 40 * (k // 8) + WCOL[k % 8]:40 * (k // 8) + WCOL[k % 8] + 1]
         return T.win[:, k:k + 1]
 
     ident = T.zi[:, 15:143]
@@ -225,14 +238,24 @@ def rank_main(g, core, T, topo):
     dma("s", [], ["lei"], T.lei[0:8, 0:1], T.le[:], "dle")
 
     iota(["bsel"], T.bsel[0:8, :], [[1, 8], [0, 16]], 0, -1)
-    iota(["c3"], T.col[0:8, 3:4], [[0, 1]], 0, 16)
-    iota(["c16"], T.c16[:, 0:CH], [[16, CH]], 0, 1)
+    iota(["c3"], T.col[0:8, 21:22], [[0, 1]], 0, 16)
+    iota(["c3"], T.col[0:8, 22:23], [[0, 1]], 0, L)
     op("g", [], ["pi"], lambda: g.iota(T.pi[:, 0:1], [[0, 1]], 0, 1))
     iota(["xf"], T.xf[:], [[1, 160]], 0, 0)
+    iota(["kone"], T.kone[:], [[0, 160]], 1, 0)
+    iota(["jc"], T.jc[:, 0:154], [[1, 154]], -HL, CH)
+    select(["kone"], ["zi"], T.zi[:], T.kone[:], [[1, 160]], A.is_equal, 0.0, -15, -1)
+    iota(["c16"], T.c16[:, 0:CH], [[16, CH]], 0, 1)
     iota(["x16"], T.x16[:, 0:128], [[0, 8], [1, 16]], 0, 0)
-    iota(["xg"], T.xg[:, 0:128], [[16, 8], [0, 16]], 0, 0)
+    iota(["km256"], T.km256[:], [[0, 24]], -256, 0)
+    select(["kone"], ["sgn"], T.sgn[:], T.kone[:, 0:24], [[0, 8], [1, 3]], A.is_gt, -1.0, 0, 0)
+    iota(["x15"], T.x15[:], [[0, 8], [1, 16]], -15, 0)
+    iota(["wadd0"], T.wadd[:], [[0, 120]], 0, 0)
+    for k, (lo, hi, step, base) in enumerate(((32, 120, 0, -8), (35, 80, 16, 96), (36, 80, -16, -96), (115, 116, 0, -96), (116, 117, 0, 96))):
+        op("g", ["wadd0"], ["wadd%d" % min(1 + k, 3)], lambda: g.iota(T.wadd[:, lo:hi:40], [[step, len(range(lo, hi, 40))]], base, 0,
+                                                                      allow_small_or_imprecise_dtypes=True))
     iota(["sm0"], T.sm[:, 0:18], [[16, 9], [0, 2]], 0, 0)
-    iota(["crowb"], T.crow[:, 1:145], [[16, CH]], 0, 0)
+    iota(["thr"], T.thr[:, 0:9], [[512, 9]], 31, 32)
 
     ms(["stw0"], T.stw[:, 0:FA], -1.0)
     act(["stw0"], ["stw2"], T.stw[:, M + 16 - FA:M + 16], T.stw[:, 0:FA], F.Copy)
@@ -241,20 +264,21 @@ def rank_main(g, core, T, topo):
     dma("s", ["stb"], ["stw0", "stw1", "stw2"], T.stw[0:128:16, 0:M], T.stb[:], "dsw")
     dma("s", [], ["ves"], T.ves[:, 0:M], T.ve[:], "dve")
     ts(["bsel"], ["bsel"], T.bsel[0:8, :], T.bsel[0:8, :], 0.0, A.is_equal)
-    ts(["lei", "c3"], ["lef"], T.col[0:8, 5:6], T.lei[0:8, 0:1], T.col[0:8, 3:4], A.add)
-    mm(["bsel", "lef"], ["ps4"], T.ps4[:, 0:1], T.bsel[0:8, :], T.col[0:8, 5:6], True, True)
     ts(["pi"], ["pm"], T.pi[:, 1:2], T.pi[:, 0:1], 15, A.bitwise_and)
-    ms(["ggl"], T.gg[:, 0:16], -1.0)
+    cp(["lei"], ["lef0"], T.col[0:8, 20:21], T.lei[0:8, 0:1])
+    cp(["posi"], ["posu"], T.posu[:], T.posi[:])
     cp(["pi", "pm"], ["c01"], T.col[:, 0:2], T.pi[:, 0:2])
-    ts(["c16", "ps4"], ["ps3a"], T.ps3[:, 0:CH], T.c16[:, 0:CH], T.ps4[:, 0:1], A.is_ge, float(M), A.mult)
-    ts(["c01"], ["c4"], C(4), C(1), 0.0, A.is_equal)
-    tt(["ps3a", "posi"], ["ri"], T.ri[:], T.ps3[:, 0:CH], T.posi[:], A.max)
-    ts(["c01"], ["c9"], C(9), C(0), 15.0, A.add)
-    cp(["ri"], ["posu"], T.posu[:], T.ri[:])
-    ts(["xf", "c9", "c4"], ["z1"], T.z1[:, 0:144], T.xf[:, 0:144], C(9), A.is_equal, C(4), A.mult)
+    ts(["lef0", "c3"], ["lef"], T.col[0:8, 5:7], T.col[0:8, 21:23], T.col[0:8, 20:21], A.add)
+    mm(["bsel", "lef"], ["ps4"], T.ps4[:, 0:2], T.bsel[0:8, :], T.col[0:8, 5:7], True, True)
+    ms(["ggl"], T.gg[:, 0:16], -1.0)
     ms(["ggr"], T.gg[:, 16 + L:32 + L], -1.0)
+    ts(["c01"], ["c4"], C(4), C(1), 0.0, A.is_equal)
+    ts(["c01"], ["c9"], C(9), C(0), 15.0, A.add)
+    ts(["jc", "ps4"], ["vm"], T.vm[:, 0:154], T.jc[:, 0:154], T.ps4[:, 1:2], A.is_ge, -100.0, A.mult)
+    ts(["xf", "c9", "c4"], ["z1"], T.z1[:, 0:144], T.xf[:, 0:144], C(9), A.is_equal, C(4), A.mult)
+    mm(["zi", "vm"], ["ps0"], T.ps0[:, 0:154], ident, T.vm[:, 0:154], True, False)
     for s in range(12, 16):
-        act(["xf"], ["oh%d" % s], T.oh[:, s:146 * 16:16], T.xf[:, 0:146], F.Copy, scale=0.0)
+        act(["xf"], ["oh%d" % s], T.oh[:, :, s], T.xf[:, 0:146], F.Copy, scale=0.0)
 
     STW = ["stw0", "stw1", "stw2", "posu"]
     have, todo = [], list(range(16))
@@ -268,42 +292,69 @@ def rank_main(g, core, T, topo):
                 todo.remove(i)
                 mm(["z1", "ggl", "ggr"] + ["gg%d" % x for x, z in have if x < need[-1] + 1 and z > need[0]], ["ps0"],
                    T.ps0[:, 0:154], T.z1[:, 15 - i:143 - i], T.gg[:, 16 + CH * i - HL:16 + CH * i + CH + HR],
-                   len(todo) == 15, len(todo) == 0)
+                   False, len(todo) == 0)
     ms(["vesz"], T.ves[:, M:M + 16], 0.0)
-    cp(["ps0"], ["cur0"], T.cur0[:, 0:154], T.ps0[:, 0:154])
+    ts(["c16", "ps4"], ["ps3a"], T.ps3[:, 0:CH], T.c16[:, 0:CH], T.ps4[:, 0:1], A.is_ge, float(M), A.mult)
+    ts(["ps0"], ["cur0"], T.cur0[:, 0:154], T.ps0[:, 0:154], -1.0, A.max)
+    tt(["ps3a", "posi"], ["ri"], T.ri[:], T.ps3[:, 0:CH], T.posi[:], A.max)
 
     def oh_v(cur, n, s, val):
-        ts([cur], ["oh%d" % s], T.oh[:, s:16 * n:16], S(cur, 0, n), float(val), A.is_equal)
+        ts([cur], ["oh%d" % s], T.oh[:, 0:n, s], S(cur, 0, n), float(val), A.is_equal)
 
     def oh_a(cur, n, pairs):
         for k, (s, val) in enumerate(pairs):
             act([cur], ["sq%d" % k], T["sq%d" % k][:, 0:n], S(cur, 0, n), F.Square, bias=-float(val))
         for k, (s, val) in enumerate(pairs):
-            act(["sq%d" % k], ["oh%d" % s], T.oh[:, s:16 * n:16], T["sq%d" % k][:, 0:n], F.Relu, bias=1.0, scale=-1.0)
+            act(["sq%d" % k], ["oh%d" % s], T.oh[:, 0:n, s], T["sq%d" % k][:, 0:n], F.Relu, bias=1.0, scale=-1.0)
 
     OH = ["oh%d" % s for s in range(16)]
     oh_a("cur0", 145, [(11, 11)])
     for s in range(11):
         oh_v("cur0", 145, s, s)
     for m in range(18):
-        mm(OH, ["ps1"], T.ps1[:, 0:128], T.oh[:, 128 * m:128 * m + 128], T.oh[:, 128 * m + 16:128 * m + 144], m == 0, m == 17)
-    act(["ves", "vesz", "posu"], ["y0"], T.y0[:, 0:L], T.ves[:, 0:M + 1].indirect(T.posu[:]), F.Copy)
+        mm(OH, ["ps1"], T.ps1[:, 0:96], T.oh[:, 8 * m:8 * m + 8, :], T.oh[:, 8 * m + 1:8 * m + 9, 0:S0], m == 0, m == 17)
+    aff(["c01"], ["c8"], C(10), C(1), -16.0, 111.0)
     tt(["c01"], ["c2_"], C(2), C(0), C(1), A.subtract)
     ts(["xf", "c01"], ["i16"], T.i16[:], T.xf[:, 0:16], C(1), A.is_equal)
-    cp(["c01"], ["offx0"], T.offx[:, 0:1], C(0))
-    ts(["ps4", "c01"], ["c6"], C(6), T.ps4[:, 0:1], C(0), A.subtract, -float(L), A.add)
+    ts(["c01"], ["c18"], C(18), C(1), float(S0), A.is_ge, 96.0, A.mult)
+    ms(["gsz"], T.gs[:, 96:97], -256.0)
+    aff(["c2_", "c18"], ["c19"], C(19), C(2), 0.75, C(18))
     ts(["x16", "c01"], ["sel"], T.sel[:], T.x16[:, 0:128], C(1), A.is_equal, 256.0, A.mult)
-    ts(["c01"], ["c8"], C(8), C(1), -16.0, A.mult, 111.0, A.add)
     ms(["ptieb"], T.ptie[:, 16:48], -30000.0)
-    ts(["x16", "c8"], ["ptiea"], T.ptie[:, 0:16], T.x16[:, 0:16], C(8), A.subtract, -1.0 / 2048, A.mult)
+    ts(["x16", "c8"], ["ptiea"], T.ptie[:, 0:16], T.x16[:, 0:16], C(10), A.subtract, -1.0 / 2048, A.mult)
     ts(["i16"], ["poff"], T.poff[:], T.i16[:], -30000.0, A.mult, -CNT0 / 8 + 2048.0, A.add)
+    ts(["c19", "c01"], ["offx0"], T.offx[:, 0:1], C(19), C(1), A.add, 96.0, A.min)
     ms(["neg"], T.neg[:], -1e9)
-    ts(["ps1"], ["gs"], T.gs[:, 0:128], T.ps1[:, 0:128], -256.0, A.add)
-    cp(["gs", "offx0"], ["own0"], T.land0[:, 16 * rank:16 * rank + 16], T.gs[:, 0:128].indirect(T.offx[:, 0:1]))
+    cp(["ri"], ["posv"], T.posv[:], T.ri[:])
+    ts(["cur0"], ["ps3a"], P(0, -4, 149), S("cur0", -4, 149), -16.0, A.mult, 111.0, A.add)
+    aff(["c2_"], ["c7"], C(7), C(2), 3.0 / 16, 0.0)
+    aff(["c2_"], ["c7"], C(8), C(2), 3.0 / 16, 0.0)
+    aff(["zi"], ["nzi"], T.nzi[:], ident, -1.0, 0.0)
+    aff(["zi"], ["i16x"], T.i16x[:], ident, 16.0, 0.0)
+    act(["zi"], ["id32"], T.id32[:], ident, F.Copy)
+    aff(["zi"], ["n512"], T.n512[:], ident, -512.0, 0.0)
+    aff(["x16", "c8"], ["ctab"], T.ctab[:], T.x16[:, 0:16], -1.0, C(10))
+    aff(["x16"], ["xm16"], T.xm16[:], T.x16[:, 0:16], -16.0, 96.0)
+    for u in (1, 2):
+        act(["i16"], ["coef%dc" % u], T["coef%d" % u][:, 16:32], T.i16[:], F.Copy)
+    aff(["c01"], ["c11"], C(11), C(1), 1.0, PRES)
+    aff(["c2_"], ["c14"], C(14), C(2), 1.0, 15.0)
+    aff(["c2_"], ["c16_"], C(16), C(2), 1.0, 4.0)
+    aff(["c01"], ["c13"], C(13), C(1), 16384.0, 8192.0 * (1.5 - 15.5))
+    aff(["c2_"], ["oo0"], T.oo[:, 0:1], C(2), 32.0, 0.0)
+    aff(["c01"], ["c17"], C(17), C(0), -17.0, -float(L))
+    aff(["ps4", "c17"], ["c6"], C(6), T.ps4[:, 0:1], 1.0, C(17))
+
+    def gather_y0(k):
+        a, b = Y0CUT[k], Y0CUT[k + 1]
+        act(["ves", "vesz", "posv"], ["y0%d" % k], T.y0[:, 16 * a:16 * b], T.ves[:, 0:M + 1].indirect(T.posv[:, a:b]), F.Copy)
+
+    ts(["ps1"], ["gs"], T.gs[:, 0:96], T.ps1[:, 0:96], -256.0, A.add)
+    cp(["gs", "gsz", "offx0"], ["own0"], T.land0[:, 16 * rank:16 * rank + 16], T.gs[:, 0:97].indirect(T.offx[:, 0:1]))
 
     direct, relays = routes(T, topo, core)
     off_eng = topo.engines(core, direct[0])
-    on_eng = topo.engines(core, relays[0][0])
+    on_eng = [e for e in topo.engines(core, relays[0][0]) if e not in off_eng]
     per = len(on_eng) // 2
     sent = [0]
 
@@ -313,11 +364,11 @@ def rank_main(g, core, T, topo):
         deps("g", ["own%d" % t], [])
         g.remote_dma_fused([RemoteDMATransfer(dst_ids=[dst_id(topo, rl, core)], dma_engine_mask=bits(on_eng[k * per:(k + 1) * per]),
                                               remote_sem=T.sem["rl%d" % t], src=src, dst=T.hand[:, 32 * t:32 * t + w])
-                            for k, (rl, _) in enumerate(relays)], local_sem=T.sem.ls)
+                            for k, (rl, _) in enumerate(relays)], local_sem=T.sem["ls%d" % t])
         g.remote_dma_fused([RemoteDMATransfer(dst_ids=[dst_id(topo, d, core) for d in direct], dma_engine_mask=bits(off_eng),
                                               remote_sem=T.sem["ad%d" % t], srcs=[src], dsts=[src for d in direct])],
-                           local_sem=T.sem.ls)
-        sent[0] += 2 * per + len(off_eng)
+                           local_sem=T.sem["ls%d" % t])
+        sent[0] = 2 * per + len(off_eng)
 
     near = [T.rank_of(c) for c in direct]
     farr = [r for r in range(8) if r != rank and r not in near]
@@ -341,229 +392,243 @@ def rank_main(g, core, T, topo):
 
     def key_fix(u):
         mm(["sel", "dead%d" % u], ["ps2"], T.ps2[:, 0:16], T.sel[:], T["dead%d" % u][:], False, False)
-        mm(["sel", "cor%d" % u], ["ps2"], T.ps2[:, 0:16], T.sel[:], T["cor%d" % u][:], False, False)
+        mm(["sel", "cor%d" % u, "cor%db" % u], ["ps2"], T.ps2[:, 0:16], T.sel[:], T["cor%d" % u][:], False, False)
         mm(["lv%d" % u, "corv"], ["ps2"], T.ps2[:, 0:16], T["lv%d" % u][:], T.corv[:], False, False)
-
-    def key_open(t):
-        mm(["sel", "ptiea", "ptieb"], ["ps2"], T.ps2[:, 0:48], T.sel[:], T.ptie[:], True, False)
-        mm(["sel", "poff"], ["ps2"], T.ps2[:, 0:16], T.sel[:], T.poff[:], False, False)
-        for u in range(t):
-            if u > 0:
-                key_fix(u)
-            key_terms(u, list(range(8)), False)
 
     def key_close(t):
         if t > 0:
+            mm(["id32", "keep"], ["ps2"], T.ps2[:, 0:48], T.id32[:], T.keep[:], True, False)
             key_fix(t)
+        else:
+            mm(["sel", "ptiea", "ptieb"], ["ps2"], T.ps2[:, 0:48], T.sel[:], T.ptie[:], True, False)
+            mm(["sel", "poff"], ["ps2"], T.ps2[:, 0:16], T.sel[:], T.poff[:], False, False)
         key_terms(t, [rank], False)
         wait("p", ("ad%d" % t, n_ad))
         key_terms(t, near, False)
         wait("p", ("ar%d" % t, n_ar))
         key_terms(t, farr, True)
 
+    WADD = ["wadd%d" % k for k in range(8)]
     def winner(t):
         b = 8 * t
         scan(["ps2", "neg"], ["sc"], T.sc[:, 16:64], T.ps2[:, 0:48], T.neg[:], -1e9, A.max, A.max)
-        op("v", ["sc"], ["sct"], lambda: V.transpose(T.sct[:], T.sc[:, 32:64]))
-        op("v", ["sct"], ["w0%d" % t], lambda: V.tensor_reduce(W(b), T.sct[:], AxisListType.X, A.max))
-        ts(["w0%d" % t], ["w1%d" % t], W(b + 1), W(b), MAGIC, A.add, MAGIC, A.subtract)
+        if t < 2:
+            act(["ps2"], ["keep"], T.keep[:], T.ps2[:, 0:48], F.Copy)
+        op("v", ["sc"], ["sct"], lambda: V.transpose(T.sct[:, 0:32], T.sc[:, 32:64]))
+        scan(["sct", "sctz"] + WADD, ["w%d%d" % (k, t) for k in WCOL], T.wo[:, 40 * t:40 * t + 39], T.sct[:, 0:39],
+             T.wadd[:, 40 * t:40 * t + 39], -3e9, A.max, A.add)
 
     def record(t):
         b = 8 * t
-        act(["w4%d" % t, "w2%d" % t], ["w7%d" % t], W(b + 7), W(b + 4), F.Identity, bias=W(b + 2), scale=16.0)
-        act(["w1%d" % t], ["mg%db" % t], T.mgb[:, 3 * t + 2:3 * t + 3], W(b + 1), F.Identity, bias=CNT0, scale=1.0 / 256)
-        act(["w7%d" % t], ["w5%d" % t], W(b + 5), W(b + 7), F.Identity, bias=111.0, scale=-1.0)
-        act(["w4%d" % t, "w5%d" % t], ["mg%da" % t], T.mgb[:, 3 * t:3 * t + 2], T.win[:, b + 4:b + 6], F.Copy)
+        aff(["w6%d" % t], ["mg%da" % t], T.mgb[:, 3 * t:3 * t + 1], W(b + 6), 1.0, float(S0 + t))
+        aff(["w7%d" % t], ["mg%dc" % t], T.mgb[:, 3 * t + 1:3 * t + 2], W(b + 7), 1.0, float(S0 + t))
+        aff(["w1%d" % t], ["mg%db" % t], T.mgb[:, 3 * t + 2:3 * t + 3], W(b + 1), 1.0 / 256, CNT0)
 
-    def delta(t):
+    def delta_open():
+        mm(["zi", "km256"], ["ps1"], T.ps1[:, 0:24], ident, T.km256[:], True, False)
+
+    def delta(t, marks):
         b, u = 8 * t, t + 1
         cb, n = "cb%d" % t, S0 + t
-        ts([cb + "a", cb + "b", cb + "c", "w0%d" % t, "w1%d" % t], ["mrk"], T.mrk[:], T[cb][:, 3:435], W(b + 1), A.add, W(b), A.is_equal)
-        for m in range(18):
-            mm(OH + ["mrk"], ["ps1"], T.ps1[:, 0:24], T.oh[:, 128 * m:128 * m + 128], T.mrk[:, 24 * m:24 * m + 24], m == 0, m == 17)
-        tt(["w0%d" % t, "w1%d" % t], ["w2%d" % t], W(b + 2), W(b), W(b + 1), A.subtract)
-        ts(["w2%d" % t], ["w3%d" % t], W(b + 3), W(b + 2), -1.0 / 16, A.mult, 104.5 / 16, A.add)
-        ts(["w3%d" % t], ["w4%d" % t], W(b + 4), W(b + 3), ROUND, A.add, ROUND, A.subtract)
-        ts(["x16", "w4%d" % t], ["coef%da" % u], T["coef%d" % u][:, 0:n], T.x16[:, 0:n], W(b + 4), A.is_equal, -1.0, A.mult)
-        ts(["c01", "c7", "w4%d" % t], ["offx%d" % u], T.offx[:, 2 * u:2 * u + 1], C(1), W(b + 4), A.not_equal, C(7), A.add)
-        ts(["ps1"], ["gs"], T.gs[:, 0:24], T.ps1[:, 0:24], -256.0, A.add)
-        tt(["gs", "offx%d" % u, "offv", "coef%da" % u, "coef%db" % u], ["own%d" % u], T["land%d" % u][:, 32 * rank:32 * rank + 32],
+        w = ["w%d%d" % (k, t) for k in range(8)]
+        for lo, hi in ((0, 8), (8, 18)):
+            ts([cb + "a", cb + "b", cb + "c", w[0], w[1]], ["mrk%d" % lo], T.mrk[:, 24 * lo:24 * hi], T[cb][:, 3 + 24 * lo:3 + 24 * hi],
+               W(b + 1), A.add, W(b), A.is_equal)
+            for m in range(lo, hi):
+                mm(OH + ["mrk%d" % lo], ["ps1"], T.ps1[:, 0:24], T.oh[:, 8 * m:8 * m + 8, :], T.mrk[:, 24 * m:24 * m + 24],
+                   False, m == 17)
+        tt([w[0], w[1]], [w[2]], W(b + 2), W(b), W(b + 1), A.subtract)
+        ts([w[4], w[0]], [w[7]], W(b + 7), W(b + 4), W(b), A.subtract, 15.0 - n, A.add)
+        ts([w[5], w[1]], [w[6]], W(b + 6), W(b + 5), W(b + 1), A.subtract, -1.0 / 16, A.mult)
+        ts(["xm16", w[1], w[4]], ["coef%da" % u], T["coef%d" % u][:, 0:n], T.xm16[:, 0:n], W(b + 1), A.add, W(b + 4), A.is_equal)
+        marks()
+        tt(["ps1", "sgn"], ["gs"], T.gs[:, 0:24], T.ps1[:, 0:24], T.sgn[:], A.mult)
+        ts(["ctab", w[2]], ["dead%d" % u], T["dead%d" % u][:], T.ctab[:], W(b + 2), A.is_equal, -30000.0, A.mult)
+        tt(["gs", "offx%d" % u, "coef%da" % u, "coef%db" % u, "coef%dc" % u], ["own%d" % u], T["land%d" % u][:, 32 * rank:32 * rank + 32],
            T.gs[:, 0:24].indirect(T.offx[:, 2 * u:2 * u + 2]), T["coef%d" % u][:], A.mult)
         send(u)
-        record(t)
 
     def fixes(t):
         b, u, n = 8 * t, t + 1, S0 + t
-        ts(["c01", "w4%d" % t], ["w6%d" % t], W(b + 6), C(1), W(b + 4), A.is_equal, -30000.0, A.mult)
-        ts(["x16", "w5%d" % t], ["lv%d" % u], T["lv%d" % u][:], T.x16[:, 0:128], W(b + 5), A.is_equal, -256.0, A.mult)
-        ts(["coef%da" % u, "coef%db" % u], ["cor%d" % u], T["cor%d" % u][:], T["coef%d" % u][:, 0:16], 2048.0, A.mult)
-        ts(["x16", "w5%d" % t, "w6%d" % t], ["dead%d" % u], T["dead%d" % u][:], T.x16[:, 0:16], W(b + 5), A.is_equal, W(b + 6), A.mult)
-        ms(["lv%d" % u], T["lv%d" % u][:, n:128:16], 256.0)
-        key_open(u)
-        key_close(u)
+        ts(["x15", "w7%d" % t], ["lv%d" % u], T["lv%d" % u][:, :, 0:n], T.x15[:, :, 15 - n:15], W(b + 7), A.is_equal, -256.0, A.mult)
+        ts(["coef%da" % u], ["cor%d" % u], T["cor%d" % u][:, 0:n], T["coef%d" % u][:, 0:n], -2048.0, A.mult)
 
     send(0)
-    key_open(0)
-    key_close(0)
+    gather_y0(0)
+    ms(["sctz"], T.sct[:, 32:40], -3e9)
+    for k, (c, v) in enumerate(((33, MAGIC16), (34, -MAGIC16), (37, MAGIC), (38, -MAGIC))):
+        op("v", ["wadd0"], ["wadd%d" % (4 + k)], lambda: V.memset(T.wadd[:, c:120:40], v))
 
-    ts(["cur0"], ["ps3a"], P(0, -4, 149), S("cur0", -4, 149), -16.0, A.mult, 111.0, A.add)
-    ts(["c2_"], ["c7"], C(7), C(2), 3.0 / 16, A.mult)
+    BLK = [[-16, 8], [0, 16]]
+    select(["kone"], ["bt0"], T.bt0[:], T.kone[:, 0:128], BLK, A.is_ge, 0.0, 0, 1)
+    select(["bt0"], ["bones"], T.bones[:], T.bt0[:], [[16, 8], [0, 16]], A.is_ge, 0.0, 15, -1)
+    select(["bones"], ["bt0"], T.bt0[:], T.bones[:], [[1, 128]], A.is_gt, 0.0, 0, -1)
+    select(["bt0"], ["btri"], T.btri[:], T.bt0[:], [[1, 128]], A.not_equal, -0.5, 0, -1)
+    select(["bones"], ["bt0"], T.bt0[:], T.bones[:], [[-1, 128]], A.is_gt, 0.0, 0, 1)
+    select(["bt0"], ["bup"], T.bup[:], T.bt0[:], [[1, 128]], A.not_equal, 1.5, 0, -1)
+    select(["kone"], ["bs0"], T.bs0[:], T.kone[:, 0:128], BLK, A.is_equal, 0.0, 0, 1)
     tt(["ps3a", "cur0"], ["c0"], S("c0", -4, 149), P(0, -4, 149), S("cur0", -3, 150), A.subtract)
-    ts(["c7"], ["offv"], T.offx[:, 3:4], C(7), 2.0, A.add)
+    ts(["c7"], ["offx1", "offx2"], T.offx[:, 3:6:2], T.col[:, 7:9], 2.0, A.add)
     tt(["c0"], ["ps3b"], P(1, -1, 144), S("c0", 0, 145), S("c0", -2, 143), A.not_equal)
     cp(["c0"], ["cb0a"], T.cb0[:, 0:435:3], S("c0", 0, 145))
     tt(["ps3b", "c0"], ["cb0b"], T.cb0[:, 4:436:3], P(1, 0, 144), S("c0", 1, 145), A.mult)
     tt(["ps3b", "c0"], ["cb0c"], T.cb0[:, 5:437:3], P(1, -1, 143), S("c0", -2, 142), A.mult)
-    ts(["c7"], ["offv"], T.offx[:, 5:6], C(7), 2.0, A.add)
+    delta_open()
+    lin("ps6", 151, [("zi", "c0", -3)], True, False)
+    lin("ps0", 152, [("nzi", "cur0", -3)], True, False)
+    key_close(0)
     for u in (1, 2):
         n = S0 + u - 1
+        ts(["c01", "c7"], ["offx%d" % u], T.offx[:, 2 * u:2 * u + 1], C(1), float(n), A.is_equal, C(7), A.add)
+        ts(["x15"], ["lv%d" % u], T["lv%d" % u][:], T.x15[:], n - 15.0, A.is_equal, 256.0, A.mult)
         ts(["x16"], ["coef%db" % u], T["coef%d" % u][:, n:16], T.x16[:, n:16], float(n), A.is_equal)
-        cp(["i16"], ["coef%db" % u], T["coef%d" % u][:, 16:32], T.i16[:])
+        ts(["x16"], ["cor%db" % u], T["cor%d" % u][:, n:16], T.x16[:, n:16], float(n), A.is_equal, 2048.0, A.mult)
     ts(["i16"], ["corv"], T.corv[:], T.i16[:], 2048.0, A.mult)
-    ts(["xf", "c01"], ["zi"], T.zi[:], T.xf[:], -15.0, A.add, C(0), A.is_equal)
-    ms(["km93"], T.km93[:], -93.0)
-    ts(["zi"], ["i16x"], T.i16x[:], ident, 16.0, A.mult)
-    ts(["zi"], ["i93"], T.i93[:], ident, 93.0, A.mult)
-    ms(["k18"], T.k18[:], 18.0)
-    ts(["c01"], ["c11"], C(11), C(1), PRES, A.add)
-    ts(["c2_"], ["c14"], C(14), C(2), 15.0, A.add)
-    ts(["xg", "c2_"], ["bones"], T.bones[:], T.xg[:, 0:128], C(2), A.is_equal, 2.0, A.mult)
-    ts(["xf", "c14", "c11"], ["zw"], T.zw[:, 0:144], T.xf[:, 0:144], C(14), A.is_equal, C(11), A.mult)
-    ts(["xf", "c01"], ["bt0"], T.bt0[:], T.xf[:, 0:128], C(0), A.is_gt)
-    ts(["xg", "c01"], ["bs0"], T.bs0[:], T.xg[:, 0:128], C(0), A.is_equal)
-    tt(["bt0", "bones"], ["bt0"], T.bt0[:], T.bt0[:], T.bones[:], A.mult)
-    ts(["bones"], ["nbones"], T.nbones[:], T.bones[:], -1.0, A.mult)
-    tt(["bt0", "zi"], ["btri"], T.btri[:], T.bt0[:], ident, A.subtract)
-    ms(["kbig"], T.kbig[:], 8192.0)
-    ts(["btri"], ["nbtri"], T.nbtri[:], T.btri[:], -1.0, A.mult)
-    ms(["kone"], T.kone[:], 1.0)
-    ms(["crowa"], T.crow[:, 0:1], 0.0)
-    ms(["crowc"], T.crow[:, 145:147], L + PRES)
-    ms(["kt1"], T.kt[:, CH:CH + 1], 1.0)
-    ms(["lo0"], T.lo[:, 145:146], 0.0)
-    ts(["c01"], ["c13"], C(13), C(1), 16384.0, A.mult, 12288.0, A.add)
-    ts(["c16", "c2_"], ["jt"], T.jt[:, 0:16], T.c16[:, 0:16], C(2), A.subtract)
-    ts(["sm0", "c01"], ["offd"], T.offd[:], T.sm[:, 0:18], C(1), A.add)
-    ts(["jt"], ["smi"], T.smi[:, 0:9], T.jt[:, 0:9], 1.0 / 9, A.mult, -4.0 / 9, A.add)
     ts(["pi"], ["pg"], T.pi[:, 2:3], T.pi[:, 0:1], 16, A.bitwise_and)
-    ts(["jt"], ["thr"], T.thr[:, 0:9], T.jt[:, 0:9], 32.0, A.mult)
-    cp(["pg"], ["c12"], C(12), T.pi[:, 2:3])
-    ms(["y0z"], T.y0[:, L:L + 1], 0.0)
+    ts(["c16", "c16_"], ["smi"], T.smi[:, 0:9], T.c16[:, 0:9], C(16), A.subtract, 1.0 / 9, A.mult)
+    ts(["pg", "oo0"], ["c12"], C(12), T.pi[:, 2:3], T.oo[:, 0:1], A.subtract, -31.0, A.add)
+    ts(["xf", "c14", "c11"], ["zw"], T.zw[:, 0:144], T.xf[:, 0:144], C(14), A.is_equal, C(11), A.mult)
     ts(["smi", "c12"], ["sm1"], T.sm[:, 20:29], T.smi[:, 0:9], -287.0, A.mult, C(12), A.add)
-    ms(["ggr"], T.gg[:, 16 + L:32 + L], 15.0)
+    ts(["sm0", "c01"], ["offd"], T.offd[:], T.sm[:, 0:18], C(1), A.add)
     tt(["thr", "sm1"], ["sm1"], T.sm[:, 20:29], T.sm[:, 20:29], T.thr[:, 0:9], A.add)
-    ms(["oo0"], T.oo[:, 0:1], 0.0)
     cp(["sm1"], ["offt"], T.offt[:, 0:9], T.sm[:, 20:29])
-    ts(["jt"], ["thr"], T.thr[:, 0:9], T.jt[:, 0:9], 32.0, A.mult, 31.0, A.add)
 
     winner(0)
-    delta(0)
     tie0 = W(2)
-    ts(["c0", "w20"], ["h0"], S("h0", -4, 149), S("c0", -4, 149), tie0, A.is_equal)
-    lin("ps0", 152, [("zi", "cur0", -3), ("i16x", "h0", -3), ("i16x", "h0", -4)])
-    act(["ps0"], ["rc1"], S("rc1", -3, 149), T.ps0[:, 0:152], F.Relu, bias=12.0, scale=-1.0)
-    lin("ps6", 151, [("zi", "km93", -3), ("i93", "h0", -3), ("i16x", "rc1", -3), ("zi", "rc1", -2)])
-    act(["ps6"], ["cz"], S("cz", -3, 148), T.ps6[:, 0:151], F.Copy)
+
+    def marks0():
+        ts(["c0", "w20", "w70"], ["hb"], S("hb", -4, 149), S("c0", -4, 149), tie0, A.is_equal, W(7), A.mult)
+        ts(["c0", "w20", "w60"], ["ha"], S("ha", -4, 149), S("c0", -4, 149), tie0, A.is_equal, W(6), A.mult)
+
+    delta(0, marks0)
+    iota(["k35"], T.k35[:], [[0, 160]], 35, 0)
+    iota(["crowb"], T.crow[:, 0:145], [[16, 145]], -16, 0)
+    iota(["crowc"], T.crow[:, 145:147], [[0, 2]], L + int(PRES), 0)
+    iota(["kt1"], T.kt[:, CH:CH + 1], [[0, 1]], 2, 0)
+    iota(["lo0"], T.lo[:, 145:146], [[0, 1]], 0, 0)
+    ts(["c0", "w20"], ["ht"], S("ht", -4, 149), S("c0", -4, 149), tie0, A.is_equal, tie0, A.mult)
+    lin("ps0", 152, [("zi", "hb", -4), ("zi", "ha", -3)], False, True)
+    lin("ps6", 151, [("i16x", "hb", -4), ("zi", "ha", -2), ("nzi", "ht", -3)], False, True)
+    aff(["ps0"], ["rc1"], S("rc1", -3, 149), T.ps0[:, 0:152], 1.0, 12.0)
     oh_a("rc1", 144, [(10, 2), (11, 1), (12, 0)])
+    record(0)
+    ts(["c0", "w20"], ["h0"], S("h0", -4, 149), S("c0", -4, 149), tie0, A.is_equal)
     ts(["c0", "w20"], ["ps3b"], P(1, -4, 149), S("c0", -4, 149), tie0, A.not_equal)
     fixes(0)
-    oh_v("rc1", 144, 0, 12)
-    oh_v("rc1", 144, 1, 11)
-    tt(["ps6", "h0"], ["ne"], S("ne", -1, 147), T.ps6[:, 3:151], S("h0", -1, 147), A.mult)
-    scan(["h0", "cz"], ["cbk"], S("cbk", -2, 147), S("h0", -3, 146), S("cz", -3, 146), 0.0, A.mult, A.add)
-    tt(["ps6", "ne"], ["ca"], S("ca", -1, 147), T.ps6[:, 2:150], S("ne", -1, 147), A.add)
-    tt(["ps3b", "cbk"], ["ps3c"], P(2, -1, 144), P(1, -1, 144), S("cbk", -1, 144), A.mult)
-    tt(["ps3b", "ca"], ["cb1a"], T.cb1[:, 0:435:3], P(1, -1, 144), S("ca", 0, 145), A.mult)
-    oh_v("rc1", 144, 2, 10)
-    tt(["ps3c", "cb1a"], ["ne"], S("ne", -1, 144), P(2, -1, 144), T.cb1[:, 0:435:3], A.not_equal)
-    oh_v("rc1", 144, 3, 9)
-    tt(["ps3c", "ne"], ["cb1c"], T.cb1[:, 5:437:3], P(2, -1, 143), S("ne", -1, 143), A.mult)
-    tt(["cb1a", "ne"], ["cb1b"], T.cb1[:, 4:436:3], T.cb1[:, 3:435:3], S("ne", 0, 144), A.mult)
-    for s in range(4, 10):
-        oh_v("rc1", 144, s, 12 - s)
+    delta_open()
+    lin("ps5", 147, [("zi", "k35", -1), ("n512", "h0", -1), ("i16x", "rc1", -1), ("zi", "rc1", 0)], True, False)
+    lin("ps7", 147, [("zi", "h0", -1)], True, False)
+    lin("ps0", CH, [("zi", "rc1", 0)], True, False)
+    key_close(1)
+    steps = [
+        lambda: tt(["ps6", "h0"], ["ne"], S("ne", -1, 147), T.ps6[:, 3:151], S("h0", -1, 147), A.mult),
+        lambda: scan(["h0", "ps6"], ["cbk"], S("cbk", -2, 147), S("h0", -3, 146), T.ps6[:, 0:149], 0.0, A.mult, A.add),
+        lambda: tt(["ps6", "ne"], ["ca"], S("ca", -1, 147), T.ps6[:, 2:150], S("ne", -1, 147), A.add),
+        lambda: tt(["ps3b", "cbk"], ["ps3c"], P(2, -1, 144), P(1, -1, 144), S("cbk", -1, 144), A.mult),
+        lambda: tt(["ps3b", "ca"], ["cb1a"], T.cb1[:, 0:435:3], P(1, -1, 144), S("ca", 0, 145), A.mult),
+        lambda: tt(["ps3c", "cb1a"], ["ne"], S("ne", -1, 144), P(2, -1, 144), T.cb1[:, 0:435:3], A.not_equal),
+        lambda: tt(["ps3c", "ne"], ["cb1c"], T.cb1[:, 5:437:3], P(2, -1, 143), S("ne", -1, 143), A.mult),
+        lambda: tt(["cb1a", "ne"], ["cb1b"], T.cb1[:, 4:436:3], T.cb1[:, 3:435:3], S("ne", 0, 144), A.mult)]
+    hot = list(range(10))
+    for step, fill in zip(steps, (0, 1, 1, 2, 3, 3, 0, 0)):
+        step()
+        for _ in range(fill):
+            s = hot.pop(0)
+            oh_v("rc1", 144, s, 12 - s)
 
     winner(1)
-    delta(1)
     tie1 = W(10)
-    ts(["ca", "w21"], ["ma"], S("ma", -1, 147), S("ca", -1, 147), tie1, A.is_equal, -16.0, A.mult)
-    ts(["cbk", "w21"], ["mb"], S("mb", -1, 147), S("cbk", -1, 147), tie1, A.is_equal, -16.0, A.mult)
-    ts(["cz", "w21"], ["h1"], S("h1", -1, 146), S("cz", -1, 146), tie1, A.is_equal)
-    lin("ps0", 148, [("zi", "rc1", -1), ("zi", "ma", -1), ("zi", "mb", -1)])
-    act(["ps0"], ["rc2"], S("rc2", -1, 147), T.ps0[:, 0:148], F.Relu, bias=1.0)
-    lin("ps7", 147, [("zi", "h0", -1), ("zi", "h1", -1)])
-    lin("ps6", 147, [("zi", "k18", -1), ("i16x", "rc2", -1), ("zi", "rc2", 0)])
+
+    def marks1():
+        ts(["cbk", "w21", "w71"], ["mb"], S("mb", -1, 147), S("cbk", -1, 147), tie1, A.is_equal, W(15), A.mult)
+        ts(["ca", "w21", "w61"], ["ma"], S("ma", -1, 147), S("ca", -1, 147), tie1, A.is_equal, W(14), A.mult)
+
+    delta(1, marks1)
+    iota(["kbig"], T.kbig[:], [[0, 160]], 16384, 0)
+    iota(["y0z"], T.y0[:, L:L + 1], [[0, 1]], 0, 0)
+    iota(["ggr"], T.gg[:, 16 + L:32 + L], [[0, 16]], 15, 0)
+    ts(["ps6", "w21"], ["h1"], S("h1", -1, 146), T.ps6[:, 2:149], tie1, A.is_equal)
+    lin("ps5", 147, [("i16x", "mb", -1), ("zi", "ma", 0), ("n512", "h1", -1)], False, True)
+    lin("ps7", 147, [("zi", "h1", -1)], False, True)
+    lin("ps0", CH, [("zi", "ma", 0), ("zi", "mb", 0)], False, False)
+    record(1)
+    aff(["bones"], ["nbones"], T.nbones[:], T.bones[:], -2.0, 0.0)
+    aff(["btri"], ["nbtri"], T.nbtri[:], T.btri[:], -2.0, 0.0)
+    aff(["bup"], ["nbup"], T.nbup[:], T.bup[:], -2.0, 0.0)
+    gather_y0(1)
     fixes(1)
-    ts(["ps7"], ["tmpb"], S("tmpb", -1, 146), T.ps7[:, 0:147], 0.5, A.is_lt)
-    tt(["ps6", "tmpb"], ["cz2"], T.cz2[:, 16:163], T.ps6[:, 0:147], S("tmpb", -1, 146), A.mult)
+    key_close(2)
+    ts(["ps5"], ["cz2"], T.cz2[:, 16:163], T.ps5[:, 0:147], 0.0, A.max)
     cp(["cz2", "offd"], ["xd"], T.xd[:], T.cz2[:, 16:16 + CH].indirect(T.offd[:, 0:18]))
     tt(["ps7", "cz2"], ["ps3a"], P(0, 0, 145), T.cz2[:, 18:163], T.ps7[:, 1:146], A.mult)
     op("v", ["xd"], ["xt"], lambda: V.transpose(T.xt[:], T.xd[:]))
     tt(["ps3a", "cz2"], ["s1"], S("s1", 0, 145), P(0, 0, 145), T.cz2[:, 17:162], A.add)
     ts(["xt", "offt"], ["et"], T.et[:, 0:CH], T.xt[:, 0:288].indirect(T.offt[:, 0:9]), -128.0, A.add)
     tt(["ps7", "s1"], ["ps3b"], P(1, 0, 144), S("s1", 1, 145), T.ps7[:, 1:145], A.mult)
-    ts(["et"], ["kt"], T.kt[:, 0:CH], T.et[:, 0:CH], -127.5, A.is_gt)
+    ts(["et"], ["kt"], T.kt[:, 0:CH], T.et[:, 0:CH], -127.5, A.is_gt, 2.0, A.mult)
     tt(["ps3b", "cz2"], ["ca2"], S("ca2", 0, 144), P(1, 0, 144), T.cz2[:, 17:161], A.add)
     mm(["bones", "kt", "kt1"], ["ps4"], T.ps4[:, 0:145], T.bones[:], T.kt[:, 0:145], True, False)
-    mm(["zi", "kone"], ["ps5"], T.ps5[:, 0:145], ident, T.kone[:, 0:145], True, False)
-    mm(["btri", "kt", "kt1"], ["ps5"], T.ps5[:, 0:145], T.btri[:], T.kt[:, 0:145], False, False)
-    mm(["zi", "crowa", "crowb", "crowc"], ["ps6"], T.ps6[:, 0:147], ident, T.crow[:, 0:147], True, False)
+    mm(["btri", "kt", "kt1"], ["ps5"], T.ps5[:, 0:145], T.btri[:], T.kt[:, 0:145], True, False)
+    mm(["bup", "kt"], ["ps5"], T.ps5[:, 1:145], T.bup[:], T.kt[:, 0:CH], False, False)
+    mm(["zi", "crowb", "crowc"], ["ps6"], T.ps6[:, 0:147], ident, T.crow[:, 0:147], True, False)
 
     winner(2)
     ts(["et", "w02", "w12"], ["nd"], T.nd[:, 0:CH], T.et[:, 0:CH], W(17), A.add, W(16), A.is_equal)
+    mm(["nbtri", "nd"], ["ps5"], T.ps5[:, 0:CH], T.nbtri[:], T.nd[:, 0:CH], False, False)
+    mm(["nbup", "nd"], ["ps5"], T.ps5[:, 1:145], T.nbup[:], T.nd[:, 0:CH], False, True)
     mm(["nbones", "nd"], ["ps4"], T.ps4[:, 0:CH], T.nbones[:], T.nd[:, 0:CH], False, True)
-    mm(["nbtri", "nd"], ["ps5"], T.ps5[:, 0:CH], T.nbtri[:], T.nd[:, 0:CH], False, True)
     ts(["w02", "w12"], ["w62"], W(22), W(16), W(17), A.subtract, 128.0, A.add)
     ts(["ca2", "w62"], ["m14"], S("m14", 0, 144), S("ca2", 0, 144), W(22), A.is_equal, -16.0, A.mult)
-    lin("ps0", CH, [("zi", "rc2", 0), ("zi", "m14", 0)])
-    scan(["ps4", "kbig"], ["oo"], T.oo[:, 1:146], T.ps4[:, 0:145], T.kbig[:, 0:145], 0.0, A.add, A.min)
+    lin("ps0", CH, [("zi", "m14", 0)], False, True)
+    scan(["ps5", "kbig"], ["idx"], T.idx[:, 0:145], T.ps5[:, 0:145], T.kbig[:, 0:145], -14.5, A.add, A.min)
+    scan(["ps4", "kbig", "oo0"], ["oo"], T.oo[:, 1:146], T.ps4[:, 0:145], T.kbig[:, 0:145], T.oo[:, 0:1], A.add, A.min)
 
     def count(u):
         c0 = 0 if u < UA else 16 * UA
         act(["oo", "oo0", "thr"], ["eh%d" % u], T.junk[:, 146 * u + c0:146 * u + 146], T.oo[:, c0:146], F.Sign,
             bias=T.thr[:, u:u + 1], scale=-1.0, accum_out=T.eh[:, u:u + 1])
 
-    act(["ps0"], ["xs"], T.xs[:, 0:CH], T.ps0[:, 0:CH], F.Relu, bias=1.0)
+    act(["ps0"], ["xs"], T.xs[:, 0:CH], T.ps0[:, 0:CH], F.Relu, bias=2.0)
     dma("s", ["xs"], ["gg%d" % a for a, _ in VCUT + ACUT], T.gg[0:128:16, 16:16 + L], T.xs[:, 0:CH], "dsy")
-    tt(["ps5", "oo", "oo0"], ["idx"], T.idx[:], T.ps5[:, 0:145], T.oo[:, 0:145], A.add)
-    ts(["idx"], ["zz"], T.zz[:], T.idx[:], 31, A.bitwise_and)
-    cp(["zz"], ["zb"], T.zb[:, 0:145], T.zz[:])
+    ts(["idx"], ["ps3a"], T.ps3[:, 0:145], T.idx[:, 0:145], MAGIC32, A.add, MAGIC32, A.subtract)
+    tt(["idx", "ps3a"], ["zb"], T.zb[:, 0:145], T.idx[:, 0:145], T.ps3[:, 0:145], A.subtract)
     mm(["bs0", "zb"], ["ps7"], T.ps7[:, 0:145], T.bs0[:], T.zb[:, 0:145], True, True)
     for u in range(9):
         count(u)
         if u == UA - 1:
             act(["ps7", "c13"], ["ml"], T.ml[:, 0:145], T.ps7[:, 0:145], F.Identity, bias=C(13), scale=-8192.0)
     for r in range(16):
-        ts(["zb"], ["ohz%d" % r], T.ohz[:, CH * r:CH * r + CH], T.zb[:, 0:CH], 2.0 * r, A.is_equal)
+        ts(["zb"], ["ohz%d" % r], T.ohz[:, CH * r:CH * r + CH], T.zb[:, 0:CH], 2.0 * r - 15.5, A.is_equal)
         mm(["zw", "ohz%d" % r], ["ps6"], T.ps6[:, 1:145], T.zw[:, 15 - r:143 - r], T.ohz[:, CH * r:CH * r + CH], False, r == 15)
     ts(["eh%d" % u for u in range(UA)], ["ehua"], T.ehu[:, 0:UA], T.eh[:, 0:UA], 0.5, A.mult, 72.0, A.add)
-    ts(["w62"], ["w32"], W(19), W(22), -1.0 / 16, A.mult, 232.5 / 16, A.add)
+    ts(["w52", "w12"], ["mg2a"], T.mgb[:, 6:7], W(21), W(17), A.subtract, -1.0 / 16, A.mult)
     tt(["ps6", "ml"], ["lo"], T.lo[:, 0:145], T.ps6[:, 1:146], T.ml[:, 0:145], A.min)
-    ts(["w32"], ["mg2a"], T.mgb[:, 6:7], W(19), ROUND, A.add, ROUND, A.subtract)
+    ts(["w42", "w02"], ["mg2c"], T.mgb[:, 7:8], W(20), W(16), A.subtract, 15.0, A.add)
     scan(["ps6", "lo", "lo0"], ["xm"], T.xm[:, 0:146], T.ps6[:, 0:146], T.lo[:, 0:146], 0.0, A.max, A.max)
-    ts(["mg2a"], ["w72"], W(23), T.mgb[:, 6:7], -16.0, A.mult, 239.0, A.add)
+    ts(["w12"], ["mg2b"], T.mgb[:, 8:9], W(17), 1.0 / 256, A.mult, CNT0, A.add)
+    dma("s", ["mg%d%s" % (t, s) for t in range(3) for s in "abc"], [], T.mg[:], T.mgb[0:1, 0:9])
     ts(["xm", "ehua"], ["tua"], T.tu[:, 0:16 * UA], T.xm[:, 0:146].indirect(T.ehu[:, 0:UA]), -PRES, A.add)
     ts(["eh%d" % u for u in range(UA, 9)], ["ehub"], T.ehu[:, UA:9], T.eh[:, UA:9], 0.5, A.mult, 72.0 + 8 * UA, A.add)
 
-    for a, b in zip(YCUT, YCUT[1:]):
-        tu = "tua" if a == 0 else "tub"
-        cp(["y0", "y0z", tu], ["yo%d" % a], T.yo[:, 16 * a:16 * b], T.y0[:, 0:L + 1].indirect(T.tu[:, a:b]))
-        dma("s", ["yo%d" % a], [], T.y[:, 16 * a:16 * b], T.yo[:, 16 * a:16 * b])
-        if a == 0:
-            ts(["xm", "ehub"], ["tub"], T.tu[:, 16 * UA:CH], T.xm[:, 0:146].indirect(T.ehu[:, UA:9]), -PRES, A.add)
     act(["oo", "c6"], ["flv"], C(15), T.oo[:, 144:145], F.Identity, bias=C(6), scale=0.5)
-    dma("a", ["flv"], [], T.fl[:], T.col[0:128:16, 15:16])
-    for a, b in zip(FCUT, FCUT[1:]):
-        tu = "tua" if a == 0 else "tub"
-        act(["gg0", "ggr", tu], ["fso%d" % a], T.fso[:, 16 * a:16 * b], T.gg[:, 16:17 + L].indirect(T.tu[:, a:b]), F.Identity,
-            bias=14.0, scale=-1.0)
-        dma("a", ["fso%d" % a], [], T.fs[:, 16 * a:16 * b], T.fso[0:128:16, 16 * a:16 * b])
-    ts(["w72", "w62"], ["mg2c"], T.mgb[:, 7:8], W(23), W(22), A.subtract)
-    ts(["w12"], ["mg2b"], T.mgb[:, 8:9], W(17), 1.0 / 256, A.mult, CNT0, A.add)
-    dma("s", ["mg%d%s" % (t, s) for t in range(3) for s in "ab"] + ["mg2c"], [], T.mg[:], T.mgb[0:1, 0:9])
+    dma("s", ["flv"], [], T.fl[:], T.col[0:128:16, 15:16])
+    pieces = [(b, "y", a) for a, b in zip(YCUT, YCUT[1:])] + [(b, "fs", a) for a, b in zip(FCUT, FCUT[1:])]
+    for b, kind, a in sorted(pieces):
+        tu = "tua" if a < 16 * UA else "tub"
+        if kind == "y":
+            cp(["y00", "y01", "y0z", tu], ["yo%d" % a], T.yo[:, 16 * a:16 * b], T.y0[:, 0:L + 1].indirect(T.tu[:, a:b]))
+            dma("s", ["yo%d" % a], [], T.y[:, 16 * a:16 * b], T.yo[:, 16 * a:16 * b])
+            if a == 0:
+                ts(["xm", "ehub"], ["tub"], T.tu[:, 16 * UA:CH], T.xm[:, 0:146].indirect(T.ehu[:, UA:9]), -PRES, A.add)
+        else:
+            act(["gg0", "ggr", tu], ["fso%d" % a], T.fso[:, 16 * a:16 * b], T.gg[:, 16:17 + L].indirect(T.tu[:, a:b]), F.Identity,
+                bias=14.0, scale=-1.0)
+            dma("s", ["fso%d" % a], [], T.fs[:, 16 * a:16 * b], T.fso[0:128:16, 16 * a:16 * b])
 
     for q in ("v", "a", "p", "g"):
         g.wait_ge(T.sem[SEM[q]], cnt[q])
     for s in ("dpos", "dst", "dle", "dve", "dsw", "dsy"):
         g.wait_ge(T.sem[s], 16)
-    g.wait_ge(T.sem.ls, sent[0])
+    for t in range(3):
+        g.wait_ge(T.sem["ls%d" % t], sent[0])
     g.wait_ge(T.sem.dout, outs[0])

@@ -9,17 +9,18 @@ SW = M // 16
 HL, HR = 4, 6
 MAGIC = 3221225472.0
 MAGIC16 = 201326592.0
-MAGIC32 = 402653184.0
 WCOL = {0: 31, 4: 34, 5: 35, 1: 38}
 CNT0 = 28672.0
+BACK = 256.0 * 64 * 256
+NEW = BACK - 256 * CNT0
 PRES = 128.0
-FA = 800
+FA = 480
 VCUT = [(44, 72), (18, 44), (8, 18), (0, 8)]
 ACUT = [(72, 100), (100, 128), (128, 136), (136, 144)]
-YCUT, FCUT = [0, 32, 64, 92, 116, 134, 144], [0, 64, 112, 144]
+YCUT, FCUT = [0, 32, 64, 94, 120, 138, 144], [0, 64, 116, 144]
 Y0CUT = [0, 88, 144]
 UA = 4
-PAY = (16, 32, 32)
+PAY = (16, 24, 24)
 
 
 def _sb(n, d):
@@ -30,35 +31,37 @@ SCRATCH = {}
 for _n in ("cur0", "rc1", "c0", "ca", "cbk", "ne", "h0", "h1", "ha", "hb", "ht", "ma", "mb", "s1", "kone", "kbig", "crow",
            "ca2", "et", "kt", "nd", "m14", "xs", "zb", "z1", "zw", "zi", "k35", "vm", "sq0", "sq1", "sq2"):
     SCRATCH[_n] = _sb(160, "bfloat16")
-for _n in ("xf", "x16", "c16", "oo", "lo", "ml", "xm", "gs", "idx", "jc"):
+for _n in ("xf", "x16", "c16", "oo", "lo", "ml", "xm", "gs", "jc"):
     SCRATCH[_n] = _sb(160, "float32")
 for _n in ("posi", "ri"):
     SCRATCH[_n] = _sb(CH, "int32")
 for _n in ("posu", "posv", "tu"):
     SCRATCH[_n] = _sb(CH, "uint16")
-for _n in ("bones", "btri", "nbones", "nbtri", "bt0", "bs0", "bup", "nbup", "i16x", "nzi", "n512"):
+for _n in ("bones", "btri", "nbones", "nbtri", "bs0", "bup", "nbup", "i16x", "nzi", "n512", "pbig"):
     SCRATCH[_n] = _sb(128, "bfloat16")
 SCRATCH.update({
-    "sti": _sb(SW, "int32"), "stb": _sb(SW, "bfloat16"), "stw": _sb(M + 16, "bfloat16"),
+    "sti": _sb(SW, "int32"), "stb": _sb(SW, "bfloat16"), "stw": _sb(M, "bfloat16"),
     "lei": _sb(4, "int32"), "pi": _sb(8, "int32"), "col": _sb(64, "float32"),
     "win": _sb(64, "float32"), "i16": _sb(16, "bfloat16"),
     "gg": _sb(L + 32, "bfloat16"), "oh": ("sbuf", [128, 146, 16], "bfloat16"), "cz2": _sb(176, "bfloat16"),
     "ves": _sb(M + 16, "bfloat16"), "y0": _sb(L + 16, "bfloat16"), "yo": _sb(L, "bfloat16"), "fso": _sb(L, "float32"),
-    "cb0": _sb(448, "bfloat16"), "cb1": _sb(448, "bfloat16"), "mrk": _sb(432, "bfloat16"),
-    "ohz": _sb(16 * CH, "bfloat16"), "junk": _sb(9 * 146, "bfloat16"), "xd": _sb(288, "bfloat16"), "xt": _sb(288, "bfloat16"),
-    "bsel": _sb(128, "float32"), "km256": _sb(24, "bfloat16"), "sgn": _sb(24, "bfloat16"),
-    "id32": _sb(128, "float32"), "keep": _sb(48, "float32"), "ctab": _sb(16, "float32"), "xm16": _sb(16, "float32"),
-    "sel": _sb(128, "float16"),
-    "ptie": _sb(48, "float16"), "poff": _sb(16, "float16"), "cor1": _sb(16, "float16"), "cor2": _sb(16, "float16"),
-    "corv": _sb(16, "float16"), "dead1": _sb(16, "float16"), "dead2": _sb(16, "float16"),
-    "coef1": _sb(32, "float32"), "coef2": _sb(32, "float32"), "neg": _sb(48, "float32"),
+    "cb0": ("sbuf", [128, 3, 146], "bfloat16"), "cb1": ("sbuf", [128, 3, 146], "bfloat16"),
+    "mrk": ("sbuf", [128, 3, CH], "bfloat16"),
+    "ohz": _sb(16 * CH, "bfloat16"), "junk": _sb(9 * 146, "bfloat16"), "xd": ("sbuf", [128, 9, 32], "bfloat16"), "xt": _sb(288, "bfloat16"),
+    "idx": _sb(160, "float16"), "bsel": _sb(128, "float32"), "km256": _sb(24, "bfloat16"), "rst": _sb(24, "float32"),
+    "id32": _sb(128, "float32"), "id0": _sb(128, "float32"), "ctab": _sb(16, "float32"),
+    "kb1": _sb(96, "float32"), "kb2": _sb(96, "float32"), "ext": _sb(16, "float32"), "mrg": _sb(32, "float32"),
+    "sel": _sb(128, "float16"), "ptie": _sb(52, "float16"), "poff": _sb(16, "float16"), "c2048": _sb(8, "float16"),
+    "dead1": _sb(16, "bfloat16"), "dead2": _sb(16, "bfloat16"), "killa1": _sb(16, "bfloat16"), "killa2": _sb(16, "bfloat16"),
+    "killb": _sb(32, "bfloat16"), "neg": _sb(52, "float32"),
+    "selpm": ("sbuf", [128, 4, 32], "float16"), "route": ("sbuf", [128, 4, 32], "float16"),
+    "lv32": ("sbuf", [128, 8, 16], "float32"),
     "sc": _sb(64, "float32"), "sct": _sb(40, "float32"), "wo": _sb(120, "float32"), "wadd": _sb(120, "float32"),
     "x15": ("sbuf", [128, 8, 16], "bfloat16"),
-    "lv1": ("sbuf", [128, 8, 16], "float16"), "lv2": ("sbuf", [128, 8, 16], "float16"),
     "thr": _sb(16, "float32"), "eh": _sb(16, "float32"),
     "sm": _sb(32, "float32"), "smi": _sb(16, "int32"), "mgb": _sb(16, "float32"),
-    "offx": _sb(8, "uint16"), "offd": _sb(18, "uint16"), "offt": _sb(10, "uint16"), "ehu": _sb(10, "uint16"),
-    "land0": _sb(8 * 16, "float16"), "land1": _sb(8 * 32, "float16"), "land2": _sb(8 * 32, "float16"),
+    "offx": _sb(8, "uint16"), "offt": _sb(10, "uint16"), "ehu": _sb(10, "uint16"),
+    "land0": _sb(8 * 16, "float16"), "land1": _sb(8 * 24, "float16"), "land2": _sb(8 * 24, "float16"),
     "hand": _sb(3 * 32, "float16"),
 })
 for _k in range(8):
@@ -233,58 +236,63 @@ def rank_main(g, core, T, topo):
 
     ident = T.zi[:, 15:143]
 
+    dma("s", [], ["sti"], T.sti[:], T.st[:], "dst")
     dma("s", [], ["posi"], T.posi[:], T.pos[:], "dpos")
-    dma("a", [], ["sti"], T.sti[:], T.st[:], "dst")
     dma("s", [], ["lei"], T.lei[0:8, 0:1], T.le[:], "dle")
 
     iota(["bsel"], T.bsel[0:8, :], [[1, 8], [0, 16]], 0, -1)
-    iota(["c3"], T.col[0:8, 21:22], [[0, 1]], 0, 16)
-    iota(["c3"], T.col[0:8, 22:23], [[0, 1]], 0, L)
+    iota(["c30"], T.col[0:8, 21:22], [[0, 1]], 0, 16)
+    iota(["c31"], T.col[0:8, 22:23], [[0, 1]], 0, L)
     op("g", [], ["pi"], lambda: g.iota(T.pi[:, 0:1], [[0, 1]], 0, 1))
     iota(["xf"], T.xf[:], [[1, 160]], 0, 0)
-    iota(["kone"], T.kone[:], [[0, 160]], 1, 0)
     iota(["jc"], T.jc[:, 0:154], [[1, 154]], -HL, CH)
+    iota(["kone"], T.kone[:], [[0, 160]], 1, 0)
     select(["kone"], ["zi"], T.zi[:], T.kone[:], [[1, 160]], A.is_equal, 0.0, -15, -1)
     iota(["c16"], T.c16[:, 0:CH], [[16, CH]], 0, 1)
     iota(["x16"], T.x16[:, 0:128], [[0, 8], [1, 16]], 0, 0)
     iota(["km256"], T.km256[:], [[0, 24]], -256, 0)
-    select(["kone"], ["sgn"], T.sgn[:], T.kone[:, 0:24], [[0, 8], [1, 3]], A.is_gt, -1.0, 0, 0)
     iota(["x15"], T.x15[:], [[0, 8], [1, 16]], -15, 0)
+    select(["km256"], ["km256"], T.km256[:], T.km256[:], [[0, 3], [-16, 8]], A.is_ge, -20000.0, 0, 1)
     iota(["wadd0"], T.wadd[:], [[0, 120]], 0, 0)
-    for k, (lo, hi, step, base) in enumerate(((32, 120, 0, -8), (35, 80, 16, 96), (36, 80, -16, -96), (115, 116, 0, -96), (116, 117, 0, 96))):
-        op("g", ["wadd0"], ["wadd%d" % min(1 + k, 3)], lambda: g.iota(T.wadd[:, lo:hi:40], [[step, len(range(lo, hi, 40))]], base, 0,
-                                                                      allow_small_or_imprecise_dtypes=True))
-    iota(["sm0"], T.sm[:, 0:18], [[16, 9], [0, 2]], 0, 0)
+    select(["km256"], ["km256"], T.km256[:], T.km256[:], [[0, 3], [16, 8]], A.is_ge, -20000.0, 15, -1)
+    select(["wadd0"], ["rst"], T.rst[:], T.wadd[:, 0:24], [[0, 3], [1, 8]], A.is_gt, -30000.0, 0, 0)
     iota(["thr"], T.thr[:, 0:9], [[512, 9]], 31, 32)
+    WADD = ["wadd%d" % k for k in range(10)]
+    for k, (lo, hi, step, base) in enumerate(((32, 120, 0, -8), (35, 80, 16, 96), (36, 80, -16, -96), (115, 116, 0, -96), (116, 117, 0, 96))):
+        op("g", ["wadd0"], [WADD[k + 1]], lambda: g.iota(T.wadd[:, lo:hi:40], [[step, len(range(lo, hi, 40))]], base, 0,
+                                                         allow_small_or_imprecise_dtypes=True))
+    for u in (1, 2):
+        iota(["kb%dc3" % u], T["kb%d" % u][:, 19:52], [[0, 33]], -16000000, 0)
+        iota(["kb%dc4" % u], T["kb%d" % u][:, 52:64], [[0, 12]], 0, 0)
 
     ms(["stw0"], T.stw[:, 0:FA], -1.0)
-    act(["stw0"], ["stw2"], T.stw[:, M + 16 - FA:M + 16], T.stw[:, 0:FA], F.Copy)
-    ms(["stw1"], T.stw[:, FA:M + 16 - FA], -1.0)
+    act(["stw0"], ["stw2"], T.stw[:, FA:2 * FA], T.stw[:, 0:FA], F.Copy)
+    act(["stw0"], ["stw3"], T.stw[:, 2 * FA:3 * FA], T.stw[:, 0:FA], F.Copy)
+    ms(["stw1"], T.stw[:, 3 * FA:M], -1.0)
     cp(["sti"], ["stb"], T.stb[:], T.sti[:])
-    dma("s", ["stb"], ["stw0", "stw1", "stw2"], T.stw[0:128:16, 0:M], T.stb[:], "dsw")
+    dma("s", ["stb"], ["stw0", "stw1", "stw2", "stw3"], T.stw[0:128:16, 0:M], T.stb[:], "dsw")
     dma("s", [], ["ves"], T.ves[:, 0:M], T.ve[:], "dve")
     ts(["bsel"], ["bsel"], T.bsel[0:8, :], T.bsel[0:8, :], 0.0, A.is_equal)
     ts(["pi"], ["pm"], T.pi[:, 1:2], T.pi[:, 0:1], 15, A.bitwise_and)
-    cp(["lei"], ["lef0"], T.col[0:8, 20:21], T.lei[0:8, 0:1])
-    cp(["posi"], ["posu"], T.posu[:], T.posi[:])
+    for k in range(2):
+        ts(["lei", "c3%d" % k], ["lef%d" % k], T.col[0:8, 5 + k:6 + k], T.lei[0:8, 0:1], T.col[0:8, 21 + k:22 + k], A.add)
+    mm(["bsel", "lef0", "lef1"], ["ps4"], T.ps4[:, 0:2], T.bsel[0:8, :], T.col[0:8, 5:7], True, True)
     cp(["pi", "pm"], ["c01"], T.col[:, 0:2], T.pi[:, 0:2])
-    ts(["lef0", "c3"], ["lef"], T.col[0:8, 5:7], T.col[0:8, 21:23], T.col[0:8, 20:21], A.add)
-    mm(["bsel", "lef"], ["ps4"], T.ps4[:, 0:2], T.bsel[0:8, :], T.col[0:8, 5:7], True, True)
+    cp(["posi"], ["posu"], T.posu[:], T.posi[:])
     ms(["ggl"], T.gg[:, 0:16], -1.0)
-    ms(["ggr"], T.gg[:, 16 + L:32 + L], -1.0)
     ts(["c01"], ["c4"], C(4), C(1), 0.0, A.is_equal)
     ts(["c01"], ["c9"], C(9), C(0), 15.0, A.add)
-    ts(["jc", "ps4"], ["vm"], T.vm[:, 0:154], T.jc[:, 0:154], T.ps4[:, 1:2], A.is_ge, -100.0, A.mult)
+    ms(["ggr"], T.gg[:, 16 + L:32 + L], -1.0)
     ts(["xf", "c9", "c4"], ["z1"], T.z1[:, 0:144], T.xf[:, 0:144], C(9), A.is_equal, C(4), A.mult)
-    mm(["zi", "vm"], ["ps0"], T.ps0[:, 0:154], ident, T.vm[:, 0:154], True, False)
-    for s in range(12, 16):
+    ts(["jc", "ps4"], ["vm"], T.vm[:, 0:154], T.jc[:, 0:154], T.ps4[:, 1:2], A.is_ge, -100.0, A.mult)
+    for s in range(S0, 16):
         act(["xf"], ["oh%d" % s], T.oh[:, :, s], T.xf[:, 0:146], F.Copy, scale=0.0)
 
-    STW = ["stw0", "stw1", "stw2", "posu"]
+    STW = ["stw0", "posu"]
     have, todo = [], list(range(16))
     for (a, b), (c, d) in zip(VCUT, ACUT):
-        cp(STW, ["gg%d" % a], T.gg[:, 16 + 16 * a:16 + 16 * b], T.stw[:, 0:M + 1].indirect(T.posu[:, a:b]))
-        act(STW, ["gg%d" % c], T.gg[:, 16 + 16 * c:16 + 16 * d], T.stw[:, 0:M + 1].indirect(T.posu[:, c:d]), F.Copy)
+        cp(STW, ["gg%d" % a], T.gg[:, 16 + 16 * a:16 + 16 * b], T.stw[:].indirect(T.posu[:, a:b]))
+        act(STW, ["gg%d" % c], T.gg[:, 16 + 16 * c:16 + 16 * d], T.stw[:].indirect(T.posu[:, c:d]), F.Copy)
         have += [(a, b), (c, d)]
         for i in list(todo):
             need = range(max(9 * i - 1, 0), min(9 * i + 10, CH))
@@ -292,11 +300,18 @@ def rank_main(g, core, T, topo):
                 todo.remove(i)
                 mm(["z1", "ggl", "ggr"] + ["gg%d" % x for x, z in have if x < need[-1] + 1 and z > need[0]], ["ps0"],
                    T.ps0[:, 0:154], T.z1[:, 15 - i:143 - i], T.gg[:, 16 + CH * i - HL:16 + CH * i + CH + HR],
-                   False, len(todo) == 0)
+                   len(todo) == 15, len(todo) == 0)
+        if len(have) == 4:
+            mm(["zi", "vm"], ["ps0"], T.ps0[:, 0:154], ident, T.vm[:, 0:154], False, False)
     ms(["vesz"], T.ves[:, M:M + 16], 0.0)
+    aff(["c01"], ["c2_"], C(2), C(1), -1.0, C(0))
+    act(["c01"], ["c18"], C(18), C(1), F.Relu, bias=-96.0 * (S0 - 1), scale=96.0)
+    act(["xf"], ["gsz"], T.gs[:, 96:97], T.xf[:, 0:1], F.Identity, bias=-256.0)
+    aff(["c2_", "c18"], ["c19"], C(19), C(2), 0.75, C(18))
     ts(["c16", "ps4"], ["ps3a"], T.ps3[:, 0:CH], T.c16[:, 0:CH], T.ps4[:, 0:1], A.is_ge, float(M), A.mult)
     ts(["ps0"], ["cur0"], T.cur0[:, 0:154], T.ps0[:, 0:154], -1.0, A.max)
-    tt(["ps3a", "posi"], ["ri"], T.ri[:], T.ps3[:, 0:CH], T.posi[:], A.max)
+    for s in range(2):
+        ts(["ps0"], ["oh%d" % s], T.oh[:, 0:145, s], T.ps0[:, HL:HL + 145], float(s), A.is_equal)
 
     def oh_v(cur, n, s, val):
         ts([cur], ["oh%d" % s], T.oh[:, 0:n, s], S(cur, 0, n), float(val), A.is_equal)
@@ -308,35 +323,29 @@ def rank_main(g, core, T, topo):
             act(["sq%d" % k], ["oh%d" % s], T.oh[:, 0:n, s], T["sq%d" % k][:, 0:n], F.Relu, bias=1.0, scale=-1.0)
 
     OH = ["oh%d" % s for s in range(16)]
-    oh_a("cur0", 145, [(11, 11)])
-    for s in range(11):
+    for s in range(2, S0):
         oh_v("cur0", 145, s, s)
     for m in range(18):
         mm(OH, ["ps1"], T.ps1[:, 0:96], T.oh[:, 8 * m:8 * m + 8, :], T.oh[:, 8 * m + 1:8 * m + 9, 0:S0], m == 0, m == 17)
     aff(["c01"], ["c8"], C(10), C(1), -16.0, 111.0)
-    tt(["c01"], ["c2_"], C(2), C(0), C(1), A.subtract)
+    ts(["pi"], ["pg"], T.pi[:, 2:3], T.pi[:, 0:1], 16, A.bitwise_and)
+    ts(["c01"], ["c30_"], C(30), C(1), 2.0, A.is_equal)
+    tt(["ps3a", "posi"], ["ri"], T.ri[:], T.ps3[:, 0:CH], T.posi[:], A.max)
     ts(["xf", "c01"], ["i16"], T.i16[:], T.xf[:, 0:16], C(1), A.is_equal)
-    ts(["c01"], ["c18"], C(18), C(1), float(S0), A.is_ge, 96.0, A.mult)
-    ms(["gsz"], T.gs[:, 96:97], -256.0)
-    aff(["c2_", "c18"], ["c19"], C(19), C(2), 0.75, C(18))
     ts(["x16", "c01"], ["sel"], T.sel[:], T.x16[:, 0:128], C(1), A.is_equal, 256.0, A.mult)
-    ms(["ptieb"], T.ptie[:, 16:48], -30000.0)
+    ms(["ptieb"], T.ptie[:, 16:52], -30000.0)
     ts(["x16", "c8"], ["ptiea"], T.ptie[:, 0:16], T.x16[:, 0:16], C(10), A.subtract, -1.0 / 2048, A.mult)
     ts(["i16"], ["poff"], T.poff[:], T.i16[:], -30000.0, A.mult, -CNT0 / 8 + 2048.0, A.add)
     ts(["c19", "c01"], ["offx0"], T.offx[:, 0:1], C(19), C(1), A.add, 96.0, A.min)
     ms(["neg"], T.neg[:], -1e9)
-    cp(["ri"], ["posv"], T.posv[:], T.ri[:])
-    ts(["cur0"], ["ps3a"], P(0, -4, 149), S("cur0", -4, 149), -16.0, A.mult, 111.0, A.add)
-    aff(["c2_"], ["c7"], C(7), C(2), 3.0 / 16, 0.0)
-    aff(["c2_"], ["c7"], C(8), C(2), 3.0 / 16, 0.0)
+    ts(["pg"], ["odd"], C(7), T.pi[:, 2:3], 2.0 ** 23, A.mult, -2.0 ** 26, A.add)
+    ts(["pg"], ["even"], C(8), T.pi[:, 2:3], 0.0, A.is_equal)
+    aff(["zi"], ["pbig"], T.pbig[:], ident, 2.0 ** 18, 0.0)
     aff(["zi"], ["nzi"], T.nzi[:], ident, -1.0, 0.0)
     aff(["zi"], ["i16x"], T.i16x[:], ident, 16.0, 0.0)
     act(["zi"], ["id32"], T.id32[:], ident, F.Copy)
     aff(["zi"], ["n512"], T.n512[:], ident, -512.0, 0.0)
     aff(["x16", "c8"], ["ctab"], T.ctab[:], T.x16[:, 0:16], -1.0, C(10))
-    aff(["x16"], ["xm16"], T.xm16[:], T.x16[:, 0:16], -16.0, 96.0)
-    for u in (1, 2):
-        act(["i16"], ["coef%dc" % u], T["coef%d" % u][:, 16:32], T.i16[:], F.Copy)
     aff(["c01"], ["c11"], C(11), C(1), 1.0, PRES)
     aff(["c2_"], ["c14"], C(14), C(2), 1.0, 15.0)
     aff(["c2_"], ["c16_"], C(16), C(2), 1.0, 4.0)
@@ -344,13 +353,22 @@ def rank_main(g, core, T, topo):
     aff(["c2_"], ["oo0"], T.oo[:, 0:1], C(2), 32.0, 0.0)
     aff(["c01"], ["c17"], C(17), C(0), -17.0, -float(L))
     aff(["ps4", "c17"], ["c6"], C(6), T.ps4[:, 0:1], 1.0, C(17))
+    for u in (1, 2):
+        n = S0 + u - 1
+        aff(["c4"], ["c33%d" % u], C(32 + u), C(4), n - 52.0, 52.0)
+        aff(["c01"], ["cn%d" % u], C(25 + u), C(1), 1.0, -float(n))
+        aff(["c01"], ["c31%d" % u], C(30 + u), C(1), -1.0, 111.0 - 16 * n + NEW)
+        aff(["c30_", "c33%d" % u], ["ca%d" % u], C(27 + u), C(30), 12.0 + n, C(32 + u))
+    aff(["zi", "even"], ["id0"], T.id0[:], ident, C(8), 0.0)
 
     def gather_y0(k):
         a, b = Y0CUT[k], Y0CUT[k + 1]
         act(["ves", "vesz", "posv"], ["y0%d" % k], T.y0[:, 16 * a:16 * b], T.ves[:, 0:M + 1].indirect(T.posv[:, a:b]), F.Copy)
 
     ts(["ps1"], ["gs"], T.gs[:, 0:96], T.ps1[:, 0:96], -256.0, A.add)
+    ts(["cur0"], ["ps3a"], P(0, -4, 149), S("cur0", -4, 149), -16.0, A.mult, 111.0, A.add)
     cp(["gs", "gsz", "offx0"], ["own0"], T.land0[:, 16 * rank:16 * rank + 16], T.gs[:, 0:97].indirect(T.offx[:, 0:1]))
+    cp(["ri"], ["posv"], T.posv[:], T.ri[:])
 
     direct, relays = routes(T, topo, core)
     off_eng = topo.engines(core, direct[0])
@@ -387,33 +405,49 @@ def rank_main(g, core, T, topo):
             if t == 0:
                 mm(["sel"] + rk, ["ps2"], T.ps2[:, 0:16], T.sel[:], land[:, 16 * r:16 * r + 16], False, fin)
             else:
-                mm(["sel"] + rk, ["ps2"], T.ps2[:, 0:16], T.sel[:], land[:, 32 * r:32 * r + 16], False, False)
-                mm(["lv%d" % t] + rk, ["ps2"], T.ps2[:, 0:16], T["lv%d" % t][:], land[:, 32 * r + 16:32 * r + 32], False, fin)
+                mm(["selpm0", "selpm1"] + rk, ["ps2"], T.ps2[:, 16:19], T.selpm[:], land[:, 24 * r + 7:24 * r + 24:8], False, False)
+                mm(["route"] + rk, ["ps2"], T.ps2[:, 18:19], T.route[:], land[:, 24 * r + 7:24 * r + 8], False, fin)
 
-    def key_fix(u):
-        mm(["sel", "dead%d" % u], ["ps2"], T.ps2[:, 0:16], T.sel[:], T["dead%d" % u][:], False, False)
-        mm(["sel", "cor%d" % u, "cor%db" % u], ["ps2"], T.ps2[:, 0:16], T.sel[:], T["cor%d" % u][:], False, False)
-        mm(["lv%d" % u, "corv"], ["ps2"], T.ps2[:, 0:16], T["lv%d" % u][:], T.corv[:], False, False)
+    def KC(u):
+        return ["kb%dc%d" % (u, k) for k in range(5)]
 
     def key_close(t):
         if t > 0:
-            mm(["id32", "keep"], ["ps2"], T.ps2[:, 0:48], T.id32[:], T.keep[:], True, False)
-            key_fix(t)
+            kb, n = "kb%d" % t, S0 + t - 1
+            mm(["id32", kb] + KC(t), ["ps2"], T.ps2[:, 0:52], T.id32[:], T[kb][:, 0:52], True, False)
+            mm(["id0", "ext"], ["ps2"], T.ps2[:, 16:19], T.id0[:], T.ext[:, 0:3], False, False)
+            mm(["pbig", "killa%d" % t], ["ps2"], T.ps2[:, 0:n], T.pbig[:], T["killa%d" % t][:, 0:n], False, False)
+            mm(["pbig", "killb"], ["ps2"], T.ps2[:, 0:17], T.pbig[:], T.killb[:, 0:17], False, False)
+            mm(["pbig", "dead%d" % t], ["ps2"], T.ps2[:, 0:16], T.pbig[:], T["dead%d" % t][:], False, False)
+            mm(["route", "c2048"], ["ps2"], T.ps2[:, 18:19], T.route[:], T.c2048[:, 0:1], False, False)
         else:
-            mm(["sel", "ptiea", "ptieb"], ["ps2"], T.ps2[:, 0:48], T.sel[:], T.ptie[:], True, False)
+            mm(["sel", "ptiea", "ptieb"], ["ps2"], T.ps2[:, 0:52], T.sel[:], T.ptie[:], True, False)
             mm(["sel", "poff"], ["ps2"], T.ps2[:, 0:16], T.sel[:], T.poff[:], False, False)
         key_terms(t, [rank], False)
         wait("p", ("ad%d" % t, n_ad))
         key_terms(t, near, False)
         wait("p", ("ar%d" % t, n_ar))
         key_terms(t, farr, True)
+        if t == 1:
+            mm(["sel", "c2048"], ["ps4"], T.ps4[:, 0:3], T.sel[:], T.c2048[:, 0:3], True, False)
+            for r in range(8):
+                mm(["sel"], ["ps4"], T.ps4[:, 0:3], T.sel[:], T.land1[:, 24 * r + 7:24 * r + 24:8], False, r == 7)
 
-    WADD = ["wadd%d" % k for k in range(8)]
+    def table2():
+        ts(["killa1", "ps4"], ["mrga"], T.mrg[:, 0:S0], T.killa1[:, 0:S0], T.ps4[:, 0:1], A.mult, 1.0 / 256, A.mult)
+        cp(["ps4"], ["mrgn"], T.mrg[:, S0:S0 + 1], T.ps4[:, 1:2])
+        ts(["i16", "ps4"], ["mrgr"], T.mrg[:, 16:32], T.i16[:], T.ps4[:, 2:3], A.mult)
+        mm(["id32", "kb1"], ["ps4"], T.ps4[:, 16:32], T.id32[:], T.kb1[:, 0:16], True, False)
+        mm(["id32", "mrga", "mrgn"], ["ps4"], T.ps4[:, 16:17 + S0], T.id32[:], T.mrg[:, 0:S0 + 1], False, False)
+        mm(["lv32", "mrgr"], ["ps4"], T.ps4[:, 16:32], T.lv32[:], T.mrg[:, 16:32], False, False)
+        mm(["pbig", "dead1"], ["ps4"], T.ps4[:, 16:32], T.pbig[:], T.dead1[:], False, True)
+        act(["ps4"], ["kb2"], T.kb2[:, 0:16], T.ps4[:, 16:32], F.Copy)
+
     def winner(t):
         b = 8 * t
-        scan(["ps2", "neg"], ["sc"], T.sc[:, 16:64], T.ps2[:, 0:48], T.neg[:], -1e9, A.max, A.max)
-        if t < 2:
-            act(["ps2"], ["keep"], T.keep[:], T.ps2[:, 0:48], F.Copy)
+        scan(["ps2", "neg"], ["sc"], T.sc[:, 12:64], T.ps2[:, 0:52], T.neg[:], -1e9, A.max, A.max)
+        if t == 0:
+            act(["ps2"], ["kb1"], T.kb1[:, 0:16], T.ps2[:, 0:16], F.Copy)
         op("v", ["sc"], ["sct"], lambda: V.transpose(T.sct[:, 0:32], T.sc[:, 32:64]))
         scan(["sct", "sctz"] + WADD, ["w%d%d" % (k, t) for k in WCOL], T.wo[:, 40 * t:40 * t + 39], T.sct[:, 0:39],
              T.wadd[:, 40 * t:40 * t + 39], -3e9, A.max, A.add)
@@ -427,71 +461,86 @@ def rank_main(g, core, T, topo):
     def delta_open():
         mm(["zi", "km256"], ["ps1"], T.ps1[:, 0:24], ident, T.km256[:], True, False)
 
-    def delta(t, marks):
+    def delta(t, marks, more):
         b, u = 8 * t, t + 1
         cb, n = "cb%d" % t, S0 + t
         w = ["w%d%d" % (k, t) for k in range(8)]
         for lo, hi in ((0, 8), (8, 18)):
-            ts([cb + "a", cb + "b", cb + "c", w[0], w[1]], ["mrk%d" % lo], T.mrk[:, 24 * lo:24 * hi], T[cb][:, 3 + 24 * lo:3 + 24 * hi],
+            ts([cb + "a", cb + "b", cb + "c", w[0], w[1]], ["mrk%d" % lo], T.mrk[:, :, 8 * lo:8 * hi], T[cb][:, :, 1 + 8 * lo:1 + 8 * hi],
                W(b + 1), A.add, W(b), A.is_equal)
             for m in range(lo, hi):
-                mm(OH + ["mrk%d" % lo], ["ps1"], T.ps1[:, 0:24], T.oh[:, 8 * m:8 * m + 8, :], T.mrk[:, 24 * m:24 * m + 24],
+                mm(OH + ["mrk%d" % lo], ["ps1"], T.ps1[:, 0:24], T.oh[:, 8 * m:8 * m + 8, :], T.mrk[:, :, 8 * m:8 * m + 8],
                    False, m == 17)
         tt([w[0], w[1]], [w[2]], W(b + 2), W(b), W(b + 1), A.subtract)
         ts([w[4], w[0]], [w[7]], W(b + 7), W(b + 4), W(b), A.subtract, 15.0 - n, A.add)
         ts([w[5], w[1]], [w[6]], W(b + 6), W(b + 5), W(b + 1), A.subtract, -1.0 / 16, A.mult)
-        ts(["xm16", w[1], w[4]], ["coef%da" % u], T["coef%d" % u][:, 0:n], T.xm16[:, 0:n], W(b + 1), A.add, W(b + 4), A.is_equal)
+        if t == 1:
+            table2()
         marks()
-        tt(["ps1", "sgn"], ["gs"], T.gs[:, 0:24], T.ps1[:, 0:24], T.sgn[:], A.mult)
-        ts(["ctab", w[2]], ["dead%d" % u], T["dead%d" % u][:], T.ctab[:], W(b + 2), A.is_equal, -30000.0, A.mult)
-        tt(["gs", "offx%d" % u, "coef%da" % u, "coef%db" % u, "coef%dc" % u], ["own%d" % u], T["land%d" % u][:, 32 * rank:32 * rank + 32],
-           T.gs[:, 0:24].indirect(T.offx[:, 2 * u:2 * u + 2]), T["coef%d" % u][:], A.mult)
+        scan(["rst", "ps1"], ["own%d" % u], T["land%d" % u][:, 24 * rank:24 * rank + 24], T.rst[:], T.ps1[:, 0:24], -30000.0,
+             A.add, A.max)
         send(u)
+        more()
 
     def fixes(t):
         b, u, n = 8 * t, t + 1, S0 + t
-        ts(["x15", "w7%d" % t], ["lv%d" % u], T["lv%d" % u][:, :, 0:n], T.x15[:, :, 15 - n:15], W(b + 7), A.is_equal, -256.0, A.mult)
-        ts(["coef%da" % u], ["cor%d" % u], T["cor%d" % u][:, 0:n], T["coef%d" % u][:, 0:n], -2048.0, A.mult)
+        w2, w6, w7 = "w2%d" % t, "w6%d" % t, "w7%d" % t
+        ts(["cn%d" % u, w7], ["colb"], C(24), C(26 + t), W(b + 7), A.is_equal, -256.0, A.mult)
+        ts(["c4", "ca%d" % u, w6], ["offt1"], C(25), C(4), W(b + 6), A.mult, C(28 + t), A.add)
+        ts(["x15", w6], ["killa%d" % u], T["killa%d" % u][:, 0:n], T.x15[:, 0, 15 - n:15], W(b + 6), A.is_equal, -256.0, A.mult)
+        ts(["ctab", w2], ["dead%d" % u], T["dead%d" % u][:], T.ctab[:], W(b + 2), A.is_equal, -256.0, A.mult)
+        if t == 0:
+            ts(["x15", w7], ["lv32"], T.lv32[:, :, 0:n], T.x15[:, :, 15 - n:15], W(b + 7), A.is_equal, -0.125, A.mult)
+        ts(["kone", "colb"], ["killb"], T.killb[:, 0:17], T.kone[:, 0:17], C(24), A.mult)
+        ts(["x15", w6, "colb"], ["route"], T.route[:, :, 0:n], T.x15[:, 0:4, 15 - n:15], W(b + 6), A.is_equal, C(24), A.mult)
+        ts(["c30_", w7, "offt1"], ["offx"], T.offx[:, 2:3], C(30), W(b + 7), A.mult, C(25), A.add)
+
+    def turn(u):
+        kb = "kb%d" % u
+        op("v", [kb] + KC(u), [kb + "t"], lambda: V.transpose(T[kb][:, 64:96], T[kb][:, 0:32]))
+
+    def pick(u):
+        kb = "kb%d" % u
+        cp(KC(u) + [kb, kb + "t", "offx"], ["ext"], T.ext[:], T[kb][:].indirect(T.offx[:, 2:3]))
 
     send(0)
     gather_y0(0)
-    ms(["sctz"], T.sct[:, 32:40], -3e9)
-    for k, (c, v) in enumerate(((33, MAGIC16), (34, -MAGIC16), (37, MAGIC), (38, -MAGIC))):
-        op("v", ["wadd0"], ["wadd%d" % (4 + k)], lambda: V.memset(T.wadd[:, c:120:40], v))
 
     BLK = [[-16, 8], [0, 16]]
-    select(["kone"], ["bt0"], T.bt0[:], T.kone[:, 0:128], BLK, A.is_ge, 0.0, 0, 1)
-    select(["bt0"], ["bones"], T.bones[:], T.bt0[:], [[16, 8], [0, 16]], A.is_ge, 0.0, 15, -1)
-    select(["bones"], ["bt0"], T.bt0[:], T.bones[:], [[1, 128]], A.is_gt, 0.0, 0, -1)
-    select(["bt0"], ["btri"], T.btri[:], T.bt0[:], [[1, 128]], A.not_equal, -0.5, 0, -1)
-    select(["bones"], ["bt0"], T.bt0[:], T.bones[:], [[-1, 128]], A.is_gt, 0.0, 0, 1)
-    select(["bt0"], ["bup"], T.bup[:], T.bt0[:], [[1, 128]], A.not_equal, 1.5, 0, -1)
+    select(["kone"], ["bones"], T.bones[:], T.kone[:, 0:128], BLK, A.is_ge, 0.0, 0, 1)
     select(["kone"], ["bs0"], T.bs0[:], T.kone[:, 0:128], BLK, A.is_equal, 0.0, 0, 1)
+    select(["bones"], ["bones"], T.bones[:], T.bones[:], [[16, 8], [0, 16]], A.is_ge, 0.0, 15, -1)
+    iota(["k35"], T.k35[:], [[0, 160]], 35, 0)
+    select(["bones"], ["btri"], T.btri[:], T.bones[:], [[1, 128]], A.is_gt, 0.0, 0, -1)
     tt(["ps3a", "cur0"], ["c0"], S("c0", -4, 149), P(0, -4, 149), S("cur0", -3, 150), A.subtract)
-    ts(["c7"], ["offx1", "offx2"], T.offx[:, 3:6:2], T.col[:, 7:9], 2.0, A.add)
+    ms(["c2048"], T.c2048[:], 2048.0)
+    ms(["route"], T.route[:], 0.0)
+    ms(["sctz"], T.sct[:, 32:40], -3e9)
     tt(["c0"], ["ps3b"], P(1, -1, 144), S("c0", 0, 145), S("c0", -2, 143), A.not_equal)
-    cp(["c0"], ["cb0a"], T.cb0[:, 0:435:3], S("c0", 0, 145))
-    tt(["ps3b", "c0"], ["cb0b"], T.cb0[:, 4:436:3], P(1, 0, 144), S("c0", 1, 145), A.mult)
-    tt(["ps3b", "c0"], ["cb0c"], T.cb0[:, 5:437:3], P(1, -1, 143), S("c0", -2, 142), A.mult)
+    cp(["c0"], ["cb0a"], T.cb0[:, 0, 0:145], S("c0", 0, 145))
+    for k, (c, v) in enumerate(((33, MAGIC16), (34, -MAGIC16), (37, MAGIC), (38, -MAGIC))):
+        op("v", ["wadd0"], [WADD[k + 6]], lambda: V.memset(T.wadd[:, c:120:40], v))
+    tt(["ps3b", "c0"], ["cb0b"], T.cb0[:, 1, 1:145], P(1, 0, 144), S("c0", 1, 145), A.mult)
+    tt(["ps3b", "c0"], ["cb0c"], T.cb0[:, 2, 1:145], P(1, -1, 143), S("c0", -2, 142), A.mult)
     delta_open()
     lin("ps6", 151, [("zi", "c0", -3)], True, False)
     lin("ps0", 152, [("nzi", "cur0", -3)], True, False)
     key_close(0)
-    for u in (1, 2):
-        n = S0 + u - 1
-        ts(["c01", "c7"], ["offx%d" % u], T.offx[:, 2 * u:2 * u + 1], C(1), float(n), A.is_equal, C(7), A.add)
-        ts(["x15"], ["lv%d" % u], T["lv%d" % u][:], T.x15[:], n - 15.0, A.is_equal, 256.0, A.mult)
-        ts(["x16"], ["coef%db" % u], T["coef%d" % u][:, n:16], T.x16[:, n:16], float(n), A.is_equal)
-        ts(["x16"], ["cor%db" % u], T["cor%d" % u][:, n:16], T.x16[:, n:16], float(n), A.is_equal, 2048.0, A.mult)
-    ts(["i16"], ["corv"], T.corv[:], T.i16[:], 2048.0, A.mult)
-    ts(["pi"], ["pg"], T.pi[:, 2:3], T.pi[:, 0:1], 16, A.bitwise_and)
     ts(["c16", "c16_"], ["smi"], T.smi[:, 0:9], T.c16[:, 0:9], C(16), A.subtract, 1.0 / 9, A.mult)
     ts(["pg", "oo0"], ["c12"], C(12), T.pi[:, 2:3], T.oo[:, 0:1], A.subtract, -31.0, A.add)
-    ts(["xf", "c14", "c11"], ["zw"], T.zw[:, 0:144], T.xf[:, 0:144], C(14), A.is_equal, C(11), A.mult)
+    for u in (1, 2):
+        ts(["odd"], ["kb%dc0" % u], T["kb%d" % u][:, 16:17], C(7), -1.0, A.mult, -BACK, A.min)
+        ts(["odd", "c8"], ["kb%dc1" % u], T["kb%d" % u][:, 17:18], C(10), NEW - (S0 + u - 1), A.add, C(7), A.min)
     ts(["smi", "c12"], ["sm1"], T.sm[:, 20:29], T.smi[:, 0:9], -287.0, A.mult, C(12), A.add)
-    ts(["sm0", "c01"], ["offd"], T.offd[:], T.sm[:, 0:18], C(1), A.add)
-    tt(["thr", "sm1"], ["sm1"], T.sm[:, 20:29], T.sm[:, 20:29], T.thr[:, 0:9], A.add)
-    cp(["sm1"], ["offt"], T.offt[:, 0:9], T.sm[:, 20:29])
+    ts(["x15"], ["lv32"], T.lv32[:], T.x15[:], S0 - 15.0, A.is_equal, 0.125, A.mult)
+    for u in (1, 2):
+        kb = T["kb%d" % u]
+        ts(["odd", "c31%d" % u, "kb%dc0" % u], ["kb%dc2" % u], kb[:, 18:19], C(30 + u), C(7), A.min, kb[:, 16:17], A.max)
+    tt(["thr", "sm1"], ["sm2"], T.sm[:, 0:9], T.sm[:, 20:29], T.thr[:, 0:9], A.add)
+    for h, v in enumerate((-256.0, 256.0)):
+        ts(["x16", "c01"], ["selpm%d" % h], T.selpm[:, :, 16 * h:16 * h + 16], T.x16[:, 0:64], C(1), A.is_equal, v, A.mult)
+    ts(["xf", "c14", "c11"], ["zw"], T.zw[:, 0:144], T.xf[:, 0:144], C(14), A.is_equal, C(11), A.mult)
+    cp(["sm2"], ["offt"], T.offt[:, 0:9], T.sm[:, 0:9])
 
     winner(0)
     tie0 = W(2)
@@ -500,21 +549,23 @@ def rank_main(g, core, T, topo):
         ts(["c0", "w20", "w70"], ["hb"], S("hb", -4, 149), S("c0", -4, 149), tie0, A.is_equal, W(7), A.mult)
         ts(["c0", "w20", "w60"], ["ha"], S("ha", -4, 149), S("c0", -4, 149), tie0, A.is_equal, W(6), A.mult)
 
-    delta(0, marks0)
-    iota(["k35"], T.k35[:], [[0, 160]], 35, 0)
-    iota(["crowb"], T.crow[:, 0:145], [[16, 145]], -16, 0)
-    iota(["crowc"], T.crow[:, 145:147], [[0, 2]], L + int(PRES), 0)
-    iota(["kt1"], T.kt[:, CH:CH + 1], [[0, 1]], 2, 0)
-    iota(["lo0"], T.lo[:, 145:146], [[0, 1]], 0, 0)
-    ts(["c0", "w20"], ["ht"], S("ht", -4, 149), S("c0", -4, 149), tie0, A.is_equal, tie0, A.mult)
+    def more0():
+        ts(["c0", "w20"], ["ht"], S("ht", -4, 149), S("c0", -4, 149), tie0, A.is_equal, tie0, A.mult)
+
+    delta(0, marks0, more0)
+    ts(["c0", "w20"], ["h0"], S("h0", -4, 149), S("c0", -4, 149), tie0, A.is_equal)
+    select(["bones"], ["bup"], T.bup[:], T.bones[:], [[-1, 128]], A.is_gt, 0.0, 0, 1)
+    select(["btri"], ["btri"], T.btri[:], T.btri[:], [[1, 128]], A.not_equal, -0.5, 0, -1)
+    select(["bup"], ["bup"], T.bup[:], T.bup[:], [[1, 128]], A.not_equal, 1.5, 0, -1)
     lin("ps0", 152, [("zi", "hb", -4), ("zi", "ha", -3)], False, True)
     lin("ps6", 151, [("i16x", "hb", -4), ("zi", "ha", -2), ("nzi", "ht", -3)], False, True)
     aff(["ps0"], ["rc1"], S("rc1", -3, 149), T.ps0[:, 0:152], 1.0, 12.0)
     oh_a("rc1", 144, [(10, 2), (11, 1), (12, 0)])
     record(0)
-    ts(["c0", "w20"], ["h0"], S("h0", -4, 149), S("c0", -4, 149), tie0, A.is_equal)
     ts(["c0", "w20"], ["ps3b"], P(1, -4, 149), S("c0", -4, 149), tie0, A.not_equal)
+    turn(1)
     fixes(0)
+    pick(1)
     delta_open()
     lin("ps5", 147, [("zi", "k35", -1), ("n512", "h0", -1), ("i16x", "rc1", -1), ("zi", "rc1", 0)], True, False)
     lin("ps7", 147, [("zi", "h0", -1)], True, False)
@@ -525,10 +576,10 @@ def rank_main(g, core, T, topo):
         lambda: scan(["h0", "ps6"], ["cbk"], S("cbk", -2, 147), S("h0", -3, 146), T.ps6[:, 0:149], 0.0, A.mult, A.add),
         lambda: tt(["ps6", "ne"], ["ca"], S("ca", -1, 147), T.ps6[:, 2:150], S("ne", -1, 147), A.add),
         lambda: tt(["ps3b", "cbk"], ["ps3c"], P(2, -1, 144), P(1, -1, 144), S("cbk", -1, 144), A.mult),
-        lambda: tt(["ps3b", "ca"], ["cb1a"], T.cb1[:, 0:435:3], P(1, -1, 144), S("ca", 0, 145), A.mult),
-        lambda: tt(["ps3c", "cb1a"], ["ne"], S("ne", -1, 144), P(2, -1, 144), T.cb1[:, 0:435:3], A.not_equal),
-        lambda: tt(["ps3c", "ne"], ["cb1c"], T.cb1[:, 5:437:3], P(2, -1, 143), S("ne", -1, 143), A.mult),
-        lambda: tt(["cb1a", "ne"], ["cb1b"], T.cb1[:, 4:436:3], T.cb1[:, 3:435:3], S("ne", 0, 144), A.mult)]
+        lambda: tt(["ps3b", "ca"], ["cb1a"], T.cb1[:, 0, 0:145], P(1, -1, 144), S("ca", 0, 145), A.mult),
+        lambda: tt(["ps3c", "cb1a"], ["ne"], S("ne", -1, 144), P(2, -1, 144), T.cb1[:, 0, 0:145], A.not_equal),
+        lambda: tt(["ps3c", "ne"], ["cb1c"], T.cb1[:, 2, 1:145], P(2, -1, 143), S("ne", -1, 143), A.mult),
+        lambda: tt(["cb1a", "ne"], ["cb1b"], T.cb1[:, 1, 1:145], T.cb1[:, 0, 1:145], S("ne", 0, 144), A.mult)]
     hot = list(range(10))
     for step, fill in zip(steps, (0, 1, 1, 2, 3, 3, 0, 0)):
         step()
@@ -543,27 +594,36 @@ def rank_main(g, core, T, topo):
         ts(["cbk", "w21", "w71"], ["mb"], S("mb", -1, 147), S("cbk", -1, 147), tie1, A.is_equal, W(15), A.mult)
         ts(["ca", "w21", "w61"], ["ma"], S("ma", -1, 147), S("ca", -1, 147), tie1, A.is_equal, W(14), A.mult)
 
-    delta(1, marks1)
-    iota(["kbig"], T.kbig[:], [[0, 160]], 16384, 0)
+    def more1():
+        ts(["ps6", "w21"], ["h1"], S("h1", -1, 146), T.ps6[:, 2:149], tie1, A.is_equal)
+        lin("ps5", 147, [("i16x", "mb", -1), ("zi", "ma", 0), ("n512", "h1", -1)], False, True)
+        lin("ps7", 147, [("zi", "h1", -1)], False, True)
+        lin("ps0", CH, [("zi", "ma", 0), ("zi", "mb", 0)], False, False)
+
+    delta(1, marks1, more1)
+    iota(["crowb"], T.crow[:, 0:145], [[16, 145]], -16, 0)
+    iota(["crowc"], T.crow[:, 145:147], [[0, 2]], L + int(PRES), 0)
+    iota(["kt1"], T.kt[:, CH:CH + 1], [[0, 1]], 2, 0)
+    iota(["lo0"], T.lo[:, 145:146], [[0, 1]], 0, 0)
+    iota(["kbig"], T.kbig[:], [[0, 160]], 49152, 0)
     iota(["y0z"], T.y0[:, L:L + 1], [[0, 1]], 0, 0)
     iota(["ggr"], T.gg[:, 16 + L:32 + L], [[0, 16]], 15, 0)
-    ts(["ps6", "w21"], ["h1"], S("h1", -1, 146), T.ps6[:, 2:149], tie1, A.is_equal)
-    lin("ps5", 147, [("i16x", "mb", -1), ("zi", "ma", 0), ("n512", "h1", -1)], False, True)
-    lin("ps7", 147, [("zi", "h1", -1)], False, True)
-    lin("ps0", CH, [("zi", "ma", 0), ("zi", "mb", 0)], False, False)
     record(1)
     aff(["bones"], ["nbones"], T.nbones[:], T.bones[:], -2.0, 0.0)
     aff(["btri"], ["nbtri"], T.nbtri[:], T.btri[:], -2.0, 0.0)
     aff(["bup"], ["nbup"], T.nbup[:], T.bup[:], -2.0, 0.0)
     gather_y0(1)
     fixes(1)
+    turn(2)
+    for h in range(2):
+        ts(["ps5"], ["xd%d" % h], T.xd[:, :, 16 * h:16 * h + 16], T.ps5[:, 0:CH], 0.0, A.max)
+    pick(2)
     key_close(2)
     ts(["ps5"], ["cz2"], T.cz2[:, 16:163], T.ps5[:, 0:147], 0.0, A.max)
-    cp(["cz2", "offd"], ["xd"], T.xd[:], T.cz2[:, 16:16 + CH].indirect(T.offd[:, 0:18]))
+    op("v", ["xd0", "xd1"], ["xt"], lambda: V.transpose(T.xt[:], T.xd[:]))
     tt(["ps7", "cz2"], ["ps3a"], P(0, 0, 145), T.cz2[:, 18:163], T.ps7[:, 1:146], A.mult)
-    op("v", ["xd"], ["xt"], lambda: V.transpose(T.xt[:], T.xd[:]))
-    tt(["ps3a", "cz2"], ["s1"], S("s1", 0, 145), P(0, 0, 145), T.cz2[:, 17:162], A.add)
     ts(["xt", "offt"], ["et"], T.et[:, 0:CH], T.xt[:, 0:288].indirect(T.offt[:, 0:9]), -128.0, A.add)
+    tt(["ps3a", "cz2"], ["s1"], S("s1", 0, 145), P(0, 0, 145), T.cz2[:, 17:162], A.add)
     tt(["ps7", "s1"], ["ps3b"], P(1, 0, 144), S("s1", 1, 145), T.ps7[:, 1:145], A.mult)
     ts(["et"], ["kt"], T.kt[:, 0:CH], T.et[:, 0:CH], -127.5, A.is_gt, 2.0, A.mult)
     tt(["ps3b", "cz2"], ["ca2"], S("ca2", 0, 144), P(1, 0, 144), T.cz2[:, 17:161], A.add)
@@ -580,7 +640,8 @@ def rank_main(g, core, T, topo):
     ts(["w02", "w12"], ["w62"], W(22), W(16), W(17), A.subtract, 128.0, A.add)
     ts(["ca2", "w62"], ["m14"], S("m14", 0, 144), S("ca2", 0, 144), W(22), A.is_equal, -16.0, A.mult)
     lin("ps0", CH, [("zi", "m14", 0)], False, True)
-    scan(["ps5", "kbig"], ["idx"], T.idx[:, 0:145], T.ps5[:, 0:145], T.kbig[:, 0:145], -14.5, A.add, A.min)
+    scan(["ps5", "kbig"], ["ps3a"], T.ps3[:, 0:145], T.ps5[:, 0:145], T.kbig[:, 0:145], 32800 - 14.5, A.add, A.min)
+    scan(["ps5", "kbig"], ["idx"], T.idx[:, 0:145], T.ps5[:, 0:145], T.kbig[:, 0:145], 32800 - 14.5, A.add, A.min)
     scan(["ps4", "kbig", "oo0"], ["oo"], T.oo[:, 1:146], T.ps4[:, 0:145], T.kbig[:, 0:145], T.oo[:, 0:1], A.add, A.min)
 
     def count(u):
@@ -590,8 +651,7 @@ def rank_main(g, core, T, topo):
 
     act(["ps0"], ["xs"], T.xs[:, 0:CH], T.ps0[:, 0:CH], F.Relu, bias=2.0)
     dma("s", ["xs"], ["gg%d" % a for a, _ in VCUT + ACUT], T.gg[0:128:16, 16:16 + L], T.xs[:, 0:CH], "dsy")
-    ts(["idx"], ["ps3a"], T.ps3[:, 0:145], T.idx[:, 0:145], MAGIC32, A.add, MAGIC32, A.subtract)
-    tt(["idx", "ps3a"], ["zb"], T.zb[:, 0:145], T.idx[:, 0:145], T.ps3[:, 0:145], A.subtract)
+    tt(["idx", "ps3a"], ["zb"], T.zb[:, 0:145], T.ps3[:, 0:145], T.idx[:, 0:145], A.subtract)
     mm(["bs0", "zb"], ["ps7"], T.ps7[:, 0:145], T.bs0[:], T.zb[:, 0:145], True, True)
     for u in range(9):
         count(u)
@@ -616,7 +676,10 @@ def rank_main(g, core, T, topo):
     for b, kind, a in sorted(pieces):
         tu = "tua" if a < 16 * UA else "tub"
         if kind == "y":
-            cp(["y00", "y01", "y0z", tu], ["yo%d" % a], T.yo[:, 16 * a:16 * b], T.y0[:, 0:L + 1].indirect(T.tu[:, a:b]))
+            if b < CH:
+                cp(["y00", "y01", "y0z", tu], ["yo%d" % a], T.yo[:, 16 * a:16 * b], T.y0[:, 0:L + 1].indirect(T.tu[:, a:b]))
+            else:
+                act(["y00", "y01", "y0z", tu], ["yo%d" % a], T.yo[:, 16 * a:16 * b], T.y0[:, 0:L + 1].indirect(T.tu[:, a:b]), F.Copy)
             dma("s", ["yo%d" % a], [], T.y[:, 16 * a:16 * b], T.yo[:, 16 * a:16 * b])
             if a == 0:
                 ts(["xm", "ehub"], ["tub"], T.tu[:, 16 * UA:CH], T.xm[:, 0:146].indirect(T.ehu[:, UA:9]), -PRES, A.add)

from concourse.bass import DstId, RemoteDMATransfer
from concourse.mybir import AluOpType, AxisListType, ActivationFunctionType

A = AluOpType
F = ActivationFunctionType
L, M, S0 = 2304, 3584, 12
CH = L // 16
SW = M // 16
HL, HR = 4, 6
MAGIC = 3221225472.0
MAGIC16 = 201326592.0
WCOL = {0: 31, 4: 34, 5: 35, 1: 38}
CNT0 = 28672.0
BACK = 256.0 * 64 * 256
NEW = BACK - 256 * CNT0
PRES = 128.0
FA = 480
VCUT = [(44, 72), (18, 44), (8, 18), (0, 8)]
ACUT = [(72, 100), (100, 128), (128, 136), (136, 144)]
YCUT, FCUT = [0, 32, 64, 94, 120, 138, 144], [0, 64, 116, 144]
Y0CUT = [0, 88, 144]
UA = 4
PAY = (16, 24, 24)


def _sb(n, d):
    return ("sbuf", [128, n], d)


SCRATCH = {}
for _n in ("cur0", "rc1", "c0", "ca", "cbk", "ne", "h0", "h1", "ha", "hb", "ht", "ma", "mb", "s1", "kone", "kbig", "crow",
           "ca2", "et", "kt", "nd", "m14", "xs", "zb", "z1", "zw", "zi", "k35", "vm", "sq0", "sq1", "sq2"):
    SCRATCH[_n] = _sb(160, "bfloat16")
for _n in ("xf", "x16", "c16", "oo", "lo", "ml", "xm", "gs", "jc"):
    SCRATCH[_n] = _sb(160, "float32")
for _n in ("posi", "ri"):
    SCRATCH[_n] = _sb(CH, "int32")
for _n in ("posu", "posv", "tu"):
    SCRATCH[_n] = _sb(CH, "uint16")
for _n in ("bones", "btri", "nbones", "nbtri", "bs0", "bup", "nbup", "i16x", "nzi", "n512", "pbig"):
    SCRATCH[_n] = _sb(128, "bfloat16")
SCRATCH.update({
    "sti": _sb(SW, "int32"), "stb": _sb(SW, "bfloat16"), "stw": _sb(M, "bfloat16"),
    "lei": _sb(4, "int32"), "pi": _sb(8, "int32"), "col": _sb(64, "float32"),
    "win": _sb(64, "float32"), "i16": _sb(16, "bfloat16"),
    "gg": _sb(L + 32, "bfloat16"), "oh": ("sbuf", [128, 146, 16], "bfloat16"), "cz2": _sb(176, "bfloat16"),
    "ves": _sb(M + 16, "bfloat16"), "y0": _sb(L + 16, "bfloat16"), "yo": _sb(L, "bfloat16"), "fso": _sb(L, "float32"),
    "cb0": ("sbuf", [128, 3, 146], "bfloat16"), "cb1": ("sbuf", [128, 3, 146], "bfloat16"),
    "mrk": ("sbuf", [128, 3, CH], "bfloat16"),
    "ohz": _sb(16 * CH, "bfloat16"), "junk": _sb(9 * 146, "bfloat16"), "xd": ("sbuf", [128, 9, 32], "bfloat16"), "xt": _sb(288, "bfloat16"),
    "idx": _sb(160, "float16"), "bsel": _sb(128, "float32"), "km256": _sb(24, "bfloat16"), "rst": _sb(24, "float32"),
    "id32": _sb(128, "float32"), "id0": _sb(128, "float32"), "ctab": _sb(16, "float32"),
    "kb1": _sb(96, "float32"), "kb2": _sb(96, "float32"), "ext": _sb(16, "float32"), "mrg": _sb(32, "float32"),
    "sel": _sb(128, "float16"), "ptie": _sb(52, "float16"), "poff": _sb(16, "float16"), "c2048": _sb(8, "float16"),
    "dead1": _sb(16, "bfloat16"), "dead2": _sb(16, "bfloat16"), "killa1": _sb(16, "bfloat16"), "killa2": _sb(16, "bfloat16"),
    "killb": _sb(32, "bfloat16"), "neg": _sb(52, "float32"),
    "selpm": ("sbuf", [128, 4, 32], "float16"), "route": ("sbuf", [128, 4, 32], "float16"),
    "lv32": ("sbuf", [128, 8, 16], "float32"),
    "sc": _sb(64, "float32"), "sct": _sb(40, "float32"), "wo": _sb(120, "float32"), "wadd": _sb(120, "float32"),
    "x15": ("sbuf", [128, 8, 16], "bfloat16"),
    "thr": _sb(16, "float32"), "eh": _sb(16, "float32"),
    "sm": _sb(32, "float32"), "smi": _sb(16, "int32"), "mgb": _sb(16, "float32"),
    "offx": _sb(8, "uint16"), "offt": _sb(10, "uint16"), "ehu": _sb(10, "uint16"),
    "land0": _sb(8 * 16, "float16"), "land1": _sb(8 * 24, "float16"), "land2": _sb(8 * 24, "float16"),
    "hand": _sb(3 * 32, "float16"),
})
for _k in range(8):
    SCRATCH["ps%d" % _k] = ("psum", [128, 512], "float32")

SEMAPHORES = ["sv", "sa", "sp", "sg", "ls", "ls0", "ls1", "ls2", "ad0", "ad1", "ad2", "ar0", "ar1", "ar2", "rl0", "rl1", "rl2",
              "dpos", "dst", "dle", "dve", "dsw", "dsy", "dout"]


def bits(engines):
    m = 0
    for e in engines:
        m |= 1 << e
    return m


def routes(T, topo, core):
    others = [c for c in T.cores if c != core]
    direct = [c for c in others if topo.may_write(core, c)]
    far = [c for c in others if not topo.may_write(core, c)]
    cand = [c for c in topo.cores_of(core) if T.rank_of(c) is None and all(topo.may_write(c, d) for d in far)]
    cand.sort(key=lambda c: (topo.die(c) != topo.die(core), c))
    rel = cand[:2]
    half = (len(far) + 1) // 2
    return direct, [(rel[0], far[:half]), (rel[1], far[half:])]


def dst_id(topo, d, s):
    rid, pid = topo.addr(d, s)
    return DstId(rid=rid, pnc=pid)


def relay_main(g, core, T, topo, owner, dests):
    r = T.rank_of(owner)
    eng = topo.engines(core, dests[0])
    per = len(eng) // len(dests)
    n_in = (len(topo.engines(owner, core)) - len(eng)) // 2
    for t in range(3):
        w = PAY[t]
        g.wait_ge(T.sem["rl%d" % t], n_in)
        g.remote_dma_fused([RemoteDMATransfer(dst_ids=[dst_id(topo, d, core)], dma_engine_mask=bits(eng[k * per:(k + 1) * per]),
                                              remote_sem=T.sem["ar%d" % t], src=T.hand[:, 32 * t:32 * t + w],
                                              dst=T["land%d" % t][:, w * r:w * r + w]) for k, d in enumerate(dests)],
                           local_sem=T.sem.ls)
    g.wait_ge(T.sem.ls, 3 * per * len(dests))


def rank_program(g, core, T, topo):
    if T.rank_of(core) is not None:
        rank_main(g, core, T, topo)
        return
    for c in topo.cores_of(core):
        if T.rank_of(c) is not None:
            for rl, dests in routes(T, topo, c)[1]:
                if rl == core:
                    relay_main(g, core, T, topo, c, dests)


def rank_main(g, core, T, topo):
    rank = T.rank_of(core)
    Q = {"v": g.vector, "a": g.scalar, "p": g.tensor, "g": g, "s": g.sync}
    SEM = {"v": "sv", "a": "sa", "p": "sp", "g": "sg"}
    cnt = {"v": 0, "a": 0, "p": 0, "g": 0}
    seen = {}
    wr, rd = {}, {}

    def deps(q, r, w):
        need = {}

        def add(h):
            need[h[0]] = max(need.get(h[0], 0), h[1])
        for k in r:
            if k in wr:
                add(wr[k])
            if k.startswith("ps"):
                bank = k[:3]
                for h in rd.get(bank, []):
                    if h[0] != SEM.get(q):
                        add(h)
        for k in w:
            if k in wr:
                add(wr[k])
            for h in rd.get(k, []):
                add(h)
        for s in need:
            wait(q, (s, need[s]))

    def wait(q, h):
        if h[0] == "sp" and q == "p":
            return
        if seen.get((q, h[0]), 0) < h[1]:
            Q[q].wait_ge(T.sem[h[0]], h[1])
            seen[(q, h[0])] = h[1]

    def note(h, r, w):
        for k in r:
            rd.setdefault(k, []).append(h)
        for k in w:
            wr[k] = h
            rd[k] = []

    def op(q, r, w, fn):
        deps(q, r, w)
        cnt[q] += 1
        fn().then_inc(T.sem[SEM[q]], 1)
        note((SEM[q], cnt[q]), r, w)

    outs = [0]

    def dma(q, r, w, out, in_, sem=None):
        deps(q, r, w)
        if sem is None:
            outs[0] += 16
            Q[q].dma_start(out, in_).then_inc(T.sem.dout, 16)
        else:
            Q[q].dma_start(out, in_).then_inc(T.sem[sem], 16)
            note((sem, 16), r, w)

    V, ACT, PE = g.vector, g.scalar, g.tensor

    def ts(r, w, out, in0, s1, o1, s2=None, o2=None):
        if o2 is None:
            op("v", r, w, lambda: V.tensor_scalar(out, in0, s1, None, o1))
        else:
            op("v", r, w, lambda: V.tensor_scalar(out, in0, s1, s2, o1, o2))

    def tt(r, w, out, in0, in1, o):
        op("v", r, w, lambda: V.tensor_tensor(out, in0, in1, o))

    def cp(r, w, out, in_):
        op("v", r, w, lambda: V.tensor_copy(out, in_))

    def ms(w, ap, c):
        op("v", [], w, lambda: V.memset(ap, c))

    def scan(r, w, out, d0, d1, init, o0, o1):
        op("v", r, w, lambda: V.tensor_tensor_scan(out, d0, d1, init, o0, o1))

    def mm(r, w, out, lhsT, rhs, start, stop):
        op("p", r, w, lambda: PE.matmul(out, lhsT, rhs, start, stop))

    def lin(bank, n, terms, first=True, last=True):
        for k, (mat, name, lo) in enumerate(terms):
            lhsT = ident if mat == "zi" else T[mat][:]
            mm([mat, name], [bank], T[bank][:, 0:n], lhsT, S(name, lo, lo + n), first and k == 0, last and k == len(terms) - 1)

    def act(r, w, out, in_, func, **kw):
        op("a", r, w, lambda: ACT.activation(out, in_, func, **kw))

    def iota(w, out, pat, base, cm):
        op("g", [], w, lambda: g.iota(out, pat, base, cm, allow_small_or_imprecise_dtypes=True))

    def select(r, w, out, in_, pat, cmp, fill, base, cm):
        op("g", r, w, lambda: g.affine_select(out, in_, pat, cmp, fill, base, cm))

    def aff(r, w, out, in_, scale, bias):
        act(r, w, out, in_, F.Identity, bias=bias, scale=scale)

    def S(name, lo, hi):
        return T[name][:, HL + lo:HL + hi]

    def P(k, lo, hi):
        return T.ps3[:, 160 * k + HL + lo:160 * k + HL + hi]

    def C(k):
        return T.col[:, k:k + 1]

    def W(k):
        if k % 8 in WCOL:
            return T.wo[:, 40 * (k // 8) + WCOL[k % 8]:40 * (k // 8) + WCOL[k % 8] + 1]
        return T.win[:, k:k + 1]

    ident = T.zi[:, 15:143]

    dma("s", [], ["sti"], T.sti[:], T.st[:], "dst")
    dma("s", [], ["posi"], T.posi[:], T.pos[:], "dpos")
    dma("s", [], ["lei"], T.lei[0:8, 0:1], T.le[:], "dle")

    iota(["bsel"], T.bsel[0:8, :], [[1, 8], [0, 16]], 0, -1)
    iota(["c30"], T.col[0:8, 21:22], [[0, 1]], 0, 16)
    iota(["c31"], T.col[0:8, 22:23], [[0, 1]], 0, L)
    op("g", [], ["pi"], lambda: g.iota(T.pi[:, 0:1], [[0, 1]], 0, 1))
    iota(["xf"], T.xf[:], [[1, 160]], 0, 0)
    iota(["jc"], T.jc[:, 0:154], [[1, 154]], -HL, CH)
    iota(["kone"], T.kone[:], [[0, 160]], 1, 0)
    select(["kone"], ["zi"], T.zi[:], T.kone[:], [[1, 160]], A.is_equal, 0.0, -15, -1)
    iota(["c16"], T.c16[:, 0:CH], [[16, CH]], 0, 1)
    iota(["x16"], T.x16[:, 0:128], [[0, 8], [1, 16]], 0, 0)
    iota(["km256"], T.km256[:], [[0, 24]], -256, 0)
    iota(["x15"], T.x15[:], [[0, 8], [1, 16]], -15, 0)
    select(["km256"], ["km256"], T.km256[:], T.km256[:], [[0, 3], [-16, 8]], A.is_ge, -20000.0, 0, 1)
    iota(["wadd0"], T.wadd[:], [[0, 120]], 0, 0)
    select(["km256"], ["km256"], T.km256[:], T.km256[:], [[0, 3], [16, 8]], A.is_ge, -20000.0, 15, -1)
    select(["wadd0"], ["rst"], T.rst[:], T.wadd[:, 0:24], [[0, 3], [1, 8]], A.is_gt, -30000.0, 0, 0)
    iota(["thr"], T.thr[:, 0:9], [[512, 9]], 31, 32)
    WADD = ["wadd%d" % k for k in range(10)]
    for k, (lo, hi, step, base) in enumerate(((32, 120, 0, -8), (35, 80, 16, 96), (36, 80, -16, -96), (115, 116, 0, -96), (116, 117, 0, 96))):
        op("g", ["wadd0"], [WADD[k + 1]], lambda: g.iota(T.wadd[:, lo:hi:40], [[step, len(range(lo, hi, 40))]], base, 0,
                                                         allow_small_or_imprecise_dtypes=True))
    for u in (1, 2):
        iota(["kb%dc3" % u], T["kb%d" % u][:, 19:52], [[0, 33]], -16000000, 0)
        iota(["kb%dc4" % u], T["kb%d" % u][:, 52:64], [[0, 12]], 0, 0)

    ms(["stw0"], T.stw[:, 0:FA], -1.0)
    act(["stw0"], ["stw2"], T.stw[:, FA:2 * FA], T.stw[:, 0:FA], F.Copy)
    act(["stw0"], ["stw3"], T.stw[:, 2 * FA:3 * FA], T.stw[:, 0:FA], F.Copy)
    ms(["stw1"], T.stw[:, 3 * FA:M], -1.0)
    cp(["sti"], ["stb"], T.stb[:], T.sti[:])
    dma("s", ["stb"], ["stw0", "stw1", "stw2", "stw3"], T.stw[0:128:16, 0:M], T.stb[:], "dsw")
    dma("s", [], ["ves"], T.ves[:, 0:M], T.ve[:], "dve")
    ts(["bsel"], ["bsel"], T.bsel[0:8, :], T.bsel[0:8, :], 0.0, A.is_equal)
    ts(["pi"], ["pm"], T.pi[:, 1:2], T.pi[:, 0:1], 15, A.bitwise_and)
    for k in range(2):
        ts(["lei", "c3%d" % k], ["lef%d" % k], T.col[0:8, 5 + k:6 + k], T.lei[0:8, 0:1], T.col[0:8, 21 + k:22 + k], A.add)
    mm(["bsel", "lef0", "lef1"], ["ps4"], T.ps4[:, 0:2], T.bsel[0:8, :], T.col[0:8, 5:7], True, True)
    cp(["pi", "pm"], ["c01"], T.col[:, 0:2], T.pi[:, 0:2])
    cp(["posi"], ["posu"], T.posu[:], T.posi[:])
    ms(["ggl"], T.gg[:, 0:16], -1.0)
    ts(["c01"], ["c4"], C(4), C(1), 0.0, A.is_equal)
    ts(["c01"], ["c9"], C(9), C(0), 15.0, A.add)
    ms(["ggr"], T.gg[:, 16 + L:32 + L], -1.0)
    ts(["xf", "c9", "c4"], ["z1"], T.z1[:, 0:144], T.xf[:, 0:144], C(9), A.is_equal, C(4), A.mult)
    ts(["jc", "ps4"], ["vm"], T.vm[:, 0:154], T.jc[:, 0:154], T.ps4[:, 1:2], A.is_ge, -100.0, A.mult)
    for s in range(S0, 16):
        act(["xf"], ["oh%d" % s], T.oh[:, :, s], T.xf[:, 0:146], F.Copy, scale=0.0)

    STW = ["stw0", "posu"]
    have, todo = [], list(range(16))
    for (a, b), (c, d) in zip(VCUT, ACUT):
        cp(STW, ["gg%d" % a], T.gg[:, 16 + 16 * a:16 + 16 * b], T.stw[:].indirect(T.posu[:, a:b]))
        act(STW, ["gg%d" % c], T.gg[:, 16 + 16 * c:16 + 16 * d], T.stw[:].indirect(T.posu[:, c:d]), F.Copy)
        have += [(a, b), (c, d)]
        for i in list(todo):
            need = range(max(9 * i - 1, 0), min(9 * i + 10, CH))
            if all(any(x <= u < z for x, z in have) for u in need):
                todo.remove(i)
                mm(["z1", "ggl", "ggr"] + ["gg%d" % x for x, z in have if x < need[-1] + 1 and z > need[0]], ["ps0"],
                   T.ps0[:, 0:154], T.z1[:, 15 - i:143 - i], T.gg[:, 16 + CH * i - HL:16 + CH * i + CH + HR],
                   len(todo) == 15, len(todo) == 0)
        if len(have) == 4:
            mm(["zi", "vm"], ["ps0"], T.ps0[:, 0:154], ident, T.vm[:, 0:154], False, False)
    ms(["vesz"], T.ves[:, M:M + 16], 0.0)
    aff(["c01"], ["c2_"], C(2), C(1), -1.0, C(0))
    act(["c01"], ["c18"], C(18), C(1), F.Relu, bias=-96.0 * (S0 - 1), scale=96.0)
    act(["xf"], ["gsz"], T.gs[:, 96:97], T.xf[:, 0:1], F.Identity, bias=-256.0)
    aff(["c2_", "c18"], ["c19"], C(19), C(2), 0.75, C(18))
    ts(["c16", "ps4"], ["ps3a"], T.ps3[:, 0:CH], T.c16[:, 0:CH], T.ps4[:, 0:1], A.is_ge, float(M), A.mult)
    ts(["ps0"], ["cur0"], T.cur0[:, 0:154], T.ps0[:, 0:154], -1.0, A.max)
    for s in range(2):
        ts(["ps0"], ["oh%d" % s], T.oh[:, 0:145, s], T.ps0[:, HL:HL + 145], float(s), A.is_equal)

    def oh_v(cur, n, s, val):
        ts([cur], ["oh%d" % s], T.oh[:, 0:n, s], S(cur, 0, n), float(val), A.is_equal)

    def oh_a(cur, n, pairs):
        for k, (s, val) in enumerate(pairs):
            act([cur], ["sq%d" % k], T["sq%d" % k][:, 0:n], S(cur, 0, n), F.Square, bias=-float(val))
        for k, (s, val) in enumerate(pairs):
            act(["sq%d" % k], ["oh%d" % s], T.oh[:, 0:n, s], T["sq%d" % k][:, 0:n], F.Relu, bias=1.0, scale=-1.0)

    OH = ["oh%d" % s for s in range(16)]
    for s in range(2, S0):
        oh_v("cur0", 145, s, s)
    for m in range(18):
        mm(OH, ["ps1"], T.ps1[:, 0:96], T.oh[:, 8 * m:8 * m + 8, :], T.oh[:, 8 * m + 1:8 * m + 9, 0:S0], m == 0, m == 17)
    aff(["c01"], ["c8"], C(10), C(1), -16.0, 111.0)
    ts(["pi"], ["pg"], T.pi[:, 2:3], T.pi[:, 0:1], 16, A.bitwise_and)
    ts(["c01"], ["c30_"], C(30), C(1), 2.0, A.is_equal)
    tt(["ps3a", "posi"], ["ri"], T.ri[:], T.ps3[:, 0:CH], T.posi[:], A.max)
    ts(["xf", "c01"], ["i16"], T.i16[:], T.xf[:, 0:16], C(1), A.is_equal)
    ts(["x16", "c01"], ["sel"], T.sel[:], T.x16[:, 0:128], C(1), A.is_equal, 256.0, A.mult)
    ms(["ptieb"], T.ptie[:, 16:52], -30000.0)
    ts(["x16", "c8"], ["ptiea"], T.ptie[:, 0:16], T.x16[:, 0:16], C(10), A.subtract, -1.0 / 2048, A.mult)
    ts(["i16"], ["poff"], T.poff[:], T.i16[:], -30000.0, A.mult, -CNT0 / 8 + 2048.0, A.add)
    ts(["c19", "c01"], ["offx0"], T.offx[:, 0:1], C(19), C(1), A.add, 96.0, A.min)
    ms(["neg"], T.neg[:], -1e9)
    ts(["pg"], ["odd"], C(7), T.pi[:, 2:3], 2.0 ** 23, A.mult, -2.0 ** 26, A.add)
    ts(["pg"], ["even"], C(8), T.pi[:, 2:3], 0.0, A.is_equal)
    aff(["zi"], ["pbig"], T.pbig[:], ident, 2.0 ** 18, 0.0)
    aff(["zi"], ["nzi"], T.nzi[:], ident, -1.0, 0.0)
    aff(["zi"], ["i16x"], T.i16x[:], ident, 16.0, 0.0)
    act(["zi"], ["id32"], T.id32[:], ident, F.Copy)
    aff(["zi"], ["n512"], T.n512[:], ident, -512.0, 0.0)
    aff(["x16", "c8"], ["ctab"], T.ctab[:], T.x16[:, 0:16], -1.0, C(10))
    aff(["c01"], ["c11"], C(11), C(1), 1.0, PRES)
    aff(["c2_"], ["c14"], C(14), C(2), 1.0, 15.0)
    aff(["c2_"], ["c16_"], C(16), C(2), 1.0, 4.0)
    aff(["c01"], ["c13"], C(13), C(1), 16384.0, 8192.0 * (1.5 - 15.5))
    aff(["c2_"], ["oo0"], T.oo[:, 0:1], C(2), 32.0, 0.0)
    aff(["c01"], ["c17"], C(17), C(0), -17.0, -float(L))
    aff(["ps4", "c17"], ["c6"], C(6), T.ps4[:, 0:1], 1.0, C(17))
    for u in (1, 2):
        n = S0 + u - 1
        aff(["c4"], ["c33%d" % u], C(32 + u), C(4), n - 52.0, 52.0)
        aff(["c01"], ["cn%d" % u], C(25 + u), C(1), 1.0, -float(n))
        aff(["c01"], ["c31%d" % u], C(30 + u), C(1), -1.0, 111.0 - 16 * n + NEW)
        aff(["c30_", "c33%d" % u], ["ca%d" % u], C(27 + u), C(30), 12.0 + n, C(32 + u))
    aff(["zi", "even"], ["id0"], T.id0[:], ident, C(8), 0.0)

    def gather_y0(k):
        a, b = Y0CUT[k], Y0CUT[k + 1]
        act(["ves", "vesz", "posv"], ["y0%d" % k], T.y0[:, 16 * a:16 * b], T.ves[:, 0:M + 1].indirect(T.posv[:, a:b]), F.Copy)

    ts(["ps1"], ["gs"], T.gs[:, 0:96], T.ps1[:, 0:96], -256.0, A.add)
    ts(["cur0"], ["ps3a"], P(0, -4, 149), S("cur0", -4, 149), -16.0, A.mult, 111.0, A.add)
    cp(["gs", "gsz", "offx0"], ["own0"], T.land0[:, 16 * rank:16 * rank + 16], T.gs[:, 0:97].indirect(T.offx[:, 0:1]))
    cp(["ri"], ["posv"], T.posv[:], T.ri[:])

    direct, relays = routes(T, topo, core)
    off_eng = topo.engines(core, direct[0])
    on_eng = [e for e in topo.engines(core, relays[0][0]) if e not in off_eng]
    per = len(on_eng) // 2
    sent = [0]

    def send(t):
        w = PAY[t]
        src = T["land%d" % t][:, w * rank:w * rank + w]
        deps("g", ["own%d" % t], [])
        g.remote_dma_fused([RemoteDMATransfer(dst_ids=[dst_id(topo, rl, core)], dma_engine_mask=bits(on_eng[k * per:(k + 1) * per]),
                                              remote_sem=T.sem["rl%d" % t], src=src, dst=T.hand[:, 32 * t:32 * t + w])
                            for k, (rl, _) in enumerate(relays)], local_sem=T.sem["ls%d" % t])
        g.remote_dma_fused([RemoteDMATransfer(dst_ids=[dst_id(topo, d, core) for d in direct], dma_engine_mask=bits(off_eng),
                                              remote_sem=T.sem["ad%d" % t], srcs=[src], dsts=[src for d in direct])],
                           local_sem=T.sem["ls%d" % t])
        sent[0] = 2 * per + len(off_eng)

    near = [T.rank_of(c) for c in direct]
    farr = [r for r in range(8) if r != rank and r not in near]
    n_ad = sum(len(topo.engines(c, core)) for c in direct)
    n_ar = 0
    for r in farr:
        for rl, dests in routes(T, topo, T.cores[r])[1]:
            if core in dests:
                n_ar += len(topo.engines(rl, core)) // len(dests)

    def key_terms(t, ranks, last):
        land = T["land%d" % t]
        for n, r in enumerate(ranks):
            fin = last and n == len(ranks) - 1
            rk = ["own%d" % t] if r == rank else []
            if t == 0:
                mm(["sel"] + rk, ["ps2"], T.ps2[:, 0:16], T.sel[:], land[:, 16 * r:16 * r + 16], False, fin)
            else:
                mm(["selpm0", "selpm1"] + rk, ["ps2"], T.ps2[:, 16:19], T.selpm[:], land[:, 24 * r + 7:24 * r + 24:8], False, False)
                mm(["route"] + rk, ["ps2"], T.ps2[:, 18:19], T.route[:], land[:, 24 * r + 7:24 * r + 8], False, fin)

    def KC(u):
        return ["kb%dc%d" % (u, k) for k in range(5)]

    def key_close(t):
        if t > 0:
            kb, n = "kb%d" % t, S0 + t - 1
            mm(["id32", kb] + KC(t), ["ps2"], T.ps2[:, 0:52], T.id32[:], T[kb][:, 0:52], True, False)
            mm(["id0", "ext"], ["ps2"], T.ps2[:, 16:19], T.id0[:], T.ext[:, 0:3], False, False)
            mm(["pbig", "killa%d" % t], ["ps2"], T.ps2[:, 0:n], T.pbig[:], T["killa%d" % t][:, 0:n], False, False)
            mm(["pbig", "killb"], ["ps2"], T.ps2[:, 0:17], T.pbig[:], T.killb[:, 0:17], False, False)
            mm(["pbig", "dead%d" % t], ["ps2"], T.ps2[:, 0:16], T.pbig[:], T["dead%d" % t][:], False, False)
            mm(["route", "c2048"], ["ps2"], T.ps2[:, 18:19], T.route[:], T.c2048[:, 0:1], False, False)
        else:
            mm(["sel", "ptiea", "ptieb"], ["ps2"], T.ps2[:, 0:52], T.sel[:], T.ptie[:], True, False)
            mm(["sel", "poff"], ["ps2"], T.ps2[:, 0:16], T.sel[:], T.poff[:], False, False)
        key_terms(t, [rank], False)
        wait("p", ("ad%d" % t, n_ad))
        key_terms(t, near, False)
        wait("p", ("ar%d" % t, n_ar))
        key_terms(t, farr, True)
        if t == 1:
            mm(["sel", "c2048"], ["ps4"], T.ps4[:, 0:3], T.sel[:], T.c2048[:, 0:3], True, False)
            for r in range(8):
                mm(["sel"], ["ps4"], T.ps4[:, 0:3], T.sel[:], T.land1[:, 24 * r + 7:24 * r + 24:8], False, r == 7)

    def table2():
        ts(["killa1", "ps4"], ["mrga"], T.mrg[:, 0:S0], T.killa1[:, 0:S0], T.ps4[:, 0:1], A.mult, 1.0 / 256, A.mult)
        cp(["ps4"], ["mrgn"], T.mrg[:, S0:S0 + 1], T.ps4[:, 1:2])
        ts(["i16", "ps4"], ["mrgr"], T.mrg[:, 16:32], T.i16[:], T.ps4[:, 2:3], A.mult)
        mm(["id32", "kb1"], ["ps4"], T.ps4[:, 16:32], T.id32[:], T.kb1[:, 0:16], True, False)
        mm(["id32", "mrga", "mrgn"], ["ps4"], T.ps4[:, 16:17 + S0], T.id32[:], T.mrg[:, 0:S0 + 1], False, False)
        mm(["lv32", "mrgr"], ["ps4"], T.ps4[:, 16:32], T.lv32[:], T.mrg[:, 16:32], False, False)
        mm(["pbig", "dead1"], ["ps4"], T.ps4[:, 16:32], T.pbig[:], T.dead1[:], False, True)
        act(["ps4"], ["kb2"], T.kb2[:, 0:16], T.ps4[:, 16:32], F.Copy)

    def winner(t):
        b = 8 * t
        scan(["ps2", "neg"], ["sc"], T.sc[:, 12:64], T.ps2[:, 0:52], T.neg[:], -1e9, A.max, A.max)
        if t == 0:
            act(["ps2"], ["kb1"], T.kb1[:, 0:16], T.ps2[:, 0:16], F.Copy)
        op("v", ["sc"], ["sct"], lambda: V.transpose(T.sct[:, 0:32], T.sc[:, 32:64]))
        scan(["sct", "sctz"] + WADD, ["w%d%d" % (k, t) for k in WCOL], T.wo[:, 40 * t:40 * t + 39], T.sct[:, 0:39],
             T.wadd[:, 40 * t:40 * t + 39], -3e9, A.max, A.add)

    def record(t):
        b = 8 * t
        aff(["w6%d" % t], ["mg%da" % t], T.mgb[:, 3 * t:3 * t + 1], W(b + 6), 1.0, float(S0 + t))
        aff(["w7%d" % t], ["mg%dc" % t], T.mgb[:, 3 * t + 1:3 * t + 2], W(b + 7), 1.0, float(S0 + t))
        aff(["w1%d" % t], ["mg%db" % t], T.mgb[:, 3 * t + 2:3 * t + 3], W(b + 1), 1.0 / 256, CNT0)

    def delta_open():
        mm(["zi", "km256"], ["ps1"], T.ps1[:, 0:24], ident, T.km256[:], True, False)

    def delta(t, marks, more):
        b, u = 8 * t, t + 1
        cb, n = "cb%d" % t, S0 + t
        w = ["w%d%d" % (k, t) for k in range(8)]
        for lo, hi in ((0, 8), (8, 18)):
            ts([cb + "a", cb + "b", cb + "c", w[0], w[1]], ["mrk%d" % lo], T.mrk[:, :, 8 * lo:8 * hi], T[cb][:, :, 1 + 8 * lo:1 + 8 * hi],
               W(b + 1), A.add, W(b), A.is_equal)
            for m in range(lo, hi):
                mm(OH + ["mrk%d" % lo], ["ps1"], T.ps1[:, 0:24], T.oh[:, 8 * m:8 * m + 8, :], T.mrk[:, :, 8 * m:8 * m + 8],
                   False, m == 17)
        tt([w[0], w[1]], [w[2]], W(b + 2), W(b), W(b + 1), A.subtract)
        ts([w[4], w[0]], [w[7]], W(b + 7), W(b + 4), W(b), A.subtract, 15.0 - n, A.add)
        ts([w[5], w[1]], [w[6]], W(b + 6), W(b + 5), W(b + 1), A.subtract, -1.0 / 16, A.mult)
        if t == 1:
            table2()
        marks()
        scan(["rst", "ps1"], ["own%d" % u], T["land%d" % u][:, 24 * rank:24 * rank + 24], T.rst[:], T.ps1[:, 0:24], -30000.0,
             A.add, A.max)
        send(u)
        more()

    def fixes(t):
        b, u, n = 8 * t, t + 1, S0 + t
        w2, w6, w7 = "w2%d" % t, "w6%d" % t, "w7%d" % t
        ts(["cn%d" % u, w7], ["colb"], C(24), C(26 + t), W(b + 7), A.is_equal, -256.0, A.mult)
        ts(["c4", "ca%d" % u, w6], ["offt1"], C(25), C(4), W(b + 6), A.mult, C(28 + t), A.add)
        ts(["x15", w6], ["killa%d" % u], T["killa%d" % u][:, 0:n], T.x15[:, 0, 15 - n:15], W(b + 6), A.is_equal, -256.0, A.mult)
        ts(["ctab", w2], ["dead%d" % u], T["dead%d" % u][:], T.ctab[:], W(b + 2), A.is_equal, -256.0, A.mult)
        if t == 0:
            ts(["x15", w7], ["lv32"], T.lv32[:, :, 0:n], T.x15[:, :, 15 - n:15], W(b + 7), A.is_equal, -0.125, A.mult)
        ts(["kone", "colb"], ["killb"], T.killb[:, 0:17], T.kone[:, 0:17], C(24), A.mult)
        ts(["x15", w6, "colb"], ["route"], T.route[:, :, 0:n], T.x15[:, 0:4, 15 - n:15], W(b + 6), A.is_equal, C(24), A.mult)
        ts(["c30_", w7, "offt1"], ["offx"], T.offx[:, 2:3], C(30), W(b + 7), A.mult, C(25), A.add)

    def turn(u):
        kb = "kb%d" % u
        op("v", [kb] + KC(u), [kb + "t"], lambda: V.transpose(T[kb][:, 64:96], T[kb][:, 0:32]))

    def pick(u):
        kb = "kb%d" % u
        cp(KC(u) + [kb, kb + "t", "offx"], ["ext"], T.ext[:], T[kb][:].indirect(T.offx[:, 2:3]))

    send(0)
    gather_y0(0)

    BLK = [[-16, 8], [0, 16]]
    select(["kone"], ["bones"], T.bones[:], T.kone[:, 0:128], BLK, A.is_ge, 0.0, 0, 1)
    select(["kone"], ["bs0"], T.bs0[:], T.kone[:, 0:128], BLK, A.is_equal, 0.0, 0, 1)
    select(["bones"], ["bones"], T.bones[:], T.bones[:], [[16, 8], [0, 16]], A.is_ge, 0.0, 15, -1)
    iota(["k35"], T.k35[:], [[0, 160]], 35, 0)
    select(["bones"], ["btri"], T.btri[:], T.bones[:], [[1, 128]], A.is_gt, 0.0, 0, -1)
    tt(["ps3a", "cur0"], ["c0"], S("c0", -4, 149), P(0, -4, 149), S("cur0", -3, 150), A.subtract)
    ms(["c2048"], T.c2048[:], 2048.0)
    ms(["route"], T.route[:], 0.0)
    ms(["sctz"], T.sct[:, 32:40], -3e9)
    tt(["c0"], ["ps3b"], P(1, -1, 144), S("c0", 0, 145), S("c0", -2, 143), A.not_equal)
    cp(["c0"], ["cb0a"], T.cb0[:, 0, 0:145], S("c0", 0, 145))
    for k, (c, v) in enumerate(((33, MAGIC16), (34, -MAGIC16), (37, MAGIC), (38, -MAGIC))):
        op("v", ["wadd0"], [WADD[k + 6]], lambda: V.memset(T.wadd[:, c:120:40], v))
    tt(["ps3b", "c0"], ["cb0b"], T.cb0[:, 1, 1:145], P(1, 0, 144), S("c0", 1, 145), A.mult)
    tt(["ps3b", "c0"], ["cb0c"], T.cb0[:, 2, 1:145], P(1, -1, 143), S("c0", -2, 142), A.mult)
    delta_open()
    lin("ps6", 151, [("zi", "c0", -3)], True, False)
    lin("ps0", 152, [("nzi", "cur0", -3)], True, False)
    key_close(0)
    ts(["c16", "c16_"], ["smi"], T.smi[:, 0:9], T.c16[:, 0:9], C(16), A.subtract, 1.0 / 9, A.mult)
    ts(["pg", "oo0"], ["c12"], C(12), T.pi[:, 2:3], T.oo[:, 0:1], A.subtract, -31.0, A.add)
    for u in (1, 2):
        ts(["odd"], ["kb%dc0" % u], T["kb%d" % u][:, 16:17], C(7), -1.0, A.mult, -BACK, A.min)
        ts(["odd", "c8"], ["kb%dc1" % u], T["kb%d" % u][:, 17:18], C(10), NEW - (S0 + u - 1), A.add, C(7), A.min)
    ts(["smi", "c12"], ["sm1"], T.sm[:, 20:29], T.smi[:, 0:9], -287.0, A.mult, C(12), A.add)
    ts(["x15"], ["lv32"], T.lv32[:], T.x15[:], S0 - 15.0, A.is_equal, 0.125, A.mult)
    for u in (1, 2):
        kb = T["kb%d" % u]
        ts(["odd", "c31%d" % u, "kb%dc0" % u], ["kb%dc2" % u], kb[:, 18:19], C(30 + u), C(7), A.min, kb[:, 16:17], A.max)
    tt(["thr", "sm1"], ["sm2"], T.sm[:, 0:9], T.sm[:, 20:29], T.thr[:, 0:9], A.add)
    for h, v in enumerate((-256.0, 256.0)):
        ts(["x16", "c01"], ["selpm%d" % h], T.selpm[:, :, 16 * h:16 * h + 16], T.x16[:, 0:64], C(1), A.is_equal, v, A.mult)
    ts(["xf", "c14", "c11"], ["zw"], T.zw[:, 0:144], T.xf[:, 0:144], C(14), A.is_equal, C(11), A.mult)
    cp(["sm2"], ["offt"], T.offt[:, 0:9], T.sm[:, 0:9])

    winner(0)
    tie0 = W(2)

    def marks0():
        ts(["c0", "w20", "w70"], ["hb"], S("hb", -4, 149), S("c0", -4, 149), tie0, A.is_equal, W(7), A.mult)
        ts(["c0", "w20", "w60"], ["ha"], S("ha", -4, 149), S("c0", -4, 149), tie0, A.is_equal, W(6), A.mult)

    def more0():
        ts(["c0", "w20"], ["ht"], S("ht", -4, 149), S("c0", -4, 149), tie0, A.is_equal, tie0, A.mult)

    delta(0, marks0, more0)
    ts(["c0", "w20"], ["h0"], S("h0", -4, 149), S("c0", -4, 149), tie0, A.is_equal)
    select(["bones"], ["bup"], T.bup[:], T.bones[:], [[-1, 128]], A.is_gt, 0.0, 0, 1)
    select(["btri"], ["btri"], T.btri[:], T.btri[:], [[1, 128]], A.not_equal, -0.5, 0, -1)
    select(["bup"], ["bup"], T.bup[:], T.bup[:], [[1, 128]], A.not_equal, 1.5, 0, -1)
    lin("ps0", 152, [("zi", "hb", -4), ("zi", "ha", -3)], False, True)
    lin("ps6", 151, [("i16x", "hb", -4), ("zi", "ha", -2), ("nzi", "ht", -3)], False, True)
    aff(["ps0"], ["rc1"], S("rc1", -3, 149), T.ps0[:, 0:152], 1.0, 12.0)
    oh_a("rc1", 144, [(10, 2), (11, 1), (12, 0)])
    record(0)
    ts(["c0", "w20"], ["ps3b"], P(1, -4, 149), S("c0", -4, 149), tie0, A.not_equal)
    turn(1)
    fixes(0)
    pick(1)
    delta_open()
    lin("ps5", 147, [("zi", "k35", -1), ("n512", "h0", -1), ("i16x", "rc1", -1), ("zi", "rc1", 0)], True, False)
    lin("ps7", 147, [("zi", "h0", -1)], True, False)
    lin("ps0", CH, [("zi", "rc1", 0)], True, False)
    key_close(1)
    steps = [
        lambda: tt(["ps6", "h0"], ["ne"], S("ne", -1, 147), T.ps6[:, 3:151], S("h0", -1, 147), A.mult),
        lambda: scan(["h0", "ps6"], ["cbk"], S("cbk", -2, 147), S("h0", -3, 146), T.ps6[:, 0:149], 0.0, A.mult, A.add),
        lambda: tt(["ps6", "ne"], ["ca"], S("ca", -1, 147), T.ps6[:, 2:150], S("ne", -1, 147), A.add),
        lambda: tt(["ps3b", "cbk"], ["ps3c"], P(2, -1, 144), P(1, -1, 144), S("cbk", -1, 144), A.mult),
        lambda: tt(["ps3b", "ca"], ["cb1a"], T.cb1[:, 0, 0:145], P(1, -1, 144), S("ca", 0, 145), A.mult),
        lambda: tt(["ps3c", "cb1a"], ["ne"], S("ne", -1, 144), P(2, -1, 144), T.cb1[:, 0, 0:145], A.not_equal),
        lambda: tt(["ps3c", "ne"], ["cb1c"], T.cb1[:, 2, 1:145], P(2, -1, 143), S("ne", -1, 143), A.mult),
        lambda: tt(["cb1a", "ne"], ["cb1b"], T.cb1[:, 1, 1:145], T.cb1[:, 0, 1:145], S("ne", 0, 144), A.mult)]
    hot = list(range(10))
    for step, fill in zip(steps, (0, 1, 1, 2, 3, 3, 0, 0)):
        step()
        for _ in range(fill):
            s = hot.pop(0)
            oh_v("rc1", 144, s, 12 - s)

    winner(1)
    tie1 = W(10)

    def marks1():
        ts(["cbk", "w21", "w71"], ["mb"], S("mb", -1, 147), S("cbk", -1, 147), tie1, A.is_equal, W(15), A.mult)
        ts(["ca", "w21", "w61"], ["ma"], S("ma", -1, 147), S("ca", -1, 147), tie1, A.is_equal, W(14), A.mult)

    def more1():
        ts(["ps6", "w21"], ["h1"], S("h1", -1, 146), T.ps6[:, 2:149], tie1, A.is_equal)
        lin("ps5", 147, [("i16x", "mb", -1), ("zi", "ma", 0), ("n512", "h1", -1)], False, True)
        lin("ps7", 147, [("zi", "h1", -1)], False, True)
        lin("ps0", CH, [("zi", "ma", 0), ("zi", "mb", 0)], False, False)

    delta(1, marks1, more1)
    iota(["crowb"], T.crow[:, 0:145], [[16, 145]], -16, 0)
    iota(["crowc"], T.crow[:, 145:147], [[0, 2]], L + int(PRES), 0)
    iota(["kt1"], T.kt[:, CH:CH + 1], [[0, 1]], 2, 0)
    iota(["lo0"], T.lo[:, 145:146], [[0, 1]], 0, 0)
    iota(["kbig"], T.kbig[:], [[0, 160]], 49152, 0)
    iota(["y0z"], T.y0[:, L:L + 1], [[0, 1]], 0, 0)
    iota(["ggr"], T.gg[:, 16 + L:32 + L], [[0, 16]], 15, 0)
    record(1)
    aff(["bones"], ["nbones"], T.nbones[:], T.bones[:], -2.0, 0.0)
    aff(["btri"], ["nbtri"], T.nbtri[:], T.btri[:], -2.0, 0.0)
    aff(["bup"], ["nbup"], T.nbup[:], T.bup[:], -2.0, 0.0)
    gather_y0(1)
    fixes(1)
    turn(2)
    for h in range(2):
        ts(["ps5"], ["xd%d" % h], T.xd[:, :, 16 * h:16 * h + 16], T.ps5[:, 0:CH], 0.0, A.max)
    pick(2)
    key_close(2)
    ts(["ps5"], ["cz2"], T.cz2[:, 16:163], T.ps5[:, 0:147], 0.0, A.max)
    op("v", ["xd0", "xd1"], ["xt"], lambda: V.transpose(T.xt[:], T.xd[:]))
    tt(["ps7", "cz2"], ["ps3a"], P(0, 0, 145), T.cz2[:, 18:163], T.ps7[:, 1:146], A.mult)
    ts(["xt", "offt"], ["et"], T.et[:, 0:CH], T.xt[:, 0:288].indirect(T.offt[:, 0:9]), -128.0, A.add)
    tt(["ps3a", "cz2"], ["s1"], S("s1", 0, 145), P(0, 0, 145), T.cz2[:, 17:162], A.add)
    tt(["ps7", "s1"], ["ps3b"], P(1, 0, 144), S("s1", 1, 145), T.ps7[:, 1:145], A.mult)
    ts(["et"], ["kt"], T.kt[:, 0:CH], T.et[:, 0:CH], -127.5, A.is_gt, 2.0, A.mult)
    tt(["ps3b", "cz2"], ["ca2"], S("ca2", 0, 144), P(1, 0, 144), T.cz2[:, 17:161], A.add)
    mm(["bones", "kt", "kt1"], ["ps4"], T.ps4[:, 0:145], T.bones[:], T.kt[:, 0:145], True, False)
    mm(["btri", "kt", "kt1"], ["ps5"], T.ps5[:, 0:145], T.btri[:], T.kt[:, 0:145], True, False)
    mm(["bup", "kt"], ["ps5"], T.ps5[:, 1:145], T.bup[:], T.kt[:, 0:CH], False, False)
    mm(["zi", "crowb", "crowc"], ["ps6"], T.ps6[:, 0:147], ident, T.crow[:, 0:147], True, False)

    winner(2)
    ts(["et", "w02", "w12"], ["nd"], T.nd[:, 0:CH], T.et[:, 0:CH], W(17), A.add, W(16), A.is_equal)
    mm(["nbtri", "nd"], ["ps5"], T.ps5[:, 0:CH], T.nbtri[:], T.nd[:, 0:CH], False, False)
    mm(["nbup", "nd"], ["ps5"], T.ps5[:, 1:145], T.nbup[:], T.nd[:, 0:CH], False, True)
    mm(["nbones", "nd"], ["ps4"], T.ps4[:, 0:CH], T.nbones[:], T.nd[:, 0:CH], False, True)
    ts(["w02", "w12"], ["w62"], W(22), W(16), W(17), A.subtract, 128.0, A.add)
    ts(["ca2", "w62"], ["m14"], S("m14", 0, 144), S("ca2", 0, 144), W(22), A.is_equal, -16.0, A.mult)
    lin("ps0", CH, [("zi", "m14", 0)], False, True)
    scan(["ps5", "kbig"], ["ps3a"], T.ps3[:, 0:145], T.ps5[:, 0:145], T.kbig[:, 0:145], 32800 - 14.5, A.add, A.min)
    scan(["ps5", "kbig"], ["idx"], T.idx[:, 0:145], T.ps5[:, 0:145], T.kbig[:, 0:145], 32800 - 14.5, A.add, A.min)
    scan(["ps4", "kbig", "oo0"], ["oo"], T.oo[:, 1:146], T.ps4[:, 0:145], T.kbig[:, 0:145], T.oo[:, 0:1], A.add, A.min)

    def count(u):
        c0 = 0 if u < UA else 16 * UA
        act(["oo", "oo0", "thr"], ["eh%d" % u], T.junk[:, 146 * u + c0:146 * u + 146], T.oo[:, c0:146], F.Sign,
            bias=T.thr[:, u:u + 1], scale=-1.0, accum_out=T.eh[:, u:u + 1])

    act(["ps0"], ["xs"], T.xs[:, 0:CH], T.ps0[:, 0:CH], F.Relu, bias=2.0)
    dma("s", ["xs"], ["gg%d" % a for a, _ in VCUT + ACUT], T.gg[0:128:16, 16:16 + L], T.xs[:, 0:CH], "dsy")
    tt(["idx", "ps3a"], ["zb"], T.zb[:, 0:145], T.ps3[:, 0:145], T.idx[:, 0:145], A.subtract)
    mm(["bs0", "zb"], ["ps7"], T.ps7[:, 0:145], T.bs0[:], T.zb[:, 0:145], True, True)
    for u in range(9):
        count(u)
        if u == UA - 1:
            act(["ps7", "c13"], ["ml"], T.ml[:, 0:145], T.ps7[:, 0:145], F.Identity, bias=C(13), scale=-8192.0)
    for r in range(16):
        ts(["zb"], ["ohz%d" % r], T.ohz[:, CH * r:CH * r + CH], T.zb[:, 0:CH], 2.0 * r - 15.5, A.is_equal)
        mm(["zw", "ohz%d" % r], ["ps6"], T.ps6[:, 1:145], T.zw[:, 15 - r:143 - r], T.ohz[:, CH * r:CH * r + CH], False, r == 15)
    ts(["eh%d" % u for u in range(UA)], ["ehua"], T.ehu[:, 0:UA], T.eh[:, 0:UA], 0.5, A.mult, 72.0, A.add)
    ts(["w52", "w12"], ["mg2a"], T.mgb[:, 6:7], W(21), W(17), A.subtract, -1.0 / 16, A.mult)
    tt(["ps6", "ml"], ["lo"], T.lo[:, 0:145], T.ps6[:, 1:146], T.ml[:, 0:145], A.min)
    ts(["w42", "w02"], ["mg2c"], T.mgb[:, 7:8], W(20), W(16), A.subtract, 15.0, A.add)
    scan(["ps6", "lo", "lo0"], ["xm"], T.xm[:, 0:146], T.ps6[:, 0:146], T.lo[:, 0:146], 0.0, A.max, A.max)
    ts(["w12"], ["mg2b"], T.mgb[:, 8:9], W(17), 1.0 / 256, A.mult, CNT0, A.add)
    dma("s", ["mg%d%s" % (t, s) for t in range(3) for s in "abc"], [], T.mg[:], T.mgb[0:1, 0:9])
    ts(["xm", "ehua"], ["tua"], T.tu[:, 0:16 * UA], T.xm[:, 0:146].indirect(T.ehu[:, 0:UA]), -PRES, A.add)
    ts(["eh%d" % u for u in range(UA, 9)], ["ehub"], T.ehu[:, UA:9], T.eh[:, UA:9], 0.5, A.mult, 72.0 + 8 * UA, A.add)

    act(["oo", "c6"], ["flv"], C(15), T.oo[:, 144:145], F.Identity, bias=C(6), scale=0.5)
    dma("s", ["flv"], [], T.fl[:], T.col[0:128:16, 15:16])
    pieces = [(b, "y", a) for a, b in zip(YCUT, YCUT[1:])] + [(b, "fs", a) for a, b in zip(FCUT, FCUT[1:])]
    for b, kind, a in sorted(pieces):
        tu = "tua" if a < 16 * UA else "tub"
        if kind == "y":
            if b < CH:
                cp(["y00", "y01", "y0z", tu], ["yo%d" % a], T.yo[:, 16 * a:16 * b], T.y0[:, 0:L + 1].indirect(T.tu[:, a:b]))
            else:
                act(["y00", "y01", "y0z", tu], ["yo%d" % a], T.yo[:, 16 * a:16 * b], T.y0[:, 0:L + 1].indirect(T.tu[:, a:b]), F.Copy)
            dma("s", ["yo%d" % a], [], T.y[:, 16 * a:16 * b], T.yo[:, 16 * a:16 * b])
            if a == 0:
                ts(["xm", "ehub"], ["tub"], T.tu[:, 16 * UA:CH], T.xm[:, 0:146].indirect(T.ehu[:, UA:9]), -PRES, A.add)
        else:
            act(["gg0", "ggr", tu], ["fso%d" % a], T.fso[:, 16 * a:16 * b], T.gg[:, 16:17 + L].indirect(T.tu[:, a:b]), F.Identity,
                bias=14.0, scale=-1.0)
            dma("s", ["fso%d" % a], [], T.fs[:, 16 * a:16 * b], T.fso[0:128:16, 16 * a:16 * b])

    for q in ("v", "a", "p", "g"):
        g.wait_ge(T.sem[SEM[q]], cnt[q])
    for s in ("dpos", "dst", "dle", "dve", "dsw", "dsy"):
        g.wait_ge(T.sem[s], 16)
    for t in range(3):
        g.wait_ge(T.sem["ls%d" % t], sent[0])
    g.wait_ge(T.sem.dout, outs[0])
